import numpy as np
import ml_dtypes


def mxq(x, axis, fmt="e4m3"):
    dtype, down = {"e4m3": (ml_dtypes.float8_e4m3fn, 7), "e5m2": (ml_dtypes.float8_e5m2, 14)}[fmt]
    v = np.moveaxis(np.asarray(x, np.float32).astype(ml_dtypes.bfloat16).astype(np.float64), axis, -1)
    blocks = v.reshape(v.shape[:-1] + (-1, 32))
    amax = np.abs(blocks).max(-1, keepdims=True)
    byte = np.maximum(np.where(amax > 0, np.frexp(amax)[1] - 1 + 127, 0) - down, 1)
    scale = np.exp2(byte - 127.0)
    codes = (blocks / scale).astype(np.float32).astype(dtype).astype(np.float64)
    return np.moveaxis((codes * scale).reshape(v.shape), -1, axis)


WIDE = False


def mx_kscale(k):
    if not WIDE:
        return np.ones(k)
    levels = np.array([18, -18])
    if k % 512:
        return np.exp2(np.random.permutation(np.resize(levels, k // 32))).repeat(32)
    a = np.empty((k // 512, 16))
    for p in range(k // 512):
        a[p, :8] = np.random.permutation(np.resize(levels, 8))
        for g in range(8):
            far = levels[np.abs(levels - a[p, g]) >= 10]
            a[p, g + 8] = far[np.random.randint(len(far))]
    return np.exp2(a.ravel()).repeat(32)


def f64(x):
    return np.asarray(x).astype(np.float64)


def striped(idx):
    return np.tile(np.asarray(idx).reshape(-1, 16).T, (8, 1)).astype(np.uint16)


def unstriped(offs):
    return offs[:16].T.reshape(-1).astype(np.int64)

def planes(y):
    n, m = y.shape
    v = y.astype(np.float32).astype(ml_dtypes.bfloat16).astype(np.float64).reshape(n // 32, 32, m)
    top = np.abs(v).max(1)
    byte = np.clip(np.where(top > 0, np.frexp(top)[1] - 1 + 127 - 7, 1), 1, 254)
    codes = (v * np.exp2(127.0 - byte)[:, None, :]).reshape(n, m).astype(np.float32).astype(ml_dtypes.float8_e4m3fn).view(np.uint8)
    words = codes.reshape(n // 512, 128, 4, m).transpose(0, 1, 3, 2)
    return np.ascontiguousarray(words), np.ascontiguousarray(byte.astype(np.uint8).reshape(n // 512, 16, m))


B, N, T, D, R = 1, 512, 2048, 512, 1024
LR = 0.1
WD = 0.5


def setup_inputs():
    n = np.random.standard_normal
    idx = np.random.permutation(T)[:B * N]
    s = mx_kscale(D)[:, None]
    z = mx_kscale(R)[:, None]
    x = n((B, D, R))
    return {
        "xT": (x * s).astype(np.float32),
        "wT": (n((D, T)) * (1.00 / np.sqrt(D)) / s).astype(np.float32),
        "y": np.random.randint(0, 2, (B, R, N)).astype(np.float32),
        "wt": (np.random.uniform(0.5, 1.5, (B, R, 1)) * 1.0 / np.sqrt(R) * z).astype(np.float32),
        "xm": (x.transpose(0, 2, 1) / z / s[:, 0]).astype(np.float32),
        "offs": striped(idx),
    }


def reference(xT, wT, y, wt, xm, offs):
    idx = unstriped(offs)
    pick = lambda x: x[:, idx].reshape(x.shape[0], B, N).transpose(1, 0, 2)
    w = pick(f64(wT))
    a = mxq(f64(xT), 1, "e4m3").transpose(0, 2, 1) @ mxq(w, 1, "e4m3")
    g = f64(wt) * (1.0 / (1.0 + np.exp(-a)) - f64(y))
    dw = mxq(f64(xm), 1, "e4m3").transpose(0, 2, 1) @ mxq(g, 1, "e5m2")
    nw = (1.0 - LR * WD) * w - LR * dw
    tables = []
    for old, new in ((wT, nw),):
        table = f64(old)
        table[:, idx] = new.transpose(1, 0, 2).reshape(D, B * N)
        tables.append(table)
    return tuple(tables) + planes(tables[0])

@@ -1,0 +1,207 @@
+from contextlib import ExitStack
+
+import concourse.mybir as mybir
+
+N, T, D, R = 512, 2048, 512, 1024
+LR, WD = 0.1, 0.5
+FLOPS = 2 * 2 * N * D * R
+
+F32 = mybir.dt.float32
+BF16 = mybir.dt.bfloat16
+I32 = mybir.dt.int32
+U32 = mybir.dt.uint32
+U16 = mybir.dt.uint16
+U8 = mybir.dt.uint8
+E4 = mybir.dt.float8_e4m3fn_x4
+E5 = mybir.dt.float8_e5m2_x4
+ACT = mybir.ActivationFunctionType
+ALU = mybir.AluOpType
+
+P = 128
+PACK = 4
+PASSES = R // (P * PACK)
+CHUNK = 512
+CHUNKS = T // CHUNK
+
+
+def tile_attend_gnce_pl_sgd_kernel(tc, xT, wT, y, wt, xm, offs, out_0, out_1, out_2):
+    nc = tc.nc
+    with ExitStack() as ctx:
+        held = ctx.enter_context(tc.tile_pool(name="held", bufs=1))
+        ring = ctx.enter_context(tc.tile_pool(name="ring", bufs=4))
+        score_psum = ctx.enter_context(tc.psum_pool(name="score_psum", bufs=4))
+        grad_psum = ctx.enter_context(tc.psum_pool(name="grad_psum", bufs=1))
+
+        def sb(shape, dtype, name, tag=""):
+            return held.tile(shape, dtype, name=name, tag=tag or name, align_bytes=64)
+
+        offsets = held.tile([P, N // 16], U16, name="offsets")
+        nc.sync.dma_start(offsets[:], offs)
+
+        w_planes = wT.rearrange("(p t) c -> p t c", t=PACK)
+        out_planes = out_0.rearrange("(p t) c -> p t c", t=PACK)
+        source = [sb([P, T], F32, "source%d" % t) for t in range(PACK)]
+        for t in range(PACK):
+            nc.sync.dma_start(source[t][:], w_planes[:, t, :])
+        x_raw = [sb([P, PACK, 512], F32, "x_raw%d" % g) for g in range(PASSES)]
+        y_raw = [sb([P, PACK, N], F32, "y_raw%d" % g) for g in range(PASSES)]
+        xm_raw = [sb([P, PACK, D], F32, "xm_raw%d" % g) for g in range(PASSES)]
+        weight = sb([P, PASSES, 8], F32, "weight")
+        for g in range(PASSES):
+            nc.sync.dma_start(x_raw[g][:], xT[0, :, g * 512:(g + 1) * 512].rearrange("(p t) r -> p t r", t=PACK))
+        nc.sync.dma_start(weight[:, :, 0:PACK], wt[0].rearrange("(g p j) o -> p g (j o)", g=PASSES, j=PACK))
+        for g in range(PASSES):
+            nc.sync.dma_start(y_raw[g][:], y[0, g * 512:(g + 1) * 512, :].rearrange("(p j) n -> p j n", j=PACK))
+        for g in range(PASSES):
+            nc.sync.dma_start(xm_raw[g][:], xm[0, g * 512:(g + 1) * 512, :].rearrange("(p j) d -> p j d", j=PACK))
+        window = [sb([P, T], F32, "window%d" % t) for t in range(PACK)]
+        for t in range(PACK):
+            nc.sync.dma_start(window[t][:], w_planes[:, t, :])
+
+        warm = sb([P, 16], F32, "warm")
+        nc.vector.memset(warm[:, 0:8], 0.0)
+        nc.scalar.activation(warm[:, 8:16], warm[:, 0:8], ACT.Sigmoid)
+
+        picked = [sb([P, 2, N], F32, "picked%d" % u) for u in range(2)]
+        w_bf = sb([P, N, PACK], BF16, "w_bf")
+        decayed = sb([P, PACK, N], F32, "decayed")
+        for t in range(PACK):
+            nc.vector.tensor_copy(picked[t // 2][:, t % 2, :], source[t][:].indirect(offsets[:]))
+            if t == 1:
+                nc.scalar.copy(w_bf[:, :, 0:2], picked[0][:].rearrange("p e n -> p n e"))
+            if t < 2:
+                nc.scalar.activation(decayed[:, t, :], picked[0][:, t, :], ACT.Copy, scale=1.0 - LR * WD)
+        nc.vector.tensor_copy(w_bf[:, :, 2:4], picked[1][:].rearrange("p e n -> p n e"))
+        for t in range(2, PACK):
+            nc.scalar.activation(decayed[:, t, :], picked[1][:, t - 2, :], ACT.Copy, scale=1.0 - LR * WD)
+        w_codes = sb([P, N], U32, "w_codes")
+        w_scales = sb([P, N], U8, "w_scales")
+        nc.vector.quantize_mx(w_codes[:].bitcast(E4), w_scales[:], w_bf[:].rearrange("p n t -> p (n t)"))
+
+        def deal(engine_copy, dst, raw, lo, hi):
+            engine_copy(
+                dst[:, :, lo:hi, :].rearrange("p j s t -> p s t j"),
+                raw[:].rearrange("p t (s j) -> p s t j", j=PACK)[:, lo:hi, :, :],
+            )
+
+        x_bf = [sb([P, PACK, P, PACK], BF16, "x_bf%d" % g) for g in range(PASSES)]
+        x_codes = [sb([P, 512], U32, "x_codes%d" % g) for g in range(PASSES)]
+        x_scales = [sb([P, 512], U8, "x_scales%d" % g) for g in range(PASSES)]
+        xm_bf = [sb([P, PACK, P, PACK], BF16, "xm_bf%d" % g) for g in range(PASSES)]
+        xm_codes = [sb([P, D], U32, "xm_codes%d" % g) for g in range(PASSES)]
+        xm_scales = [sb([P, D], U8, "xm_scales%d" % g) for g in range(PASSES)]
+        g_rows = [sb([P, PACK, N], BF16, "g_rows%d" % g) for g in range(PASSES)]
+        g_bf = [sb([P, N, PACK], BF16, "g_bf%d" % g) for g in range(PASSES)]
+        g_codes = [sb([P, N], U32, "g_codes%d" % g) for g in range(PASSES)]
+        g_scales = [sb([P, N], U8, "g_scales%d" % g) for g in range(PASSES)]
+
+        def quantise_x(g):
+            nc.vector.quantize_mx(x_codes[g][:].bitcast(E4), x_scales[g][:], x_bf[g][:].rearrange("p j s t -> p (j s t)"))
+
+        def scores(g):
+            sig = []
+            for j in range(PACK):
+                bank = score_psum.tile([P, N], F32, name="bank")
+                cols = slice(j * P, (j + 1) * P)
+                nc.tensor.matmul_mx(bank[:], lhsT=x_codes[g][:, cols].bitcast(E4), lhsT_scale=x_scales[g][:, cols],
+                                    rhs=w_codes[:].bitcast(E4), rhs_scale=w_scales[:], start=True, stop=True)
+                s = ring.tile([P, N], F32, name="sig", bufs=8)
+                nc.scalar.activation(s[:], bank[:], ACT.Sigmoid)
+                sig.append(s)
+            return sig
+
+        def gradient(g, sig):
+            for j in range(PACK):
+                nc.vector.scalar_tensor_tensor(g_rows[g][:, j, :], sig[j][:], weight[:, g, j:j + 1], y_raw[g][:, j, :],
+                                               ALU.mult, ALU.subtract)
+
+        def weave_g(g):
+            nc.vector.tensor_copy(g_bf[g][:].rearrange("p (c i) j -> p c j i", i=4),
+                                  g_rows[g][:].rearrange("p j (c i) -> p c j i", i=4))
+
+        def quantise_g(g):
+            nc.vector.quantize_mx(g_codes[g][:].bitcast(E5), g_scales[g][:], g_bf[g][:].rearrange("p n j -> p (n j)"))
+
+        deal(nc.scalar.copy, x_bf[0], x_raw[0], 0, 48)
+        deal(nc.vector.tensor_copy, x_bf[0], x_raw[0], 48, P)
+        quantise_x(0)
+        sig0 = scores(0)
+        deal(nc.vector.tensor_copy, x_bf[1], x_raw[1], 0, P)
+        quantise_x(1)
+        sig1 = scores(1)
+        for j in range(PACK):
+            nc.vector.tensor_scalar(y_raw[0][:, j, :], y_raw[0][:, j, :], weight[:, 0, j:j + 1], None, ALU.mult)
+        gradient(0, sig0)
+        for j in range(PACK):
+            nc.scalar.activation(y_raw[1][:, j, :], y_raw[1][:, j, :], ACT.Copy, scale=weight[:, 1, j:j + 1])
+        weave_g(0)
+        deal(nc.scalar.copy, xm_bf[0], xm_raw[0], 0, P)
+        gradient(1, sig1)
+        quantise_g(0)
+        weave_g(1)
+        deal(nc.scalar.copy, xm_bf[1], xm_raw[1], 0, 64)
+        nc.vector.quantize_mx(xm_codes[0][:].bitcast(E4), xm_scales[0][:], xm_bf[0][:].rearrange("p t m j -> p (t m j)"))
+        quantise_g(1)
+        deal(nc.vector.tensor_copy, xm_bf[1], xm_raw[1], 64, P)
+
+        grads = []
+        for t in range(PACK):
+            cols = slice(t * P, (t + 1) * P)
+            nc.vector.quantize_mx(xm_codes[1][:, cols].bitcast(E4), xm_scales[1][:, cols],
+                                  xm_bf[1][:, t, :, :].rearrange("p m j -> p (m j)"))
+            acc = grad_psum.tile([P, N], F32, name="grad%d" % t)
+            for g in range(PASSES):
+                nc.tensor.matmul_mx(acc[:], lhsT=xm_codes[g][:, cols].bitcast(E4), lhsT_scale=xm_scales[g][:, cols],
+                                    rhs=g_codes[g][:].bitcast(E5), rhs_scale=g_scales[g][:],
+                                    start=(g == 0), stop=(g == PASSES - 1))
+            grads.append(acc)
+
+        pairs = [sb([P, 2, 2 * CHUNK, 2], BF16, "pairs%d" % h, tag="x_raw%d" % h) for h in range(2)]
+        for t in range(PACK):
+            fresh = ring.tile([P, N], F32, name="fresh", bufs=2)
+            nc.vector.scalar_tensor_tensor(fresh[:], grads[t][:], -LR, decayed[:, t, :], ALU.mult, ALU.add)
+            nc.vector.tensor_copy(window[t][:].indirect(offsets[:]), fresh[:])
+            nc.sync.dma_start(out_planes[:, t, :], window[t][:])
+            if t < PACK - 1:
+                for h in range(2):
+                    half = window[t][:, h * 2 * CHUNK:(h + 1) * 2 * CHUNK]
+                    if (t, h) == (2, 0):
+                        nc.scalar.copy(pairs[h][:, 1, :, :], half.unsqueeze(2).to_broadcast([P, 2 * CHUNK, 2]))
+                    else:
+                        nc.scalar.copy(pairs[h][:, t // 2, :, t % 2], half)
+
+        out_bf = [sb([P, CHUNK, PACK], BF16, "out_bf%d" % c, tag=("x_bf%d" % c if c < 2 else "g_rows%d" % (c - 2)))
+                  for c in range(CHUNKS)]
+        out_codes = [sb([P, CHUNK], U32, "out_codes%d" % c) for c in range(CHUNKS)]
+        out_scales = sb([P, T], U8, "out_scales")
+        words_out = out_1[0].rearrange("p c l -> p (c l)").bitcast(I32)
+
+        def last_plane(engine_copy, c):
+            lo = (c % 2) * CHUNK
+            engine_copy(pairs[c // 2][:, 1, lo:lo + CHUNK, 1], window[PACK - 1][:, c * CHUNK:(c + 1) * CHUNK])
+
+        def weave_out(engine_copy, word, c):
+            lo = (c % 2) * CHUNK
+            src = pairs[c // 2][:].rearrange("p u n e -> p u (n e)").bitcast(word)[:, :, lo:lo + CHUNK]
+            dst = out_bf[c][:].rearrange("p n t -> p (n t)").bitcast(word).rearrange("p (n u) -> p n u", u=2)
+            engine_copy(dst, src.rearrange("p u n -> p n u"))
+
+        def quantise_out(c):
+            cols = slice(c * CHUNK, (c + 1) * CHUNK)
+            nc.vector.quantize_mx(out_codes[c][:].bitcast(E4), out_scales[:, cols],
+                                  out_bf[c][:].rearrange("p n t -> p (n t)"))
+            nc.sync.dma_start(words_out[:, cols], out_codes[c][:].bitcast(I32))
+
+        for c in (0, 1):
+            last_plane(nc.vector.tensor_copy, c)
+        for c in (2, 3):
+            last_plane(nc.scalar.copy, c)
+            weave_out(nc.scalar.copy, U32, c)
+        for c in (0, 1):
+            weave_out(nc.vector.tensor_copy, I32, c)
+        for c in range(CHUNKS):
+            quantise_out(c)
+        scales_out = out_2[0].bitcast(I32)
+        for q in range(4):
+            queue = nc.sync if q % 2 == 0 else nc.scalar
+            queue.dma_start(scales_out[4 * q:4 * q + 4, :], out_scales[32 * q:32 * q + 4, :].bitcast(I32))

@@ -44,14 +44,16 @@ def tile_attend_gnce_pl_sgd_kernel(tc, xT, wT, y, wt, xm, offs, out_0, out_1, ou
         for t in range(PACK):
             nc.sync.dma_start(source[t][:], w_planes[:, t, :])
         x_raw = [sb([P, PACK, 512], F32, "x_raw%d" % g) for g in range(PASSES)]
-        y_raw = [sb([P, PACK, N], F32, "y_raw%d" % g) for g in range(PASSES)]
+        y_raw = [[sb([P, 2, N], F32, "y_raw%d%d" % (g, u)) for u in range(2)] for g in range(PASSES)]
         xm_raw = [sb([P, PACK, D], F32, "xm_raw%d" % g) for g in range(PASSES)]
         weight = sb([P, PASSES, 8], F32, "weight")
         for g in range(PASSES):
             nc.sync.dma_start(x_raw[g][:], xT[0, :, g * 512:(g + 1) * 512].rearrange("(p t) r -> p t r", t=PACK))
         nc.sync.dma_start(weight[:, :, 0:PACK], wt[0].rearrange("(g p j) o -> p g (j o)", g=PASSES, j=PACK))
         for g in range(PASSES):
-            nc.sync.dma_start(y_raw[g][:], y[0, g * 512:(g + 1) * 512, :].rearrange("(p j) n -> p j n", j=PACK))
+            y_rows = y[0, g * 512:(g + 1) * 512, :].rearrange("(p j) n -> p j n", j=PACK)
+            for u in range(2):
+                nc.sync.dma_start(y_raw[g][u][:], y_rows[:, 2 * u:2 * u + 2, :])
         for g in range(PASSES):
             nc.sync.dma_start(xm_raw[g][:], xm[0, g * 512:(g + 1) * 512, :].rearrange("(p j) d -> p j d", j=PACK))
         window = [sb([P, T], F32, "window%d" % t) for t in range(PACK)]
@@ -87,9 +89,9 @@ def tile_attend_gnce_pl_sgd_kernel(tc, xT, wT, y, wt, xm, offs, out_0, out_1, ou
         x_bf = [sb([P, PACK, P, PACK], BF16, "x_bf%d" % g) for g in range(PASSES)]
         x_codes = [sb([P, 512], U32, "x_codes%d" % g) for g in range(PASSES)]
         x_scales = [sb([P, 512], U8, "x_scales%d" % g) for g in range(PASSES)]
-        xm_bf = [sb([P, PACK, P, PACK], BF16, "xm_bf%d" % g) for g in range(PASSES)]
-        xm_codes = [sb([P, D], U32, "xm_codes%d" % g) for g in range(PASSES)]
-        xm_scales = [sb([P, D], U8, "xm_scales%d" % g) for g in range(PASSES)]
+        xm_bf = [[sb([P, 2, P, PACK], BF16, "xm_bf%d%d" % (g, u)) for u in range(2)] for g in range(PASSES)]
+        xm_codes = [[sb([P, 2 * P], U32, "xm_codes%d%d" % (g, u)) for u in range(2)] for g in range(PASSES)]
+        xm_scales = [[sb([P, 2 * P], U8, "xm_scales%d%d" % (g, u)) for u in range(2)] for g in range(PASSES)]
         g_rows = [sb([P, PACK, N], BF16, "g_rows%d" % g) for g in range(PASSES)]
         g_bf = [sb([P, N, PACK], BF16, "g_bf%d" % g) for g in range(PASSES)]
         g_codes = [sb([P, N], U32, "g_codes%d" % g) for g in range(PASSES)]
@@ -98,77 +100,106 @@ def tile_attend_gnce_pl_sgd_kernel(tc, xT, wT, y, wt, xm, offs, out_0, out_1, ou
         def quantise_x(g):
             nc.vector.quantize_mx(x_codes[g][:].bitcast(E4), x_scales[g][:], x_bf[g][:].rearrange("p j s t -> p (j s t)"))
 
-        def scores(g):
-            sig = []
-            for j in range(PACK):
-                bank = score_psum.tile([P, N], F32, name="bank")
-                cols = slice(j * P, (j + 1) * P)
-                nc.tensor.matmul_mx(bank[:], lhsT=x_codes[g][:, cols].bitcast(E4), lhsT_scale=x_scales[g][:, cols],
-                                    rhs=w_codes[:].bitcast(E4), rhs_scale=w_scales[:], start=True, stop=True)
-                s = ring.tile([P, N], F32, name="sig", bufs=8)
-                nc.scalar.activation(s[:], bank[:], ACT.Sigmoid)
-                sig.append(s)
-            return sig
+        def score(g, j):
+            bank = score_psum.tile([P, N], F32, name="bank")
+            cols = slice(j * P, (j + 1) * P)
+            nc.tensor.matmul_mx(bank[:], lhsT=x_codes[g][:, cols].bitcast(E4), lhsT_scale=x_scales[g][:, cols],
+                                rhs=w_codes[:].bitcast(E4), rhs_scale=w_scales[:], start=True, stop=True)
+            s = ring.tile([P, N], F32, name="sig", bufs=8)
+            nc.scalar.activation(s[:], bank[:], ACT.Sigmoid)
+            return s
 
-        def gradient(g, sig):
-            for j in range(PACK):
-                nc.vector.scalar_tensor_tensor(g_rows[g][:, j, :], sig[j][:], weight[:, g, j:j + 1], y_raw[g][:, j, :],
-                                               ALU.mult, ALU.subtract)
+        def weigh_y(on_vector, g, j):
+            rows = y_raw[g][j // 2][:, j % 2, :]
+            if on_vector:
+                nc.vector.tensor_scalar(rows, rows, weight[:, g, j:j + 1], None, ALU.mult)
+            else:
+                nc.scalar.activation(rows, rows, ACT.Copy, scale=weight[:, g, j:j + 1])
 
-        def weave_g(g):
-            nc.vector.tensor_copy(g_bf[g][:].rearrange("p (c i) j -> p c j i", i=4),
-                                  g_rows[g][:].rearrange("p j (c i) -> p c j i", i=4))
+        def gradient(g, j, sig):
+            nc.vector.scalar_tensor_tensor(g_rows[g][:, j, :], sig[:], weight[:, g, j:j + 1],
+                                           y_raw[g][j // 2][:, j % 2, :], ALU.mult, ALU.subtract)
+
+        def weave_g(engine_copy, g, lo, hi):
+            engine_copy(g_bf[g][:, lo:hi, :].rearrange("p (c i) j -> p c j i", i=4),
+                        g_rows[g][:, :, lo:hi].rearrange("p j (c i) -> p c j i", i=4))
 
         def quantise_g(g):
             nc.vector.quantize_mx(g_codes[g][:].bitcast(E5), g_scales[g][:], g_bf[g][:].rearrange("p n j -> p (n j)"))
 
+        def deal_xm(g, u):
+            nc.scalar.copy(
+                xm_bf[g][u][:].rearrange("p e m j -> p m j e"),
+                xm_raw[g][:].rearrange("p j (m t) -> p m j t", t=PACK)[:, :, :, 2 * u:2 * u + 2],
+            )
+
+        def quantise_xm(g, u):
+            nc.vector.quantize_mx(xm_codes[g][u][:].bitcast(E4), xm_scales[g][u][:],
+                                  xm_bf[g][u][:].rearrange("p e m j -> p (e m j)"))
+
         deal(nc.scalar.copy, x_bf[0], x_raw[0], 0, 48)
         deal(nc.vector.tensor_copy, x_bf[0], x_raw[0], 48, P)
         quantise_x(0)
-        sig0 = scores(0)
-        deal(nc.vector.tensor_copy, x_bf[1], x_raw[1], 0, P)
+        deal(nc.scalar.copy, x_bf[1], x_raw[1], 0, 48)
+        deal(nc.vector.tensor_copy, x_bf[1], x_raw[1], 48, P)
+        sig0 = [score(0, j) for j in range(PACK)]
         quantise_x(1)
-        sig1 = scores(1)
+        for j in range(3):
+            weigh_y(True, 0, j)
+        weigh_y(False, 0, 3)
+        sig1 = [score(1, j) for j in range(PACK)]
         for j in range(PACK):
-            nc.vector.tensor_scalar(y_raw[0][:, j, :], y_raw[0][:, j, :], weight[:, 0, j:j + 1], None, ALU.mult)
-        gradient(0, sig0)
+            gradient(0, j, sig0[j])
+        weave_g(nc.scalar.copy, 0, 0, 256)
         for j in range(PACK):
-            nc.scalar.activation(y_raw[1][:, j, :], y_raw[1][:, j, :], ACT.Copy, scale=weight[:, 1, j:j + 1])
-        weave_g(0)
-        deal(nc.scalar.copy, xm_bf[0], xm_raw[0], 0, P)
-        gradient(1, sig1)
+            weigh_y(True, 1, j)
+        gradient(1, 0, sig1[0])
+        weave_g(nc.vector.tensor_copy, 0, 256, N)
+        deal_xm(0, 0)
+        for j in range(1, PACK):
+            gradient(1, j, sig1[j])
+        deal_xm(1, 0)
         quantise_g(0)
-        weave_g(1)
-        deal(nc.scalar.copy, xm_bf[1], xm_raw[1], 0, 64)
-        nc.vector.quantize_mx(xm_codes[0][:].bitcast(E4), xm_scales[0][:], xm_bf[0][:].rearrange("p t m j -> p (t m j)"))
+        weave_g(nc.scalar.copy, 1, 0, 192)
+        weave_g(nc.vector.tensor_copy, 1, 192, N)
+        quantise_xm(0, 0)
+        quantise_xm(1, 0)
         quantise_g(1)
-        deal(nc.vector.tensor_copy, xm_bf[1], xm_raw[1], 64, P)
+        for g in range(PASSES):
+            deal_xm(g, 1)
 
-        grads = []
-        for t in range(PACK):
-            cols = slice(t * P, (t + 1) * P)
-            nc.vector.quantize_mx(xm_codes[1][:, cols].bitcast(E4), xm_scales[1][:, cols],
-                                  xm_bf[1][:, t, :, :].rearrange("p m j -> p (m j)"))
+        def table_gradient(t):
+            cols = slice((t % 2) * P, (t % 2 + 1) * P)
             acc = grad_psum.tile([P, N], F32, name="grad%d" % t)
             for g in range(PASSES):
-                nc.tensor.matmul_mx(acc[:], lhsT=xm_codes[g][:, cols].bitcast(E4), lhsT_scale=xm_scales[g][:, cols],
+                nc.tensor.matmul_mx(acc[:], lhsT=xm_codes[g][t // 2][:, cols].bitcast(E4),
+                                    lhsT_scale=xm_scales[g][t // 2][:, cols],
                                     rhs=g_codes[g][:].bitcast(E5), rhs_scale=g_scales[g][:],
                                     start=(g == 0), stop=(g == PASSES - 1))
-            grads.append(acc)
+            return acc
+
+        grads = [table_gradient(0), table_gradient(1)]
+        for g in range(PASSES):
+            quantise_xm(g, 1)
+        grads.extend([table_gradient(2), table_gradient(3)])
+        fresh = [sb([P, N], F32, "fresh%d" % t) for t in range(PACK)]
+        nc.vector.scalar_tensor_tensor(fresh[0][:], grads[0][:], -LR, decayed[:, 0, :], ALU.mult, ALU.add)
+        for t in range(1, PACK):
+            step = ring.tile([P, N], F32, name="step", bufs=3)
+            nc.scalar.activation(step[:], grads[t][:], ACT.Copy, scale=-LR)
+            nc.gpsimd.tensor_tensor(fresh[t][:], step[:], decayed[:, t, :], ALU.add)
 
         pairs = [sb([P, 2, 2 * CHUNK, 2], BF16, "pairs%d" % h, tag="x_raw%d" % h) for h in range(2)]
         for t in range(PACK):
-            fresh = ring.tile([P, N], F32, name="fresh", bufs=2)
-            nc.vector.scalar_tensor_tensor(fresh[:], grads[t][:], -LR, decayed[:, t, :], ALU.mult, ALU.add)
-            nc.vector.tensor_copy(window[t][:].indirect(offsets[:]), fresh[:])
+            nc.vector.tensor_copy(window[t][:].indirect(offsets[:]), fresh[t][:])
             nc.sync.dma_start(out_planes[:, t, :], window[t][:])
             if t < PACK - 1:
                 for h in range(2):
                     half = window[t][:, h * 2 * CHUNK:(h + 1) * 2 * CHUNK]
+                    nc.scalar.copy(pairs[h][:, t // 2, :, t % 2], half)
                     if (t, h) == (2, 0):
-                        nc.scalar.copy(pairs[h][:, 1, :, :], half.unsqueeze(2).to_broadcast([P, 2 * CHUNK, 2]))
-                    else:
-                        nc.scalar.copy(pairs[h][:, t // 2, :, t % 2], half)
+                        seam = slice(CHUNK - 8, CHUNK + 8)
+                        nc.scalar.copy(pairs[h][:, 1, seam, :], half[:, seam].unsqueeze(2).to_broadcast([P, 16, 2]))
 
         out_bf = [sb([P, CHUNK, PACK], BF16, "out_bf%d" % c, tag=("x_bf%d" % c if c < 2 else "g_rows%d" % (c - 2)))
                   for c in range(CHUNKS)]
@@ -203,5 +234,4 @@ def tile_attend_gnce_pl_sgd_kernel(tc, xT, wT, y, wt, xm, offs, out_0, out_1, ou
             quantise_out(c)
         scales_out = out_2[0].bitcast(I32)
         for q in range(4):
-            queue = nc.sync if q % 2 == 0 else nc.scalar
-            queue.dma_start(scales_out[4 * q:4 * q + 4, :], out_scales[32 * q:32 * q + 4, :].bitcast(I32))
+            nc.sync.dma_start(scales_out[4 * q:4 * q + 4, :], out_scales[32 * q:32 * q + 4, :].bitcast(I32))

@@ -67,13 +67,18 @@ def tile_attend_gnce_pl_sgd_kernel(tc, xT, wT, y, wt, xm, offs, out_0, out_1, ou
         picked = [sb([P, 2, N], F32, "picked%d" % u) for u in range(2)]
         w_bf = sb([P, N, PACK], BF16, "w_bf")
         decayed = sb([P, PACK, N], F32, "decayed")
-        for t in range(PACK):
+        for t in range(PACK - 1):
             nc.vector.tensor_copy(picked[t // 2][:, t % 2, :], source[t][:].indirect(offsets[:]))
             if t == 1:
                 nc.scalar.copy(w_bf[:, :, 0:2], picked[0][:].rearrange("p e n -> p n e"))
             if t < 2:
                 nc.scalar.activation(decayed[:, t, :], picked[0][:, t, :], ACT.Copy, scale=1.0 - LR * WD)
-        nc.vector.tensor_copy(w_bf[:, :, 2:4], picked[1][:].rearrange("p e n -> p n e"))
+        half = N // 2
+        for h in range(2):
+            nc.vector.tensor_copy(picked[1][:, 1, h * half:(h + 1) * half],
+                                  source[PACK - 1][:].indirect(offsets[:, h * half // 16:(h + 1) * half // 16]))
+        nc.scalar.copy(w_bf[:, 0:half, 2:4], picked[1][:, :, 0:half].rearrange("p e n -> p n e"))
+        nc.vector.tensor_copy(w_bf[:, half:N, 2:4], picked[1][:, :, half:N].rearrange("p e n -> p n e"))
         for t in range(2, PACK):
             nc.scalar.activation(decayed[:, t, :], picked[1][:, t - 2, :], ACT.Copy, scale=1.0 - LR * WD)
         w_codes = sb([P, N], U32, "w_codes")
@@ -89,9 +94,9 @@ def tile_attend_gnce_pl_sgd_kernel(tc, xT, wT, y, wt, xm, offs, out_0, out_1, ou
         x_bf = [sb([P, PACK, P, PACK], BF16, "x_bf%d" % g) for g in range(PASSES)]
         x_codes = [sb([P, 512], U32, "x_codes%d" % g) for g in range(PASSES)]
         x_scales = [sb([P, 512], U8, "x_scales%d" % g) for g in range(PASSES)]
-        xm_bf = [[sb([P, 2, P, PACK], BF16, "xm_bf%d%d" % (g, u)) for u in range(2)] for g in range(PASSES)]
-        xm_codes = [[sb([P, 2 * P], U32, "xm_codes%d%d" % (g, u)) for u in range(2)] for g in range(PASSES)]
-        xm_scales = [[sb([P, 2 * P], U8, "xm_scales%d%d" % (g, u)) for u in range(2)] for g in range(PASSES)]
+        xm_bf = [sb([P, PASSES, 2, P, PACK], BF16, "xm_bf0")]
+        xm_scales = [sb([P, PASSES, 2 * P], U8, "xm_scales%d" % u) for u in range(2)]
+        xm_codes = [sb([P, PASSES, 2 * P], U32, "xm_codes0")]
         g_rows = [sb([P, PACK, N], BF16, "g_rows%d" % g) for g in range(PASSES)]
         g_bf = [sb([P, N, PACK], BF16, "g_bf%d" % g) for g in range(PASSES)]
         g_codes = [sb([P, N], U32, "g_codes%d" % g) for g in range(PASSES)]
@@ -129,13 +134,13 @@ def tile_attend_gnce_pl_sgd_kernel(tc, xT, wT, y, wt, xm, offs, out_0, out_1, ou
 
         def deal_xm(g, u):
             nc.scalar.copy(
-                xm_bf[g][u][:].rearrange("p e m j -> p m j e"),
+                xm_bf[u][:, g].rearrange("p e m j -> p m j e"),
                 xm_raw[g][:].rearrange("p j (m t) -> p m j t", t=PACK)[:, :, :, 2 * u:2 * u + 2],
             )
 
-        def quantise_xm(g, u):
-            nc.vector.quantize_mx(xm_codes[g][u][:].bitcast(E4), xm_scales[g][u][:],
-                                  xm_bf[g][u][:].rearrange("p e m j -> p (e m j)"))
+        def quantise_xm(g):
+            nc.vector.quantize_mx(xm_codes[0][:, g, :].bitcast(E4), xm_scales[0][:, g, :],
+                                  xm_bf[0][:, g].rearrange("p e m j -> p (e m j)"))
 
         deal(nc.scalar.copy, x_bf[0], x_raw[0], 0, 48)
         deal(nc.vector.tensor_copy, x_bf[0], x_raw[0], 48, P)
@@ -144,27 +149,25 @@ def tile_attend_gnce_pl_sgd_kernel(tc, xT, wT, y, wt, xm, offs, out_0, out_1, ou
         deal(nc.vector.tensor_copy, x_bf[1], x_raw[1], 48, P)
         sig0 = [score(0, j) for j in range(PACK)]
         quantise_x(1)
-        for j in range(3):
+        for j in range(PACK):
             weigh_y(True, 0, j)
-        weigh_y(False, 0, 3)
         sig1 = [score(1, j) for j in range(PACK)]
         for j in range(PACK):
             gradient(0, j, sig0[j])
-        weave_g(nc.scalar.copy, 0, 0, 256)
         for j in range(PACK):
             weigh_y(True, 1, j)
+        weave_g(nc.scalar.copy, 0, 0, N)
         gradient(1, 0, sig1[0])
-        weave_g(nc.vector.tensor_copy, 0, 256, N)
         deal_xm(0, 0)
         for j in range(1, PACK):
             gradient(1, j, sig1[j])
         deal_xm(1, 0)
         quantise_g(0)
-        weave_g(nc.scalar.copy, 1, 0, 192)
-        weave_g(nc.vector.tensor_copy, 1, 192, N)
-        quantise_xm(0, 0)
-        quantise_xm(1, 0)
+        quantise_xm(0)
+        weave_g(nc.vector.tensor_copy, 1, 0, N)
+        quantise_xm(1)
         quantise_g(1)
+        xm_bf.append(sb([P, PASSES, 2, P, PACK], BF16, "xm_bf1", tag="xm_bf0"))
         for g in range(PASSES):
             deal_xm(g, 1)
 
@@ -172,66 +175,78 @@ def tile_attend_gnce_pl_sgd_kernel(tc, xT, wT, y, wt, xm, offs, out_0, out_1, ou
             cols = slice((t % 2) * P, (t % 2 + 1) * P)
             acc = grad_psum.tile([P, N], F32, name="grad%d" % t)
             for g in range(PASSES):
-                nc.tensor.matmul_mx(acc[:], lhsT=xm_codes[g][t // 2][:, cols].bitcast(E4),
-                                    lhsT_scale=xm_scales[g][t // 2][:, cols],
+                nc.tensor.matmul_mx(acc[:], lhsT=xm_codes[t // 2][:, g, cols].bitcast(E4),
+                                    lhsT_scale=xm_scales[t // 2][:, g, cols],
                                     rhs=g_codes[g][:].bitcast(E5), rhs_scale=g_scales[g][:],
                                     start=(g == 0), stop=(g == PASSES - 1))
             return acc
 
         grads = [table_gradient(0), table_gradient(1)]
-        for g in range(PASSES):
-            quantise_xm(g, 1)
-        grads.extend([table_gradient(2), table_gradient(3)])
         fresh = [sb([P, N], F32, "fresh%d" % t) for t in range(PACK)]
-        nc.vector.scalar_tensor_tensor(fresh[0][:], grads[0][:], -LR, decayed[:, 0, :], ALU.mult, ALU.add)
-        for t in range(1, PACK):
-            step = ring.tile([P, N], F32, name="step", bufs=3)
-            nc.scalar.activation(step[:], grads[t][:], ACT.Copy, scale=-LR)
-            nc.gpsimd.tensor_tensor(fresh[t][:], step[:], decayed[:, t, :], ALU.add)
+
+        def update(t):
+            nc.vector.scalar_tensor_tensor(fresh[t][:], grads[t][:], -LR, decayed[:, t, :], ALU.mult, ALU.add)
+
+        update(0)
+        update(1)
 
         pairs = [sb([P, 2, 2 * CHUNK, 2], BF16, "pairs%d" % h, tag="x_raw%d" % h) for h in range(2)]
         for t in range(PACK):
+            if t == 2:
+                update(2)
+                update(3)
             nc.vector.tensor_copy(window[t][:].indirect(offsets[:]), fresh[t][:])
+            if t == 0:
+                xm_codes.append(sb([P, PASSES, 2 * P], U32, "xm_codes1", tag="fresh0"))
+                nc.vector.quantize_mx(xm_codes[1][:].rearrange("p g c -> p (g c)").bitcast(E4),
+                                      xm_scales[1][:].rearrange("p g c -> p (g c)"),
+                                      xm_bf[1][:].rearrange("p g e m j -> p (g e m j)"))
+                grads.extend([table_gradient(2), table_gradient(3)])
             nc.sync.dma_start(out_planes[:, t, :], window[t][:])
             if t < PACK - 1:
                 for h in range(2):
-                    half = window[t][:, h * 2 * CHUNK:(h + 1) * 2 * CHUNK]
-                    nc.scalar.copy(pairs[h][:, t // 2, :, t % 2], half)
+                    span = window[t][:, h * 2 * CHUNK:(h + 1) * 2 * CHUNK]
+                    nc.scalar.copy(pairs[h][:, t // 2, :, t % 2], span)
                     if (t, h) == (2, 0):
                         seam = slice(CHUNK - 8, CHUNK + 8)
-                        nc.scalar.copy(pairs[h][:, 1, seam, :], half[:, seam].unsqueeze(2).to_broadcast([P, 16, 2]))
+                        nc.scalar.copy(pairs[h][:, 1, seam, :], span[:, seam].unsqueeze(2).to_broadcast([P, 16, 2]))
 
-        out_bf = [sb([P, CHUNK, PACK], BF16, "out_bf%d" % c, tag=("x_bf%d" % c if c < 2 else "g_rows%d" % (c - 2)))
-                  for c in range(CHUNKS)]
-        out_codes = [sb([P, CHUNK], U32, "out_codes%d" % c) for c in range(CHUNKS)]
+        pieces = [(0, 512), (512, 1024), (1024, 1536), (1536, 1792), (1792, 2048)]
+        reuse = ["x_bf0", "x_bf1", "g_rows0", "g_bf1", "g_bf0"]
+        out_bf = [sb([P, hi - lo, PACK], BF16, "out_bf%d" % c, tag=reuse[c]) for c, (lo, hi) in enumerate(pieces)]
+        out_codes = [sb([P, hi - lo], U32, "out_codes%d" % c) for c, (lo, hi) in enumerate(pieces)]
         out_scales = sb([P, T], U8, "out_scales")
         words_out = out_1[0].rearrange("p c l -> p (c l)").bitcast(I32)
 
         def last_plane(engine_copy, c):
-            lo = (c % 2) * CHUNK
-            engine_copy(pairs[c // 2][:, 1, lo:lo + CHUNK, 1], window[PACK - 1][:, c * CHUNK:(c + 1) * CHUNK])
+            lo, hi = pieces[c]
+            h = lo // (2 * CHUNK)
+            base = h * 2 * CHUNK
+            engine_copy(pairs[h][:, 1, lo - base:hi - base, 1], window[PACK - 1][:, lo:hi])
 
         def weave_out(engine_copy, word, c):
-            lo = (c % 2) * CHUNK
-            src = pairs[c // 2][:].rearrange("p u n e -> p u (n e)").bitcast(word)[:, :, lo:lo + CHUNK]
+            lo, hi = pieces[c]
+            h = lo // (2 * CHUNK)
+            base = h * 2 * CHUNK
+            src = pairs[h][:].rearrange("p u n e -> p u (n e)").bitcast(word)[:, :, lo - base:hi - base]
             dst = out_bf[c][:].rearrange("p n t -> p (n t)").bitcast(word).rearrange("p (n u) -> p n u", u=2)
             engine_copy(dst, src.rearrange("p u n -> p n u"))
 
-        def quantise_out(c):
-            cols = slice(c * CHUNK, (c + 1) * CHUNK)
+        def quantise_out(c, queue):
+            cols = slice(pieces[c][0], pieces[c][1])
             nc.vector.quantize_mx(out_codes[c][:].bitcast(E4), out_scales[:, cols],
                                   out_bf[c][:].rearrange("p n t -> p (n t)"))
-            nc.sync.dma_start(words_out[:, cols], out_codes[c][:].bitcast(I32))
+            queue.dma_start(words_out[:, cols], out_codes[c][:].bitcast(I32))
 
         for c in (0, 1):
             last_plane(nc.vector.tensor_copy, c)
-        for c in (2, 3):
+        for c in (2, 3, 4):
             last_plane(nc.scalar.copy, c)
             weave_out(nc.scalar.copy, U32, c)
         for c in (0, 1):
             weave_out(nc.vector.tensor_copy, I32, c)
-        for c in range(CHUNKS):
-            quantise_out(c)
+        for c in range(len(pieces)):
+            quantise_out(c, nc.sync)
         scales_out = out_2[0].bitcast(I32)
         for q in range(4):
             nc.sync.dma_start(scales_out[4 * q:4 * q + 4, :], out_scales[32 * q:32 * q + 4, :].bitcast(I32))

@@ -187,14 +187,18 @@ def tile_attend_gnce_pl_sgd_kernel(tc, xT, wT, y, wt, xm, offs, out_0, out_1, ou
         def update(t):
             nc.vector.scalar_tensor_tensor(fresh[t][:], grads[t][:], -LR, decayed[:, t, :], ALU.mult, ALU.add)
 
+        def update_beside(t):
+            step = sb([P, N], F32, "step%d" % t)
+            nc.scalar.activation(step[:], grads[t][:], ACT.Copy, scale=-LR)
+            nc.gpsimd.tensor_tensor(fresh[t][:], step[:], decayed[:, t, :], ALU.add)
+
         update(0)
-        update(1)
+        update_beside(1)
 
         pairs = [sb([P, 2, 2 * CHUNK, 2], BF16, "pairs%d" % h, tag="x_raw%d" % h) for h in range(2)]
         for t in range(PACK):
             if t == 2:
                 update(2)
-                update(3)
             nc.vector.tensor_copy(window[t][:].indirect(offsets[:]), fresh[t][:])
             if t == 0:
                 xm_codes.append(sb([P, PASSES, 2 * P], U32, "xm_codes1", tag="fresh0"))
@@ -202,6 +206,7 @@ def tile_attend_gnce_pl_sgd_kernel(tc, xT, wT, y, wt, xm, offs, out_0, out_1, ou
                                       xm_scales[1][:].rearrange("p g c -> p (g c)"),
                                       xm_bf[1][:].rearrange("p g e m j -> p (g e m j)"))
                 grads.extend([table_gradient(2), table_gradient(3)])
+                update_beside(3)
             nc.sync.dma_start(out_planes[:, t, :], window[t][:])
             if t < PACK - 1:
                 for h in range(2):
@@ -224,13 +229,12 @@ def tile_attend_gnce_pl_sgd_kernel(tc, xT, wT, y, wt, xm, offs, out_0, out_1, ou
             base = h * 2 * CHUNK
             engine_copy(pairs[h][:, 1, lo - base:hi - base, 1], window[PACK - 1][:, lo:hi])
 
-        def weave_out(engine_copy, word, c):
-            lo, hi = pieces[c]
+        def weave_out(engine_copy, word, c, lo, hi):
             h = lo // (2 * CHUNK)
             base = h * 2 * CHUNK
             src = pairs[h][:].rearrange("p u n e -> p u (n e)").bitcast(word)[:, :, lo - base:hi - base]
             dst = out_bf[c][:].rearrange("p n t -> p (n t)").bitcast(word).rearrange("p (n u) -> p n u", u=2)
-            engine_copy(dst, src.rearrange("p u n -> p n u"))
+            engine_copy(dst[:, lo - pieces[c][0]:hi - pieces[c][0], :], src.rearrange("p u n -> p n u"))
 
         def quantise_out(c, queue):
             cols = slice(pieces[c][0], pieces[c][1])
@@ -242,9 +246,10 @@ def tile_attend_gnce_pl_sgd_kernel(tc, xT, wT, y, wt, xm, offs, out_0, out_1, ou
             last_plane(nc.vector.tensor_copy, c)
         for c in (2, 3, 4):
             last_plane(nc.scalar.copy, c)
-            weave_out(nc.scalar.copy, U32, c)
+            weave_out(nc.scalar.copy, U32, c, max(pieces[c][0], 1280), pieces[c][1])
         for c in (0, 1):
-            weave_out(nc.vector.tensor_copy, I32, c)
+            weave_out(nc.vector.tensor_copy, I32, c, pieces[c][0], pieces[c][1])
+        weave_out(nc.vector.tensor_copy, I32, 2, 1024, 1280)
         for c in range(len(pieces)):
             quantise_out(c, nc.sync)
         scales_out = out_2[0].bitcast(I32)

@@ -60,9 +60,6 @@ def tile_attend_gnce_pl_sgd_kernel(tc, xT, wT, y, wt, xm, offs, out_0, out_1, ou
         for t in range(PACK):
             nc.sync.dma_start(window[t][:], w_planes[:, t, :])
 
-        warm = sb([P, 16], F32, "warm")
-        nc.vector.memset(warm[:, 0:8], 0.0)
-        nc.scalar.activation(warm[:, 8:16], warm[:, 0:8], ACT.Sigmoid)
 
         picked = [sb([P, 2, N], F32, "picked%d" % u) for u in range(2)]
         w_bf = sb([P, N, PACK], BF16, "w_bf")

@@ -28,7 +28,6 @@ def tile_attend_gnce_pl_sgd_kernel(tc, xT, wT, y, wt, xm, offs, out_0, out_1, ou
     nc = tc.nc
     with ExitStack() as ctx:
         held = ctx.enter_context(tc.tile_pool(name="held", bufs=1))
-        ring = ctx.enter_context(tc.tile_pool(name="ring", bufs=4))
         score_psum = ctx.enter_context(tc.psum_pool(name="score_psum", bufs=4))
         grad_psum = ctx.enter_context(tc.psum_pool(name="grad_psum", bufs=1))
 
@@ -47,13 +46,17 @@ def tile_attend_gnce_pl_sgd_kernel(tc, xT, wT, y, wt, xm, offs, out_0, out_1, ou
         y_raw = [[sb([P, 2, N], F32, "y_raw%d%d" % (g, u)) for u in range(2)] for g in range(PASSES)]
         xm_raw = [sb([P, PACK, D], F32, "xm_raw%d" % g) for g in range(PASSES)]
         weight = sb([P, PASSES, 8], F32, "weight")
+        nc.scalar.dma_start(weight[:, :, 0:PACK], wt[0].rearrange("(g p j) o -> p g (j o)", g=PASSES, j=PACK))
         for g in range(PASSES):
             nc.sync.dma_start(x_raw[g][:], xT[0, :, g * 512:(g + 1) * 512].rearrange("(p t) r -> p t r", t=PACK))
-        nc.sync.dma_start(weight[:, :, 0:PACK], wt[0].rearrange("(g p j) o -> p g (j o)", g=PASSES, j=PACK))
         for g in range(PASSES):
             y_rows = y[0, g * 512:(g + 1) * 512, :].rearrange("(p j) n -> p j n", j=PACK)
             for u in range(2):
-                nc.sync.dma_start(y_raw[g][u][:], y_rows[:, 2 * u:2 * u + 2, :])
+                if (g, u) == (0, 0):
+                    for e in range(2):
+                        nc.sync.dma_start(y_raw[g][u][:, e, :], y_rows[:, e, :])
+                else:
+                    nc.sync.dma_start(y_raw[g][u][:], y_rows[:, 2 * u:2 * u + 2, :])
         for g in range(PASSES):
             nc.sync.dma_start(xm_raw[g][:], xm[0, g * 512:(g + 1) * 512, :].rearrange("(p j) d -> p j d", j=PACK))
         window = [sb([P, T], F32, "window%d" % t) for t in range(PACK)]
@@ -61,6 +64,8 @@ def tile_attend_gnce_pl_sgd_kernel(tc, xT, wT, y, wt, xm, offs, out_0, out_1, ou
             nc.sync.dma_start(window[t][:], w_planes[:, t, :])
 
 
+        warm = sb([P, 1], F32, "warm")
+        nc.scalar.activation(warm[:], weight[:, 0, 0:1], ACT.Sigmoid)
         picked = [sb([P, 2, N], F32, "picked%d" % u) for u in range(2)]
         w_bf = sb([P, N, PACK], BF16, "w_bf")
         decayed = sb([P, PACK, N], F32, "decayed")
@@ -68,16 +73,13 @@ def tile_attend_gnce_pl_sgd_kernel(tc, xT, wT, y, wt, xm, offs, out_0, out_1, ou
             nc.vector.tensor_copy(picked[t // 2][:, t % 2, :], source[t][:].indirect(offsets[:]))
             if t == 1:
                 nc.scalar.copy(w_bf[:, :, 0:2], picked[0][:].rearrange("p e n -> p n e"))
-            if t < 2:
-                nc.scalar.activation(decayed[:, t, :], picked[0][:, t, :], ACT.Copy, scale=1.0 - LR * WD)
+            nc.scalar.activation(decayed[:, t, :], picked[t // 2][:, t % 2, :], ACT.Copy, scale=1.0 - LR * WD)
         half = N // 2
         for h in range(2):
             nc.vector.tensor_copy(picked[1][:, 1, h * half:(h + 1) * half],
                                   source[PACK - 1][:].indirect(offsets[:, h * half // 16:(h + 1) * half // 16]))
         nc.scalar.copy(w_bf[:, 0:half, 2:4], picked[1][:, :, 0:half].rearrange("p e n -> p n e"))
         nc.vector.tensor_copy(w_bf[:, half:N, 2:4], picked[1][:, :, half:N].rearrange("p e n -> p n e"))
-        for t in range(2, PACK):
-            nc.scalar.activation(decayed[:, t, :], picked[1][:, t - 2, :], ACT.Copy, scale=1.0 - LR * WD)
         w_codes = sb([P, N], U32, "w_codes")
         w_scales = sb([P, N], U8, "w_scales")
         nc.vector.quantize_mx(w_codes[:].bitcast(E4), w_scales[:], w_bf[:].rearrange("p n t -> p (n t)"))
@@ -91,12 +93,12 @@ def tile_attend_gnce_pl_sgd_kernel(tc, xT, wT, y, wt, xm, offs, out_0, out_1, ou
         x_bf = [sb([P, PACK, P, PACK], BF16, "x_bf%d" % g) for g in range(PASSES)]
         x_codes = [sb([P, 512], U32, "x_codes%d" % g) for g in range(PASSES)]
         x_scales = [sb([P, 512], U8, "x_scales%d" % g) for g in range(PASSES)]
-        xm_bf = [sb([P, PASSES, 2, P, PACK], BF16, "xm_bf0")]
         xm_scales = [sb([P, PASSES, 2 * P], U8, "xm_scales%d" % u) for u in range(2)]
         xm_codes = [sb([P, PASSES, 2 * P], U32, "xm_codes0")]
+        xm_late = [sb([P, 2, P, PACK], BF16, "xm_late0")]
         g_rows = [sb([P, PACK, N], BF16, "g_rows%d" % g) for g in range(PASSES)]
         g_bf = [sb([P, N, PACK], BF16, "g_bf%d" % g) for g in range(PASSES)]
-        g_codes = [sb([P, N], U32, "g_codes%d" % g) for g in range(PASSES)]
+        g_codes = [sb([P, N], U32, "g_codes0")]
         g_scales = [sb([P, N], U8, "g_scales%d" % g) for g in range(PASSES)]
 
         def quantise_x(g):
@@ -107,9 +109,8 @@ def tile_attend_gnce_pl_sgd_kernel(tc, xT, wT, y, wt, xm, offs, out_0, out_1, ou
             cols = slice(j * P, (j + 1) * P)
             nc.tensor.matmul_mx(bank[:], lhsT=x_codes[g][:, cols].bitcast(E4), lhsT_scale=x_scales[g][:, cols],
                                 rhs=w_codes[:].bitcast(E4), rhs_scale=w_scales[:], start=True, stop=True)
-            s = ring.tile([P, N], F32, name="sig", bufs=8)
-            nc.scalar.activation(s[:], bank[:], ACT.Sigmoid)
-            return s
+            nc.scalar.activation(sig_rows[g][:, j, :], bank[:], ACT.Sigmoid)
+            return sig_rows[g][:, j, :]
 
         def weigh_y(on_vector, g, j):
             rows = y_raw[g][j // 2][:, j % 2, :]
@@ -119,7 +120,7 @@ def tile_attend_gnce_pl_sgd_kernel(tc, xT, wT, y, wt, xm, offs, out_0, out_1, ou
                 nc.scalar.activation(rows, rows, ACT.Copy, scale=weight[:, g, j:j + 1])
 
         def gradient(g, j, sig):
-            nc.vector.scalar_tensor_tensor(g_rows[g][:, j, :], sig[:], weight[:, g, j:j + 1],
+            nc.vector.scalar_tensor_tensor(g_rows[g][:, j, :], sig, weight[:, g, j:j + 1],
                                            y_raw[g][j // 2][:, j % 2, :], ALU.mult, ALU.subtract)
 
         def weave_g(engine_copy, g, lo, hi):
@@ -129,89 +130,99 @@ def tile_attend_gnce_pl_sgd_kernel(tc, xT, wT, y, wt, xm, offs, out_0, out_1, ou
         def quantise_g(g):
             nc.vector.quantize_mx(g_codes[g][:].bitcast(E5), g_scales[g][:], g_bf[g][:].rearrange("p n j -> p (n j)"))
 
-        def deal_xm(g, u):
-            nc.scalar.copy(
-                xm_bf[u][:, g].rearrange("p e m j -> p m j e"),
+        def deal_xm(engine_copy, dst, g, u):
+            engine_copy(
+                dst.rearrange("p e m j -> p m j e"),
                 xm_raw[g][:].rearrange("p j (m t) -> p m j t", t=PACK)[:, :, :, 2 * u:2 * u + 2],
             )
 
-        def quantise_xm(g):
-            nc.vector.quantize_mx(xm_codes[0][:, g, :].bitcast(E4), xm_scales[0][:, g, :],
-                                  xm_bf[0][:, g].rearrange("p e m j -> p (e m j)"))
-
-        deal(nc.scalar.copy, x_bf[0], x_raw[0], 0, 48)
-        deal(nc.vector.tensor_copy, x_bf[0], x_raw[0], 48, P)
-        quantise_x(0)
-        deal(nc.scalar.copy, x_bf[1], x_raw[1], 0, 48)
-        deal(nc.vector.tensor_copy, x_bf[1], x_raw[1], 48, P)
-        sig0 = [score(0, j) for j in range(PACK)]
-        quantise_x(1)
-        for j in range(PACK):
-            weigh_y(True, 0, j)
-        sig1 = [score(1, j) for j in range(PACK)]
-        for j in range(PACK):
-            gradient(0, j, sig0[j])
-        for j in range(PACK):
-            weigh_y(True, 1, j)
-        weave_g(nc.scalar.copy, 0, 0, N)
-        gradient(1, 0, sig1[0])
-        deal_xm(0, 0)
-        for j in range(1, PACK):
-            gradient(1, j, sig1[j])
-        deal_xm(1, 0)
-        quantise_g(0)
-        quantise_xm(0)
-        weave_g(nc.vector.tensor_copy, 1, 0, N)
-        quantise_xm(1)
-        quantise_g(1)
-        xm_bf.append(sb([P, PASSES, 2, P, PACK], BF16, "xm_bf1", tag="xm_bf0"))
-        for g in range(PASSES):
-            deal_xm(g, 1)
+        def quantise_xm(u, g, src):
+            nc.vector.quantize_mx(xm_codes[u][:, g, :].bitcast(E4), xm_scales[u][:, g, :],
+                                  src.rearrange("p e m j -> p (e m j)"))
 
         def table_gradient(t):
             cols = slice((t % 2) * P, (t % 2 + 1) * P)
             acc = grad_psum.tile([P, N], F32, name="grad%d" % t)
-            for g in range(PASSES):
+            order = range(PASSES - 1, -1, -1) if t == 1 else range(PASSES)
+            for g in order:
                 nc.tensor.matmul_mx(acc[:], lhsT=xm_codes[t // 2][:, g, cols].bitcast(E4),
                                     lhsT_scale=xm_scales[t // 2][:, g, cols],
                                     rhs=g_codes[g][:].bitcast(E5), rhs_scale=g_scales[g][:],
-                                    start=(g == 0), stop=(g == PASSES - 1))
+                                    start=(g == order[0]), stop=(g == order[-1]))
             return acc
 
-        grads = [table_gradient(0), table_gradient(1)]
-        fresh = [sb([P, N], F32, "fresh%d" % t) for t in range(PACK)]
+        step = [None] + [sb([P, N], F32, "step%d" % t) for t in range(1, PACK)]
 
-        def update(t):
-            nc.vector.scalar_tensor_tensor(fresh[t][:], grads[t][:], -LR, decayed[:, t, :], ALU.mult, ALU.add)
+        def make_step(t):
+            nc.scalar.activation(step[t][:], table_gradient(t)[:], ACT.Copy, scale=-LR)
 
-        def update_beside(t):
-            step = sb([P, N], F32, "step%d" % t)
-            nc.scalar.activation(step[:], grads[t][:], ACT.Copy, scale=-LR)
-            nc.gpsimd.tensor_tensor(fresh[t][:], step[:], decayed[:, t, :], ALU.add)
-
-        update(0)
-        update_beside(1)
+        deal(nc.scalar.copy, x_bf[0], x_raw[0], 0, 56)
+        deal(nc.vector.tensor_copy, x_bf[0], x_raw[0], 56, P)
+        quantise_x(0)
+        deal(nc.scalar.copy, x_bf[1], x_raw[1], 0, 56)
+        deal(nc.vector.tensor_copy, x_bf[1], x_raw[1], 56, P)
+        sig_rows = [sb([P, PACK, N], F32, "sig_rows0", tag="x_raw1"), sb([P, PACK, N], F32, "sig_rows1")]
+        nc.scalar.activation(decayed[:, 3, :], picked[1][:, 1, :], ACT.Copy, scale=1.0 - LR * WD)
+        sig0 = [score(0, j) for j in range(PACK)]
+        weigh_y(True, 0, 0)
+        weigh_y(True, 0, 1)
+        quantise_x(1)
+        sig1 = [score(1, j) for j in range(PACK)]
+        gradient(0, 0, sig0[0])
+        weigh_y(True, 0, 2)
+        gradient(0, 1, sig0[1])
+        weigh_y(True, 0, 3)
+        gradient(0, 2, sig0[2])
+        gradient(0, 3, sig0[3])
+        weave_g(nc.scalar.copy, 0, 0, N)
+        weigh_y(True, 1, 0)
+        weigh_y(True, 1, 1)
+        gradient(1, 0, sig1[0])
+        weigh_y(True, 1, 2)
+        gradient(1, 1, sig1[1])
+        weigh_y(True, 1, 3)
+        gradient(1, 2, sig1[2])
+        gradient(1, 3, sig1[3])
+        xm_bf = [sb([P, PASSES, 2, P, PACK], BF16, "xm_bf0", tag="x_raw0")]
+        deal_xm(nc.scalar.copy, xm_bf[0][:, 0], 0, 0)
+        deal_xm(nc.scalar.copy, xm_bf[0][:, 1], 1, 0)
+        deal_xm(nc.scalar.copy, xm_late[0][:], 1, 1)
+        quantise_g(0)
+        weave_g(nc.vector.tensor_copy, 1, 0, N)
+        nc.vector.quantize_mx(xm_codes[0][:].rearrange("p g c -> p (g c)").bitcast(E4),
+                              xm_scales[0][:].rearrange("p g c -> p (g c)"),
+                              xm_bf[0][:].rearrange("p g e m j -> p (g e m j)"))
+        g_codes.append(sb([P, N], U32, "g_codes1", tag="x_raw0"))
+        quantise_g(1)
+        xm_late.append(sb([P, 2, P, PACK], BF16, "xm_late1", tag="xm_raw1"))
+        deal_xm(nc.scalar.copy, xm_late[1][:], 0, 1)
+        xm_codes.append(sb([P, PASSES, 2 * P], U32, "xm_codes1", tag="x_raw1"))
+        quantise_xm(1, 1, xm_late[0][:])
+        fresh = [sb([P, N], F32, "fresh0")]
+        nc.vector.scalar_tensor_tensor(fresh[0][:], table_gradient(0)[:], -LR, decayed[:, 0, :], ALU.mult, ALU.add)
+        quantise_xm(1, 0, xm_late[1][:])
+        later = sb([P, PACK - 1, N], F32, "later", tag="xm_raw1")
+        for t in range(1, PACK):
+            make_step(t)
+            nc.gpsimd.tensor_tensor(later[:, t - 1, :], step[t][:], decayed[:, t, :], ALU.add)
+            fresh.append(later[:, t - 1, :])
 
         pairs = [sb([P, 2, 2 * CHUNK, 2], BF16, "pairs%d" % h, tag="x_raw%d" % h) for h in range(2)]
         for t in range(PACK):
-            if t == 2:
-                update(2)
             nc.vector.tensor_copy(window[t][:].indirect(offsets[:]), fresh[t][:])
-            if t == 0:
-                xm_codes.append(sb([P, PASSES, 2 * P], U32, "xm_codes1", tag="fresh0"))
-                nc.vector.quantize_mx(xm_codes[1][:].rearrange("p g c -> p (g c)").bitcast(E4),
-                                      xm_scales[1][:].rearrange("p g c -> p (g c)"),
-                                      xm_bf[1][:].rearrange("p g e m j -> p (g e m j)"))
-                grads.extend([table_gradient(2), table_gradient(3)])
-                update_beside(3)
             nc.sync.dma_start(out_planes[:, t, :], window[t][:])
             if t < PACK - 1:
-                for h in range(2):
-                    span = window[t][:, h * 2 * CHUNK:(h + 1) * 2 * CHUNK]
-                    nc.scalar.copy(pairs[h][:, t // 2, :, t % 2], span)
-                    if (t, h) == (2, 0):
-                        seam = slice(CHUNK - 8, CHUNK + 8)
-                        nc.scalar.copy(pairs[h][:, 1, seam, :], span[:, seam].unsqueeze(2).to_broadcast([P, 16, 2]))
+                nc.scalar.copy(pairs[0][:, t // 2, :, t % 2], window[t][:, 0:2 * CHUNK])
+                if t == 2:
+                    seam = slice(CHUNK - 8, CHUNK + 8)
+                    nc.scalar.copy(pairs[0][:, 1, seam, :], window[t][:, seam].unsqueeze(2).to_broadcast([P, 16, 2]))
+                nc.scalar.copy(pairs[1][:, t // 2, 0:CHUNK, t % 2], window[t][:, 2 * CHUNK:3 * CHUNK])
+                far = window[t][:, 3 * CHUNK:T]
+                if t < 2:
+                    nc.gpsimd.tensor_scalar(pairs[1][:, 0, CHUNK:2 * CHUNK, t], far, 1.0, -0.0, ALU.mult, ALU.add)
+                else:
+                    nc.gpsimd.tensor_scalar(pairs[1][:, 1, CHUNK:2 * CHUNK, :], far.unsqueeze(2).to_broadcast([P, CHUNK, 2]),
+                                            1.0, -0.0, ALU.mult, ALU.add)
 
         pieces = [(0, 512), (512, 1024), (1024, 1536), (1536, 1792), (1792, 2048)]
         reuse = ["x_bf0", "x_bf1", "g_rows0", "g_bf1", "g_bf0"]
@@ -243,10 +254,9 @@ def tile_attend_gnce_pl_sgd_kernel(tc, xT, wT, y, wt, xm, offs, out_0, out_1, ou
             last_plane(nc.vector.tensor_copy, c)
         for c in (2, 3, 4):
             last_plane(nc.scalar.copy, c)
-            weave_out(nc.scalar.copy, U32, c, max(pieces[c][0], 1280), pieces[c][1])
+            weave_out(nc.scalar.copy, U32, c, pieces[c][0], pieces[c][1])
         for c in (0, 1):
             weave_out(nc.vector.tensor_copy, I32, c, pieces[c][0], pieces[c][1])
-        weave_out(nc.vector.tensor_copy, I32, 2, 1024, 1280)
         for c in range(len(pieces)):
             quantise_out(c, nc.sync)
         scales_out = out_2[0].bitcast(I32)

@@ -60,8 +60,7 @@ def tile_attend_gnce_pl_sgd_kernel(tc, xT, wT, y, wt, xm, offs, out_0, out_1, ou
         for g in range(PASSES):
             nc.sync.dma_start(xm_raw[g][:], xm[0, g * 512:(g + 1) * 512, :].rearrange("(p j) d -> p j d", j=PACK))
         window = [sb([P, T], F32, "window%d" % t) for t in range(PACK)]
-        for t in range(PACK):
-            nc.sync.dma_start(window[t][:], w_planes[:, t, :])
+        nc.sync.dma_start(window[PACK - 1][:], w_planes[:, PACK - 1, :])
 
 
         warm = sb([P, 1], F32, "warm")
@@ -71,6 +70,10 @@ def tile_attend_gnce_pl_sgd_kernel(tc, xT, wT, y, wt, xm, offs, out_0, out_1, ou
         decayed = sb([P, PACK, N], F32, "decayed")
         for t in range(PACK - 1):
             nc.vector.tensor_copy(picked[t // 2][:, t % 2, :], source[t][:].indirect(offsets[:]))
+            if t == 0:
+                nc.scalar.activation(window[t][:], source[t][:], ACT.Copy)
+            else:
+                nc.vector.tensor_copy(window[t][:], source[t][:])
             if t == 1:
                 nc.scalar.copy(w_bf[:, :, 0:2], picked[0][:].rearrange("p e n -> p n e"))
             nc.scalar.activation(decayed[:, t, :], picked[t // 2][:, t % 2, :], ACT.Copy, scale=1.0 - LR * WD)

@@ -43,7 +43,7 @@ def tile_attend_gnce_pl_sgd_kernel(tc, xT, wT, y, wt, xm, offs, out_0, out_1, ou
         for t in range(PACK):
             nc.sync.dma_start(source[t][:], w_planes[:, t, :])
         x_raw = [sb([P, PACK, 512], F32, "x_raw%d" % g) for g in range(PASSES)]
-        y_raw = [[sb([P, 2, N], F32, "y_raw%d%d" % (g, u)) for u in range(2)] for g in range(PASSES)]
+        y_raw = [sb([P, PACK, N], F32, "y_raw%d" % g) for g in range(PASSES)]
         xm_raw = [sb([P, PACK, D], F32, "xm_raw%d" % g) for g in range(PASSES)]
         weight = sb([P, PASSES, 8], F32, "weight")
         nc.scalar.dma_start(weight[:, :, 0:PACK], wt[0].rearrange("(g p j) o -> p g (j o)", g=PASSES, j=PACK))
@@ -51,16 +51,11 @@ def tile_attend_gnce_pl_sgd_kernel(tc, xT, wT, y, wt, xm, offs, out_0, out_1, ou
             nc.sync.dma_start(x_raw[g][:], xT[0, :, g * 512:(g + 1) * 512].rearrange("(p t) r -> p t r", t=PACK))
         for g in range(PASSES):
             y_rows = y[0, g * 512:(g + 1) * 512, :].rearrange("(p j) n -> p j n", j=PACK)
-            for u in range(2):
-                if (g, u) == (0, 0):
-                    for e in range(2):
-                        nc.sync.dma_start(y_raw[g][u][:, e, :], y_rows[:, e, :])
-                else:
-                    nc.sync.dma_start(y_raw[g][u][:], y_rows[:, 2 * u:2 * u + 2, :])
+            for lo, hi in ((0, 1), (1, 2), (2, 4)) if g == 0 else ((0, PACK),):
+                nc.sync.dma_start(y_raw[g][:, lo:hi, :], y_rows[:, lo:hi, :])
         for g in range(PASSES):
             nc.sync.dma_start(xm_raw[g][:], xm[0, g * 512:(g + 1) * 512, :].rearrange("(p j) d -> p j d", j=PACK))
-        window = [sb([P, T], F32, "window%d" % t) for t in range(PACK)]
-        nc.sync.dma_start(window[PACK - 1][:], w_planes[:, PACK - 1, :])
+        window = [sb([P, T], F32, "window%d" % t) for t in range(2)]
 
 
         warm = sb([P, 1], F32, "warm")
@@ -72,7 +67,7 @@ def tile_attend_gnce_pl_sgd_kernel(tc, xT, wT, y, wt, xm, offs, out_0, out_1, ou
             nc.vector.tensor_copy(picked[t // 2][:, t % 2, :], source[t][:].indirect(offsets[:]))
             if t == 0:
                 nc.scalar.activation(window[t][:], source[t][:], ACT.Copy)
-            else:
+            elif t == 1:
                 nc.vector.tensor_copy(window[t][:], source[t][:])
             if t == 1:
                 nc.scalar.copy(w_bf[:, :, 0:2], picked[0][:].rearrange("p e n -> p n e"))
@@ -116,7 +111,7 @@ def tile_attend_gnce_pl_sgd_kernel(tc, xT, wT, y, wt, xm, offs, out_0, out_1, ou
             return sig_rows[g][:, j, :]
 
         def weigh_y(on_vector, g, j):
-            rows = y_raw[g][j // 2][:, j % 2, :]
+            rows = y_raw[g][:, j, :]
             if on_vector:
                 nc.vector.tensor_scalar(rows, rows, weight[:, g, j:j + 1], None, ALU.mult)
             else:
@@ -124,7 +119,7 @@ def tile_attend_gnce_pl_sgd_kernel(tc, xT, wT, y, wt, xm, offs, out_0, out_1, ou
 
         def gradient(g, j, sig):
             nc.vector.scalar_tensor_tensor(g_rows[g][:, j, :], sig, weight[:, g, j:j + 1],
-                                           y_raw[g][j // 2][:, j % 2, :], ALU.mult, ALU.subtract)
+                                           y_raw[g][:, j, :], ALU.mult, ALU.subtract)
 
         def weave_g(engine_copy, g, lo, hi):
             engine_copy(g_bf[g][:, lo:hi, :].rearrange("p (c i) j -> p c j i", i=4),
@@ -159,11 +154,11 @@ def tile_attend_gnce_pl_sgd_kernel(tc, xT, wT, y, wt, xm, offs, out_0, out_1, ou
         def make_step(t):
             nc.scalar.activation(step[t][:], table_gradient(t)[:], ACT.Copy, scale=-LR)
 
-        deal(nc.scalar.copy, x_bf[0], x_raw[0], 0, 56)
-        deal(nc.vector.tensor_copy, x_bf[0], x_raw[0], 56, P)
+        deal(nc.scalar.copy, x_bf[0], x_raw[0], 0, 64)
+        deal(nc.vector.tensor_copy, x_bf[0], x_raw[0], 64, P)
         quantise_x(0)
-        deal(nc.scalar.copy, x_bf[1], x_raw[1], 0, 56)
-        deal(nc.vector.tensor_copy, x_bf[1], x_raw[1], 56, P)
+        deal(nc.scalar.copy, x_bf[1], x_raw[1], 0, 64)
+        deal(nc.vector.tensor_copy, x_bf[1], x_raw[1], 64, P)
         sig_rows = [sb([P, PACK, N], F32, "sig_rows0", tag="x_raw1"), sb([P, PACK, N], F32, "sig_rows1")]
         nc.scalar.activation(decayed[:, 3, :], picked[1][:, 1, :], ACT.Copy, scale=1.0 - LR * WD)
         sig0 = [score(0, j) for j in range(PACK)]
@@ -186,30 +181,32 @@ def tile_attend_gnce_pl_sgd_kernel(tc, xT, wT, y, wt, xm, offs, out_0, out_1, ou
         weigh_y(True, 1, 3)
         gradient(1, 2, sig1[2])
         gradient(1, 3, sig1[3])
-        xm_bf = [sb([P, PASSES, 2, P, PACK], BF16, "xm_bf0", tag="x_raw0")]
+        xm_bf = [sb([P, PASSES, 2, P, PACK], BF16, "xm_bf0")]
         deal_xm(nc.scalar.copy, xm_bf[0][:, 0], 0, 0)
         deal_xm(nc.scalar.copy, xm_bf[0][:, 1], 1, 0)
         deal_xm(nc.scalar.copy, xm_late[0][:], 1, 1)
         quantise_g(0)
         weave_g(nc.vector.tensor_copy, 1, 0, N)
-        nc.vector.quantize_mx(xm_codes[0][:].rearrange("p g c -> p (g c)").bitcast(E4),
-                              xm_scales[0][:].rearrange("p g c -> p (g c)"),
-                              xm_bf[0][:].rearrange("p g e m j -> p (g e m j)"))
+        quantise_xm(0, 0, xm_bf[0][:, 0])
         g_codes.append(sb([P, N], U32, "g_codes1", tag="x_raw0"))
         quantise_g(1)
-        xm_late.append(sb([P, 2, P, PACK], BF16, "xm_late1", tag="xm_raw1"))
-        deal_xm(nc.scalar.copy, xm_late[1][:], 0, 1)
+        quantise_xm(0, 1, xm_bf[0][:, 1])
+        xm_late.append(sb([P, 2, P, PACK], BF16, "xm_late1", tag="xm_bf0"))
+        deal_xm(nc.vector.tensor_copy, xm_late[1][:], 0, 1)
         xm_codes.append(sb([P, PASSES, 2 * P], U32, "xm_codes1", tag="x_raw1"))
         quantise_xm(1, 1, xm_late[0][:])
         fresh = [sb([P, N], F32, "fresh0")]
         nc.vector.scalar_tensor_tensor(fresh[0][:], table_gradient(0)[:], -LR, decayed[:, 0, :], ALU.mult, ALU.add)
         quantise_xm(1, 0, xm_late[1][:])
-        later = sb([P, PACK - 1, N], F32, "later", tag="xm_raw1")
+        later = sb([P, PACK - 1, N], F32, "later", tag="xm_bf0")
         for t in range(1, PACK):
             make_step(t)
             nc.gpsimd.tensor_tensor(later[:, t - 1, :], step[t][:], decayed[:, t, :], ALU.add)
             fresh.append(later[:, t - 1, :])
 
+        for g in range(PASSES):
+            window.append(sb([P, T], F32, "window%d" % (2 + g), tag=("y_raw1", "sig_rows1")[g]))
+            nc.sync.dma_start(window[2 + g][:], w_planes[:, 2 + g, :])
         pairs = [sb([P, 2, 2 * CHUNK, 2], BF16, "pairs%d" % h, tag="x_raw%d" % h) for h in range(2)]
         for t in range(PACK):
             nc.vector.tensor_copy(window[t][:].indirect(offsets[:]), fresh[t][:])

@@ -58,8 +58,6 @@ def tile_attend_gnce_pl_sgd_kernel(tc, xT, wT, y, wt, xm, offs, out_0, out_1, ou
         window = [sb([P, T], F32, "window%d" % t) for t in range(2)]
 
 
-        warm = sb([P, 1], F32, "warm")
-        nc.scalar.activation(warm[:], weight[:, 0, 0:1], ACT.Sigmoid)
         picked = [sb([P, 2, N], F32, "picked%d" % u) for u in range(2)]
         w_bf = sb([P, N, PACK], BF16, "w_bf")
         decayed = sb([P, PACK, N], F32, "decayed")
@@ -157,9 +155,8 @@ def tile_attend_gnce_pl_sgd_kernel(tc, xT, wT, y, wt, xm, offs, out_0, out_1, ou
         deal(nc.scalar.copy, x_bf[0], x_raw[0], 0, 64)
         deal(nc.vector.tensor_copy, x_bf[0], x_raw[0], 64, P)
         quantise_x(0)
-        deal(nc.scalar.copy, x_bf[1], x_raw[1], 0, 64)
-        deal(nc.vector.tensor_copy, x_bf[1], x_raw[1], 64, P)
-        sig_rows = [sb([P, PACK, N], F32, "sig_rows0", tag="x_raw1"), sb([P, PACK, N], F32, "sig_rows1")]
+        deal(nc.vector.tensor_copy, x_bf[1], x_raw[1], 0, P)
+        sig_rows = [sb([P, PACK, N], F32, "sig_rows0"), sb([P, PACK, N], F32, "sig_rows1")]
         nc.scalar.activation(decayed[:, 3, :], picked[1][:, 1, :], ACT.Copy, scale=1.0 - LR * WD)
         sig0 = [score(0, j) for j in range(PACK)]
         weigh_y(True, 0, 0)

@@ -35,20 +35,23 @@ def tile_attend_gnce_pl_sgd_kernel(tc, xT, wT, y, wt, xm, offs, out_0, out_1, ou
             return held.tile(shape, dtype, name=name, tag=tag or name, align_bytes=64)
 
         offsets = held.tile([P, N // 16], U16, name="offsets")
-        nc.sync.dma_start(offsets[:], offs)
 
         w_planes = wT.rearrange("(p t) c -> p t c", t=PACK)
         out_planes = out_0.rearrange("(p t) c -> p t c", t=PACK)
         source = [sb([P, T], F32, "source%d" % t) for t in range(PACK)]
         for t in range(PACK):
             nc.sync.dma_start(source[t][:], w_planes[:, t, :])
-        x_raw = [sb([P, PACK, 512], F32, "x_raw%d" % g) for g in range(PASSES)]
+            if t == 0:
+                nc.sync.dma_start(offsets[:], offs)
+        x_raw = [[sb([P, PACK, 256], F32, "x_raw%d_%d" % (g, h)) for h in range(2)] for g in range(PASSES)]
         y_raw = [sb([P, PACK, N], F32, "y_raw%d" % g) for g in range(PASSES)]
         xm_raw = [sb([P, PACK, D], F32, "xm_raw%d" % g) for g in range(PASSES)]
         weight = sb([P, PASSES, 8], F32, "weight")
         nc.scalar.dma_start(weight[:, :, 0:PACK], wt[0].rearrange("(g p j) o -> p g (j o)", g=PASSES, j=PACK))
         for g in range(PASSES):
-            nc.sync.dma_start(x_raw[g][:], xT[0, :, g * 512:(g + 1) * 512].rearrange("(p t) r -> p t r", t=PACK))
+            for h in range(2):
+                lo = g * 512 + h * 256
+                nc.sync.dma_start(x_raw[g][h][:], xT[0, :, lo:lo + 256].rearrange("(p t) r -> p t r", t=PACK))
         for g in range(PASSES):
             y_rows = y[0, g * 512:(g + 1) * 512, :].rearrange("(p j) n -> p j n", j=PACK)
             for lo, hi in ((0, 1), (1, 2), (2, 4)) if g == 0 else ((0, PACK),):
@@ -56,34 +59,37 @@ def tile_attend_gnce_pl_sgd_kernel(tc, xT, wT, y, wt, xm, offs, out_0, out_1, ou
         for g in range(PASSES):
             nc.sync.dma_start(xm_raw[g][:], xm[0, g * 512:(g + 1) * 512, :].rearrange("(p j) d -> p j d", j=PACK))
         window = [sb([P, T], F32, "window%d" % t) for t in range(2)]
+        warm = sb([P, 8], F32, "warm")
+        nc.scalar.activation(warm[:, 0:1], weight[:, 0, 0:1], ACT.Sigmoid)
 
-
-        picked = [sb([P, 2, N], F32, "picked%d" % u) for u in range(2)]
+        half = N // 2
+        picked = sb([P, 2, N], F32, "picked")
+        picked_late = [sb([P, 2, half], F32, "picked_late%d" % h) for h in range(2)]
         w_bf = sb([P, N, PACK], BF16, "w_bf")
-        decayed = sb([P, PACK, N], F32, "decayed")
-        for t in range(PACK - 1):
-            nc.vector.tensor_copy(picked[t // 2][:, t % 2, :], source[t][:].indirect(offsets[:]))
+        decayed = sb([P, PACK - 1, N], F32, "decayed")
+        for t in range(2):
+            nc.vector.tensor_copy(picked[:, t, :], source[t][:].indirect(offsets[:]))
             if t == 0:
                 nc.scalar.activation(window[t][:], source[t][:], ACT.Copy)
-            elif t == 1:
+            else:
                 nc.vector.tensor_copy(window[t][:], source[t][:])
-            if t == 1:
-                nc.scalar.copy(w_bf[:, :, 0:2], picked[0][:].rearrange("p e n -> p n e"))
-            nc.scalar.activation(decayed[:, t, :], picked[t // 2][:, t % 2, :], ACT.Copy, scale=1.0 - LR * WD)
-        half = N // 2
-        for h in range(2):
-            nc.vector.tensor_copy(picked[1][:, 1, h * half:(h + 1) * half],
-                                  source[PACK - 1][:].indirect(offsets[:, h * half // 16:(h + 1) * half // 16]))
-        nc.scalar.copy(w_bf[:, 0:half, 2:4], picked[1][:, :, 0:half].rearrange("p e n -> p n e"))
-        nc.vector.tensor_copy(w_bf[:, half:N, 2:4], picked[1][:, :, half:N].rearrange("p e n -> p n e"))
+                nc.scalar.copy(w_bf[:, :, 0:2], picked[:].rearrange("p e n -> p n e"))
+            nc.scalar.activation(decayed[:, t, :], picked[:, t, :], ACT.Copy, scale=1.0 - LR * WD)
+        for t in range(2, PACK):
+            for h in range(2):
+                nc.vector.tensor_copy(picked_late[h][:, t - 2, :],
+                                      source[t][:].indirect(offsets[:, h * half // 16:(h + 1) * half // 16]))
+                if t == 2:
+                    nc.scalar.activation(decayed[:, t, h * half:(h + 1) * half], picked_late[h][:, 0, :], ACT.Copy,
+                                         scale=1.0 - LR * WD)
+        nc.scalar.copy(w_bf[:, 0:half, 2:4], picked_late[0][:].rearrange("p e n -> p n e"))
         w_codes = sb([P, N], U32, "w_codes")
         w_scales = sb([P, N], U8, "w_scales")
-        nc.vector.quantize_mx(w_codes[:].bitcast(E4), w_scales[:], w_bf[:].rearrange("p n t -> p (n t)"))
 
-        def deal(engine_copy, dst, raw, lo, hi):
+        def deal(engine_copy, g, h, lo=0, hi=64):
             engine_copy(
-                dst[:, :, lo:hi, :].rearrange("p j s t -> p s t j"),
-                raw[:].rearrange("p t (s j) -> p s t j", j=PACK)[:, lo:hi, :, :],
+                x_bf[g][:, :, 64 * h + lo:64 * h + hi, :].rearrange("p j s t -> p s t j"),
+                x_raw[g][h][:].rearrange("p t (s j) -> p s t j", j=PACK)[:, lo:hi, :, :],
             )
 
         x_bf = [sb([P, PACK, P, PACK], BF16, "x_bf%d" % g) for g in range(PASSES)]
@@ -91,8 +97,7 @@ def tile_attend_gnce_pl_sgd_kernel(tc, xT, wT, y, wt, xm, offs, out_0, out_1, ou
         x_scales = [sb([P, 512], U8, "x_scales%d" % g) for g in range(PASSES)]
         xm_scales = [sb([P, PASSES, 2 * P], U8, "xm_scales%d" % u) for u in range(2)]
         xm_codes = [sb([P, PASSES, 2 * P], U32, "xm_codes0")]
-        xm_late = [sb([P, 2, P, PACK], BF16, "xm_late0")]
-        g_rows = [sb([P, PACK, N], BF16, "g_rows%d" % g) for g in range(PASSES)]
+        g_rows = [sb([P, PACK, N], BF16, "g_rows0")]
         g_bf = [sb([P, N, PACK], BF16, "g_bf%d" % g) for g in range(PASSES)]
         g_codes = [sb([P, N], U32, "g_codes0")]
         g_scales = [sb([P, N], U8, "g_scales%d" % g) for g in range(PASSES)]
@@ -152,17 +157,23 @@ def tile_attend_gnce_pl_sgd_kernel(tc, xT, wT, y, wt, xm, offs, out_0, out_1, ou
         def make_step(t):
             nc.scalar.activation(step[t][:], table_gradient(t)[:], ACT.Copy, scale=-LR)
 
-        deal(nc.scalar.copy, x_bf[0], x_raw[0], 0, 64)
-        deal(nc.vector.tensor_copy, x_bf[0], x_raw[0], 64, P)
-        quantise_x(0)
-        deal(nc.vector.tensor_copy, x_bf[1], x_raw[1], 0, P)
         sig_rows = [sb([P, PACK, N], F32, "sig_rows0"), sb([P, PACK, N], F32, "sig_rows1")]
-        nc.scalar.activation(decayed[:, 3, :], picked[1][:, 1, :], ACT.Copy, scale=1.0 - LR * WD)
+        deal(nc.vector.tensor_copy, 0, 0)
+        nc.vector.tensor_copy(w_bf[:, half:N, 2:4], picked_late[1][:].rearrange("p e n -> p n e"))
+        deal(nc.scalar.copy, 0, 1, 0, 32)
+        deal(nc.vector.tensor_copy, 0, 1, 32, 64)
+        nc.vector.quantize_mx(w_codes[:].bitcast(E4), w_scales[:], w_bf[:].rearrange("p n t -> p (n t)"))
+        for lo in (0, 2):
+            nc.vector.quantize_mx(x_codes[0][:, lo * P:(lo + 2) * P].bitcast(E4), x_scales[0][:, lo * P:(lo + 2) * P],
+                                  x_bf[0][:, lo:lo + 2].rearrange("p j s t -> p (j s t)"))
+        deal(nc.scalar.copy, 1, 0)
+        deal(nc.vector.tensor_copy, 1, 1)
         sig0 = [score(0, j) for j in range(PACK)]
         weigh_y(True, 0, 0)
-        weigh_y(True, 0, 1)
         quantise_x(1)
-        sig1 = [score(1, j) for j in range(PACK)]
+        for j in range(PACK):
+            score(1, j)
+        weigh_y(True, 0, 1)
         gradient(0, 0, sig0[0])
         weigh_y(True, 0, 2)
         gradient(0, 1, sig0[1])
@@ -170,41 +181,53 @@ def tile_attend_gnce_pl_sgd_kernel(tc, xT, wT, y, wt, xm, offs, out_0, out_1, ou
         gradient(0, 2, sig0[2])
         gradient(0, 3, sig0[3])
         weave_g(nc.scalar.copy, 0, 0, N)
-        weigh_y(True, 1, 0)
-        weigh_y(True, 1, 1)
-        gradient(1, 0, sig1[0])
-        weigh_y(True, 1, 2)
-        gradient(1, 1, sig1[1])
-        weigh_y(True, 1, 3)
-        gradient(1, 2, sig1[2])
-        gradient(1, 3, sig1[3])
-        xm_bf = [sb([P, PASSES, 2, P, PACK], BF16, "xm_bf0")]
-        deal_xm(nc.scalar.copy, xm_bf[0][:, 0], 0, 0)
-        deal_xm(nc.scalar.copy, xm_bf[0][:, 1], 1, 0)
+        for lanes, cols in ((slice(0, 2), slice(0, N)), (slice(2, 4), slice(0, half)), (slice(2, 4), slice(half, N))):
+            nc.vector.tensor_tensor(y_raw[1][:, lanes, cols], sig_rows[1][:, lanes, cols], y_raw[1][:, lanes, cols],
+                                    ALU.subtract)
+        share = 64
+        g_rows.append(sb([P, PACK, share], BF16, "g_rows1"))
+        for j in range(PACK):
+            nc.scalar.activation(g_rows[1][:, j, :], y_raw[1][:, j, 0:share], ACT.Copy, scale=weight[:, 1, j:j + 1])
+        nc.scalar.copy(g_bf[1][:, 0:share, :].rearrange("p (c i) j -> p c j i", i=4),
+                       g_rows[1][:].rearrange("p j (c i) -> p c j i", i=4))
+        for lo, hi in ((share, half), (half, N)):
+            nc.vector.tensor_tensor(g_bf[1][:, lo:hi, :].rearrange("p (c i) j -> p c j i", i=4),
+                                    y_raw[1][:, :, lo:hi].rearrange("p j (c i) -> p c j i", i=4),
+                                    weight[:, 1, 0:PACK].unsqueeze(1).unsqueeze(3).to_broadcast([P, (hi - lo) // 4, PACK, 4]),
+                                    ALU.mult)
+        xm_bf = sb([P, PASSES, 2, P, PACK], BF16, "xm_bf0")
+        xm_late = [sb([P, 2, P, PACK], BF16, "xm_late0")]
+        deal_xm(nc.scalar.copy, xm_bf[:, 0], 0, 0)
+        deal_xm(nc.scalar.copy, xm_bf[:, 1], 1, 0)
         deal_xm(nc.scalar.copy, xm_late[0][:], 1, 1)
+        g_codes.append(sb([P, N], U32, "g_codes1", tag="hold0"))
+        xm_codes.append(sb([P, PASSES, 2 * P], U32, "xm_codes1", tag="hold1"))
         quantise_g(0)
-        weave_g(nc.vector.tensor_copy, 1, 0, N)
-        quantise_xm(0, 0, xm_bf[0][:, 0])
-        g_codes.append(sb([P, N], U32, "g_codes1", tag="x_raw0"))
+        quantise_xm(0, 0, xm_bf[:, 0])
         quantise_g(1)
-        quantise_xm(0, 1, xm_bf[0][:, 1])
+        quantise_xm(0, 1, xm_bf[:, 1])
         xm_late.append(sb([P, 2, P, PACK], BF16, "xm_late1", tag="xm_bf0"))
         deal_xm(nc.vector.tensor_copy, xm_late[1][:], 0, 1)
-        xm_codes.append(sb([P, PASSES, 2 * P], U32, "xm_codes1", tag="x_raw1"))
         quantise_xm(1, 1, xm_late[0][:])
         fresh = [sb([P, N], F32, "fresh0")]
         nc.vector.scalar_tensor_tensor(fresh[0][:], table_gradient(0)[:], -LR, decayed[:, 0, :], ALU.mult, ALU.add)
         quantise_xm(1, 0, xm_late[1][:])
         later = sb([P, PACK - 1, N], F32, "later", tag="xm_bf0")
+        decayed_last = sb([P, N], F32, "decayed_last", tag="xm_raw1")
         for t in range(1, PACK):
             make_step(t)
-            nc.gpsimd.tensor_tensor(later[:, t - 1, :], step[t][:], decayed[:, t, :], ALU.add)
+            if t == 1:
+                for h in range(2):
+                    nc.scalar.activation(decayed_last[:, h * half:(h + 1) * half], picked_late[h][:, 1, :], ACT.Copy,
+                                         scale=1.0 - LR * WD)
+            kept = decayed[:, t, :] if t < PACK - 1 else decayed_last[:]
+            nc.gpsimd.tensor_tensor(later[:, t - 1, :], step[t][:], kept, ALU.add)
             fresh.append(later[:, t - 1, :])
 
         for g in range(PASSES):
-            window.append(sb([P, T], F32, "window%d" % (2 + g), tag=("y_raw1", "sig_rows1")[g]))
+            window.append(sb([P, T], F32, "window%d" % (2 + g), tag=("y_raw1", "xm_raw0")[g]))
             nc.sync.dma_start(window[2 + g][:], w_planes[:, 2 + g, :])
-        pairs = [sb([P, 2, 2 * CHUNK, 2], BF16, "pairs%d" % h, tag="x_raw%d" % h) for h in range(2)]
+        pairs = [sb([P, 2, 2 * CHUNK, 2], BF16, "pairs%d" % h, tag="hold%d" % h) for h in range(2)]
         for t in range(PACK):
             nc.vector.tensor_copy(window[t][:].indirect(offsets[:]), fresh[t][:])
             nc.sync.dma_start(out_planes[:, t, :], window[t][:])
@@ -225,7 +248,7 @@ def tile_attend_gnce_pl_sgd_kernel(tc, xT, wT, y, wt, xm, offs, out_0, out_1, ou
         reuse = ["x_bf0", "x_bf1", "g_rows0", "g_bf1", "g_bf0"]
         out_bf = [sb([P, hi - lo, PACK], BF16, "out_bf%d" % c, tag=reuse[c]) for c, (lo, hi) in enumerate(pieces)]
         out_codes = [sb([P, hi - lo], U32, "out_codes%d" % c) for c, (lo, hi) in enumerate(pieces)]
-        out_scales = sb([P, T], U8, "out_scales")
+        out_scales = sb([P, CHUNK], U8, "out_scales")
         words_out = out_1[0].rearrange("p c l -> p (c l)").bitcast(I32)
 
         def last_plane(engine_copy, c):
@@ -243,7 +266,9 @@ def tile_attend_gnce_pl_sgd_kernel(tc, xT, wT, y, wt, xm, offs, out_0, out_1, ou
 
         def quantise_out(c, queue):
             cols = slice(pieces[c][0], pieces[c][1])
-            nc.vector.quantize_mx(out_codes[c][:].bitcast(E4), out_scales[:, cols],
+            chunk, start = divmod(pieces[c][0], CHUNK)
+            nc.vector.quantize_mx(out_codes[c][:].bitcast(E4),
+                                  out_scales[4 * chunk:P, start:start + pieces[c][1] - pieces[c][0]],
                                   out_bf[c][:].rearrange("p n t -> p (n t)"))
             queue.dma_start(words_out[:, cols], out_codes[c][:].bitcast(I32))
 
@@ -258,4 +283,5 @@ def tile_attend_gnce_pl_sgd_kernel(tc, xT, wT, y, wt, xm, offs, out_0, out_1, ou
             quantise_out(c, nc.sync)
         scales_out = out_2[0].bitcast(I32)
         for q in range(4):
-            nc.sync.dma_start(scales_out[4 * q:4 * q + 4, :], out_scales[32 * q:32 * q + 4, :].bitcast(I32))
+            nc.sync.dma_start(scales_out[4 * q:4 * q + 4, :].rearrange("f (c x) -> c f x", c=CHUNKS),
+                              out_scales[32 * q:32 * q + 16, :].bitcast(I32))

@@ -43,24 +43,20 @@ def tile_attend_gnce_pl_sgd_kernel(tc, xT, wT, y, wt, xm, offs, out_0, out_1, ou
             nc.sync.dma_start(source[t][:], w_planes[:, t, :])
             if t == 0:
                 nc.sync.dma_start(offsets[:], offs)
-        x_raw = [[sb([P, PACK, 256], F32, "x_raw%d_%d" % (g, h)) for h in range(2)] for g in range(PASSES)]
+        x_raw = [sb([P, PACK, 512], F32, "x_raw%d" % g) for g in range(PASSES)]
         y_raw = [sb([P, PACK, N], F32, "y_raw%d" % g) for g in range(PASSES)]
         xm_raw = [sb([P, PACK, D], F32, "xm_raw%d" % g) for g in range(PASSES)]
         weight = sb([P, PASSES, 8], F32, "weight")
         nc.scalar.dma_start(weight[:, :, 0:PACK], wt[0].rearrange("(g p j) o -> p g (j o)", g=PASSES, j=PACK))
         for g in range(PASSES):
-            for h in range(2):
-                lo = g * 512 + h * 256
-                nc.sync.dma_start(x_raw[g][h][:], xT[0, :, lo:lo + 256].rearrange("(p t) r -> p t r", t=PACK))
+            nc.sync.dma_start(x_raw[g][:], xT[0, :, g * 512:(g + 1) * 512].rearrange("(p t) r -> p t r", t=PACK))
         for g in range(PASSES):
             y_rows = y[0, g * 512:(g + 1) * 512, :].rearrange("(p j) n -> p j n", j=PACK)
-            for lo, hi in ((0, 1), (1, 2), (2, 4)) if g == 0 else ((0, PACK),):
+            for lo, hi in ((0, 2), (2, 4)) if g == 0 else ((0, PACK),):
                 nc.sync.dma_start(y_raw[g][:, lo:hi, :], y_rows[:, lo:hi, :])
         for g in range(PASSES):
             nc.sync.dma_start(xm_raw[g][:], xm[0, g * 512:(g + 1) * 512, :].rearrange("(p j) d -> p j d", j=PACK))
         window = [sb([P, T], F32, "window%d" % t) for t in range(2)]
-        warm = sb([P, 8], F32, "warm")
-        nc.scalar.activation(warm[:, 0:1], weight[:, 0, 0:1], ACT.Sigmoid)
 
         half = N // 2
         picked = sb([P, 2, N], F32, "picked")
@@ -86,10 +82,10 @@ def tile_attend_gnce_pl_sgd_kernel(tc, xT, wT, y, wt, xm, offs, out_0, out_1, ou
         w_codes = sb([P, N], U32, "w_codes")
         w_scales = sb([P, N], U8, "w_scales")
 
-        def deal(engine_copy, g, h, lo=0, hi=64):
+        def deal(engine_copy, g, lo, hi):
             engine_copy(
-                x_bf[g][:, :, 64 * h + lo:64 * h + hi, :].rearrange("p j s t -> p s t j"),
-                x_raw[g][h][:].rearrange("p t (s j) -> p s t j", j=PACK)[:, lo:hi, :, :],
+                x_bf[g][:, :, lo:hi, :].rearrange("p j s t -> p s t j"),
+                x_raw[g][:].rearrange("p t (s j) -> p s t j", j=PACK)[:, lo:hi, :, :],
             )
 
         x_bf = [sb([P, PACK, P, PACK], BF16, "x_bf%d" % g) for g in range(PASSES)]
@@ -158,16 +154,14 @@ def tile_attend_gnce_pl_sgd_kernel(tc, xT, wT, y, wt, xm, offs, out_0, out_1, ou
             nc.scalar.activation(step[t][:], table_gradient(t)[:], ACT.Copy, scale=-LR)
 
         sig_rows = [sb([P, PACK, N], F32, "sig_rows0"), sb([P, PACK, N], F32, "sig_rows1")]
-        deal(nc.vector.tensor_copy, 0, 0)
         nc.vector.tensor_copy(w_bf[:, half:N, 2:4], picked_late[1][:].rearrange("p e n -> p n e"))
-        deal(nc.scalar.copy, 0, 1, 0, 32)
-        deal(nc.vector.tensor_copy, 0, 1, 32, 64)
         nc.vector.quantize_mx(w_codes[:].bitcast(E4), w_scales[:], w_bf[:].rearrange("p n t -> p (n t)"))
+        deal(nc.scalar.copy, 0, 0, 64)
+        deal(nc.vector.tensor_copy, 0, 64, P)
         for lo in (0, 2):
             nc.vector.quantize_mx(x_codes[0][:, lo * P:(lo + 2) * P].bitcast(E4), x_scales[0][:, lo * P:(lo + 2) * P],
                                   x_bf[0][:, lo:lo + 2].rearrange("p j s t -> p (j s t)"))
-        deal(nc.scalar.copy, 1, 0)
-        deal(nc.vector.tensor_copy, 1, 1)
+        deal(nc.vector.tensor_copy, 1, 0, P)
         sig0 = [score(0, j) for j in range(PACK)]
         weigh_y(True, 0, 0)
         quantise_x(1)
@@ -184,16 +178,16 @@ def tile_attend_gnce_pl_sgd_kernel(tc, xT, wT, y, wt, xm, offs, out_0, out_1, ou
         for lanes, cols in ((slice(0, 2), slice(0, N)), (slice(2, 4), slice(0, half)), (slice(2, 4), slice(half, N))):
             nc.vector.tensor_tensor(y_raw[1][:, lanes, cols], sig_rows[1][:, lanes, cols], y_raw[1][:, lanes, cols],
                                     ALU.subtract)
-        share = 64
+        share = 96
         g_rows.append(sb([P, PACK, share], BF16, "g_rows1"))
         for j in range(PACK):
             nc.scalar.activation(g_rows[1][:, j, :], y_raw[1][:, j, 0:share], ACT.Copy, scale=weight[:, 1, j:j + 1])
         nc.scalar.copy(g_bf[1][:, 0:share, :].rearrange("p (c i) j -> p c j i", i=4),
                        g_rows[1][:].rearrange("p j (c i) -> p c j i", i=4))
         for lo, hi in ((share, half), (half, N)):
-            nc.vector.tensor_tensor(g_bf[1][:, lo:hi, :].rearrange("p (c i) j -> p c j i", i=4),
-                                    y_raw[1][:, :, lo:hi].rearrange("p j (c i) -> p c j i", i=4),
-                                    weight[:, 1, 0:PACK].unsqueeze(1).unsqueeze(3).to_broadcast([P, (hi - lo) // 4, PACK, 4]),
+            nc.vector.tensor_tensor(g_bf[1][:, lo:hi, :].rearrange("p (c i) j -> p c j i", i=2),
+                                    y_raw[1][:, :, lo:hi].rearrange("p j (c i) -> p c j i", i=2),
+                                    weight[:, 1, 0:PACK].unsqueeze(1).unsqueeze(3).to_broadcast([P, (hi - lo) // 2, PACK, 2]),
                                     ALU.mult)
         xm_bf = sb([P, PASSES, 2, P, PACK], BF16, "xm_bf0")
         xm_late = [sb([P, 2, P, PACK], BF16, "xm_late0")]

@@ -1,6 +1,7 @@
 from contextlib import ExitStack
 
 import concourse.mybir as mybir
+from concourse.masks import make_identity
 
 N, T, D, R = 512, 2048, 512, 1024
 LR, WD = 0.1, 0.5
@@ -39,15 +40,23 @@ def tile_attend_gnce_pl_sgd_kernel(tc, xT, wT, y, wt, xm, offs, out_0, out_1, ou
         w_planes = wT.rearrange("(p t) c -> p t c", t=PACK)
         out_planes = out_0.rearrange("(p t) c -> p t c", t=PACK)
         source = [sb([P, T], F32, "source%d" % t) for t in range(PACK)]
+        wt_rows = sb([P, 512], F32, "wt_rows")
+        nc.gpsimd.memset(wt_rows[:], 0.0)
         for t in range(PACK):
             nc.sync.dma_start(source[t][:], w_planes[:, t, :])
             if t == 0:
                 nc.sync.dma_start(offsets[:], offs)
+                nc.sync.dma_start(wt_rows[0:PASSES, :], wt[0].rearrange("(g r) o -> g (r o)", g=PASSES))
         x_raw = [sb([P, PACK, 512], F32, "x_raw%d" % g) for g in range(PASSES)]
         y_raw = [sb([P, PACK, N], F32, "y_raw%d" % g) for g in range(PASSES)]
         xm_raw = [sb([P, PACK, D], F32, "xm_raw%d" % g) for g in range(PASSES)]
-        weight = sb([P, PASSES, 8], F32, "weight")
-        nc.scalar.dma_start(weight[:, :, 0:PACK], wt[0].rearrange("(g p j) o -> p g (j o)", g=PASSES, j=PACK))
+        identity = sb([P, P], F32, "identity")
+        make_identity(nc, identity[:])
+        turned = score_psum.tile([P, N], F32, name="bank")
+        for j in range(PACK):
+            nc.tensor.transpose(turned[:, j * P:(j + 1) * P], wt_rows[:, j:512:PACK], identity[:])
+        weight = sb([P, PASSES, PACK], F32, "weight")
+        nc.scalar.copy(weight[:], turned[:].rearrange("p (j k) -> p k j", j=PACK)[:, 0:PASSES, :])
         for g in range(PASSES):
             nc.sync.dma_start(x_raw[g][:], xT[0, :, g * 512:(g + 1) * 512].rearrange("(p t) r -> p t r", t=PACK))
         for g in range(PASSES):
@@ -178,7 +187,7 @@ def tile_attend_gnce_pl_sgd_kernel(tc, xT, wT, y, wt, xm, offs, out_0, out_1, ou
         for lanes, cols in ((slice(0, 2), slice(0, N)), (slice(2, 4), slice(0, half)), (slice(2, 4), slice(half, N))):
             nc.vector.tensor_tensor(y_raw[1][:, lanes, cols], sig_rows[1][:, lanes, cols], y_raw[1][:, lanes, cols],
                                     ALU.subtract)
-        share = 96
+        share = 64
         g_rows.append(sb([P, PACK, share], BF16, "g_rows1"))
         for j in range(PACK):
             nc.scalar.activation(g_rows[1][:, j, :], y_raw[1][:, j, 0:share], ACT.Copy, scale=weight[:, 1, j:j + 1])
@@ -242,7 +251,7 @@ def tile_attend_gnce_pl_sgd_kernel(tc, xT, wT, y, wt, xm, offs, out_0, out_1, ou
         reuse = ["x_bf0", "x_bf1", "g_rows0", "g_bf1", "g_bf0"]
         out_bf = [sb([P, hi - lo, PACK], BF16, "out_bf%d" % c, tag=reuse[c]) for c, (lo, hi) in enumerate(pieces)]
         out_codes = [sb([P, hi - lo], U32, "out_codes%d" % c) for c, (lo, hi) in enumerate(pieces)]
-        out_scales = sb([P, CHUNK], U8, "out_scales")
+        out_scales = sb([P, T], U8, "out_scales")
         words_out = out_1[0].rearrange("p c l -> p (c l)").bitcast(I32)
 
         def last_plane(engine_copy, c):
@@ -260,9 +269,7 @@ def tile_attend_gnce_pl_sgd_kernel(tc, xT, wT, y, wt, xm, offs, out_0, out_1, ou
 
         def quantise_out(c, queue):
             cols = slice(pieces[c][0], pieces[c][1])
-            chunk, start = divmod(pieces[c][0], CHUNK)
-            nc.vector.quantize_mx(out_codes[c][:].bitcast(E4),
-                                  out_scales[4 * chunk:P, start:start + pieces[c][1] - pieces[c][0]],
+            nc.vector.quantize_mx(out_codes[c][:].bitcast(E4), out_scales[:, cols],
                                   out_bf[c][:].rearrange("p n t -> p (n t)"))
             queue.dma_start(words_out[:, cols], out_codes[c][:].bitcast(I32))
 
@@ -276,6 +283,5 @@ def tile_attend_gnce_pl_sgd_kernel(tc, xT, wT, y, wt, xm, offs, out_0, out_1, ou
         for c in range(len(pieces)):
             quantise_out(c, nc.sync)
         scales_out = out_2[0].bitcast(I32)
-        for q in range(4):
-            nc.sync.dma_start(scales_out[4 * q:4 * q + 4, :].rearrange("f (c x) -> c f x", c=CHUNKS),
-                              out_scales[32 * q:32 * q + 16, :].bitcast(I32))
+        for q in (0, 2, 1, 3):
+            nc.sync.dma_start(scales_out[4 * q:4 * q + 4, :], out_scales[32 * q:32 * q + 4, :].bitcast(I32))

@@ -50,6 +50,8 @@ def tile_attend_gnce_pl_sgd_kernel(tc, xT, wT, y, wt, xm, offs, out_0, out_1, ou
         x_raw = [sb([P, PACK, 512], F32, "x_raw%d" % g) for g in range(PASSES)]
         y_raw = [sb([P, PACK, N], F32, "y_raw%d" % g) for g in range(PASSES)]
         xm_raw = [sb([P, PACK, D], F32, "xm_raw%d" % g) for g in range(PASSES)]
+        warm = sb([P, 1], F32, "warm")
+        nc.scalar.activation(warm[:], wt_rows[:, 0:1], ACT.Sigmoid)
         identity = sb([P, P], F32, "identity")
         make_identity(nc, identity[:])
         turned = score_psum.tile([P, N], F32, name="bank")
@@ -91,10 +93,10 @@ def tile_attend_gnce_pl_sgd_kernel(tc, xT, wT, y, wt, xm, offs, out_0, out_1, ou
         w_codes = sb([P, N], U32, "w_codes")
         w_scales = sb([P, N], U8, "w_scales")
 
-        def deal(engine_copy, g, lo, hi):
+        def deal(engine_copy, g, lo, hi, first=0, last=PACK):
             engine_copy(
-                x_bf[g][:, :, lo:hi, :].rearrange("p j s t -> p s t j"),
-                x_raw[g][:].rearrange("p t (s j) -> p s t j", j=PACK)[:, lo:hi, :, :],
+                x_bf[g][:, first:last, lo:hi, :].rearrange("p j s t -> p s t j"),
+                x_raw[g][:].rearrange("p t (s j) -> p s t j", j=PACK)[:, lo:hi, :, first:last],
             )
 
         x_bf = [sb([P, PACK, P, PACK], BF16, "x_bf%d" % g) for g in range(PASSES)]
@@ -163,10 +165,16 @@ def tile_attend_gnce_pl_sgd_kernel(tc, xT, wT, y, wt, xm, offs, out_0, out_1, ou
             nc.scalar.activation(step[t][:], table_gradient(t)[:], ACT.Copy, scale=-LR)
 
         sig_rows = [sb([P, PACK, N], F32, "sig_rows0"), sb([P, PACK, N], F32, "sig_rows1")]
+        def quantise_w(lo, hi):
+            nc.vector.quantize_mx(w_codes[:, lo:hi].bitcast(E4), w_scales[:, lo:hi],
+                                  w_bf[:, lo:hi, :].rearrange("p n t -> p (n t)"))
+
+        quantise_w(0, half)
         nc.vector.tensor_copy(w_bf[:, half:N, 2:4], picked_late[1][:].rearrange("p e n -> p n e"))
-        nc.vector.quantize_mx(w_codes[:].bitcast(E4), w_scales[:], w_bf[:].rearrange("p n t -> p (n t)"))
-        deal(nc.scalar.copy, 0, 0, 64)
-        deal(nc.vector.tensor_copy, 0, 64, P)
+        quantise_w(half, N)
+        for first in (0, 2):
+            deal(nc.scalar.copy, 0, 0, 64, first, first + 2)
+            deal(nc.vector.tensor_copy, 0, 64, P, first, first + 2)
         for lo in (0, 2):
             nc.vector.quantize_mx(x_codes[0][:, lo * P:(lo + 2) * P].bitcast(E4), x_scales[0][:, lo * P:(lo + 2) * P],
                                   x_bf[0][:, lo:lo + 2].rearrange("p j s t -> p (j s t)"))
@@ -174,13 +182,13 @@ def tile_attend_gnce_pl_sgd_kernel(tc, xT, wT, y, wt, xm, offs, out_0, out_1, ou
         sig0 = [score(0, j) for j in range(PACK)]
         weigh_y(True, 0, 0)
         quantise_x(1)
+        weigh_y(False, 0, 3)
         for j in range(PACK):
             score(1, j)
         weigh_y(True, 0, 1)
         gradient(0, 0, sig0[0])
         weigh_y(True, 0, 2)
         gradient(0, 1, sig0[1])
-        weigh_y(True, 0, 3)
         gradient(0, 2, sig0[2])
         gradient(0, 3, sig0[3])
         weave_g(nc.scalar.copy, 0, 0, N)
@@ -251,7 +259,7 @@ def tile_attend_gnce_pl_sgd_kernel(tc, xT, wT, y, wt, xm, offs, out_0, out_1, ou
         reuse = ["x_bf0", "x_bf1", "g_rows0", "g_bf1", "g_bf0"]
         out_bf = [sb([P, hi - lo, PACK], BF16, "out_bf%d" % c, tag=reuse[c]) for c, (lo, hi) in enumerate(pieces)]
         out_codes = [sb([P, hi - lo], U32, "out_codes%d" % c) for c, (lo, hi) in enumerate(pieces)]
-        out_scales = sb([P, T], U8, "out_scales")
+        out_scales = sb([P, CHUNK], U8, "out_scales")
         words_out = out_1[0].rearrange("p c l -> p (c l)").bitcast(I32)
 
         def last_plane(engine_copy, c):
@@ -268,10 +276,13 @@ def tile_attend_gnce_pl_sgd_kernel(tc, xT, wT, y, wt, xm, offs, out_0, out_1, ou
             engine_copy(dst[:, lo - pieces[c][0]:hi - pieces[c][0], :], src.rearrange("p u n -> p n u"))
 
         def quantise_out(c, queue):
-            cols = slice(pieces[c][0], pieces[c][1])
-            nc.vector.quantize_mx(out_codes[c][:].bitcast(E4), out_scales[:, cols],
-                                  out_bf[c][:].rearrange("p n t -> p (n t)"))
-            queue.dma_start(words_out[:, cols], out_codes[c][:].bitcast(I32))
+            lo, hi = pieces[c]
+            row = 4 * (lo // CHUNK)
+            for a in range(lo, hi, half):
+                nc.vector.quantize_mx(out_codes[c][:, a - lo:a - lo + half].bitcast(E4),
+                                      out_scales[row:P, a % CHUNK:a % CHUNK + half],
+                                      out_bf[c][:, a - lo:a - lo + half, :].rearrange("p n t -> p (n t)"))
+            queue.dma_start(words_out[:, lo:hi], out_codes[c][:].bitcast(I32))
 
         for c in (0, 1):
             last_plane(nc.vector.tensor_copy, c)
@@ -283,5 +294,6 @@ def tile_attend_gnce_pl_sgd_kernel(tc, xT, wT, y, wt, xm, offs, out_0, out_1, ou
         for c in range(len(pieces)):
             quantise_out(c, nc.sync)
         scales_out = out_2[0].bitcast(I32)
-        for q in (0, 2, 1, 3):
-            nc.sync.dma_start(scales_out[4 * q:4 * q + 4, :], out_scales[32 * q:32 * q + 4, :].bitcast(I32))
+        for q in range(4):
+            nc.sync.dma_start(scales_out[4 * q:4 * q + 4, :].rearrange("i (c x) -> c i x", c=CHUNKS),
+                              out_scales[32 * q:32 * q + 16, :].bitcast(I32))

@@ -141,7 +141,7 @@ def tile_attend_gnce_pl_sgd_kernel(tc, xT, wT, y, wt, xm, offs, out_0, out_1, ou
         def deal_xm(engine_copy, dst, g, u):
             engine_copy(
                 dst.rearrange("p e m j -> p m j e"),
-                xm_raw[g][:].rearrange("p j (m t) -> p m j t", t=PACK)[:, :, :, 2 * u:2 * u + 2],
+                xm_raw[g][:].rearrange("p j (m t) -> p m j t", t=PACK)[:, :, :, u:PACK:2],
             )
 
         def quantise_xm(u, g, src):
@@ -149,20 +149,15 @@ def tile_attend_gnce_pl_sgd_kernel(tc, xT, wT, y, wt, xm, offs, out_0, out_1, ou
                                   src.rearrange("p e m j -> p (e m j)"))
 
         def table_gradient(t):
-            cols = slice((t % 2) * P, (t % 2 + 1) * P)
+            cols = slice((t // 2) * P, (t // 2 + 1) * P)
             acc = grad_psum.tile([P, N], F32, name="grad%d" % t)
-            order = range(PASSES - 1, -1, -1) if t == 1 else range(PASSES)
+            order = range(PASSES - 1, -1, -1) if t == 2 else range(PASSES)
             for g in order:
-                nc.tensor.matmul_mx(acc[:], lhsT=xm_codes[t // 2][:, g, cols].bitcast(E4),
-                                    lhsT_scale=xm_scales[t // 2][:, g, cols],
+                nc.tensor.matmul_mx(acc[:], lhsT=xm_codes[t % 2][:, g, cols].bitcast(E4),
+                                    lhsT_scale=xm_scales[t % 2][:, g, cols],
                                     rhs=g_codes[g][:].bitcast(E5), rhs_scale=g_scales[g][:],
                                     start=(g == order[0]), stop=(g == order[-1]))
             return acc
-
-        step = [None] + [sb([P, N], F32, "step%d" % t) for t in range(1, PACK)]
-
-        def make_step(t):
-            nc.scalar.activation(step[t][:], table_gradient(t)[:], ACT.Copy, scale=-LR)
 
         sig_rows = [sb([P, PACK, N], F32, "sig_rows0"), sb([P, PACK, N], F32, "sig_rows1")]
         def quantise_w(lo, hi):
@@ -211,8 +206,8 @@ def tile_attend_gnce_pl_sgd_kernel(tc, xT, wT, y, wt, xm, offs, out_0, out_1, ou
         deal_xm(nc.scalar.copy, xm_bf[:, 0], 0, 0)
         deal_xm(nc.scalar.copy, xm_bf[:, 1], 1, 0)
         deal_xm(nc.scalar.copy, xm_late[0][:], 1, 1)
-        g_codes.append(sb([P, N], U32, "g_codes1", tag="hold0"))
-        xm_codes.append(sb([P, PASSES, 2 * P], U32, "xm_codes1", tag="hold1"))
+        g_codes.append(sb([P, N], U32, "g_codes1"))
+        xm_codes.append(sb([P, PASSES, 2 * P], U32, "xm_codes1"))
         quantise_g(0)
         quantise_xm(0, 0, xm_bf[:, 0])
         quantise_g(1)
@@ -220,40 +215,44 @@ def tile_attend_gnce_pl_sgd_kernel(tc, xT, wT, y, wt, xm, offs, out_0, out_1, ou
         xm_late.append(sb([P, 2, P, PACK], BF16, "xm_late1", tag="xm_bf0"))
         deal_xm(nc.vector.tensor_copy, xm_late[1][:], 0, 1)
         quantise_xm(1, 1, xm_late[0][:])
-        fresh = [sb([P, N], F32, "fresh0")]
-        nc.vector.scalar_tensor_tensor(fresh[0][:], table_gradient(0)[:], -LR, decayed[:, 0, :], ALU.mult, ALU.add)
-        quantise_xm(1, 0, xm_late[1][:])
-        later = sb([P, PACK - 1, N], F32, "later", tag="xm_bf0")
-        decayed_last = sb([P, N], F32, "decayed_last", tag="xm_raw1")
-        for t in range(1, PACK):
-            make_step(t)
-            if t == 1:
-                for h in range(2):
-                    nc.scalar.activation(decayed_last[:, h * half:(h + 1) * half], picked_late[h][:, 1, :], ACT.Copy,
-                                         scale=1.0 - LR * WD)
-            kept = decayed[:, t, :] if t < PACK - 1 else decayed_last[:]
-            nc.gpsimd.tensor_tensor(later[:, t - 1, :], step[t][:], kept, ALU.add)
-            fresh.append(later[:, t - 1, :])
+        fresh = [sb([P, N], F32, "fresh%d" % t) for t in range(PACK)]
 
+        def update(t, kept):
+            nc.vector.scalar_tensor_tensor(fresh[t][:], table_gradient(t)[:], -LR, kept, ALU.mult, ALU.add)
+
+        update(0, decayed[:, 0, :])
+        quantise_xm(1, 0, xm_late[1][:])
+        decayed_last = sb([P, N], F32, "decayed_last", tag="xm_bf0")
+        for h in range(2):
+            nc.gpsimd.tensor_scalar(decayed_last[:, h * half:(h + 1) * half], picked_late[h][:, 1, :], 1.0 - LR * WD, 0.0,
+                                    ALU.mult, ALU.add)
+        update(2, decayed[:, 2, :])
+        update(1, decayed[:, 1, :])
         for g in range(PASSES):
             window.append(sb([P, T], F32, "window%d" % (2 + g), tag=("y_raw1", "xm_raw0")[g]))
             nc.sync.dma_start(window[2 + g][:], w_planes[:, 2 + g, :])
-        pairs = [sb([P, 2, 2 * CHUNK, 2], BF16, "pairs%d" % h, tag="hold%d" % h) for h in range(2)]
-        for t in range(PACK):
+
+        def scatter_on_scalar(t):
+            for h in range(2):
+                nc.scalar.activation(window[t][:].indirect(offsets[:, h * half // 16:(h + 1) * half // 16]),
+                                     fresh[t][:, h * half:(h + 1) * half], ACT.Copy)
+            nc.sync.dma_start(out_planes[:, t, :], window[t][:])
+
+        def scatter_on_vector(t):
             nc.vector.tensor_copy(window[t][:].indirect(offsets[:]), fresh[t][:])
             nc.sync.dma_start(out_planes[:, t, :], window[t][:])
-            if t < PACK - 1:
-                nc.scalar.copy(pairs[0][:, t // 2, :, t % 2], window[t][:, 0:2 * CHUNK])
-                if t == 2:
-                    seam = slice(CHUNK - 8, CHUNK + 8)
-                    nc.scalar.copy(pairs[0][:, 1, seam, :], window[t][:, seam].unsqueeze(2).to_broadcast([P, 16, 2]))
-                nc.scalar.copy(pairs[1][:, t // 2, 0:CHUNK, t % 2], window[t][:, 2 * CHUNK:3 * CHUNK])
-                far = window[t][:, 3 * CHUNK:T]
-                if t < 2:
-                    nc.gpsimd.tensor_scalar(pairs[1][:, 0, CHUNK:2 * CHUNK, t], far, 1.0, -0.0, ALU.mult, ALU.add)
-                else:
-                    nc.gpsimd.tensor_scalar(pairs[1][:, 1, CHUNK:2 * CHUNK, :], far.unsqueeze(2).to_broadcast([P, CHUNK, 2]),
-                                            1.0, -0.0, ALU.mult, ALU.add)
+
+        near = CHUNK
+        pairs_far = sb([P, 2, T - near, 2], BF16, "pairs_far")
+        scatter_on_scalar(0)
+        scatter_on_vector(1)
+        for t in range(2):
+            nc.gpsimd.tensor_scalar(pairs_far[:, 0, :, t], window[t][:, near:T], 1.0, -0.0, ALU.mult, ALU.add)
+        scatter_on_scalar(2)
+        update(3, decayed_last[:])
+        scatter_on_vector(3)
+        nc.scalar.copy(pairs_far[:, 1, :, 0], window[2][:, near:T])
+        pairs_near = sb([P, 2, near, 2], BF16, "pairs_near", tag="fresh3")
 
         pieces = [(0, 512), (512, 1024), (1024, 1536), (1536, 1792), (1792, 2048)]
         reuse = ["x_bf0", "x_bf1", "g_rows0", "g_bf1", "g_bf0"]
@@ -262,37 +261,33 @@ def tile_attend_gnce_pl_sgd_kernel(tc, xT, wT, y, wt, xm, offs, out_0, out_1, ou
         out_scales = sb([P, CHUNK], U8, "out_scales")
         words_out = out_1[0].rearrange("p c l -> p (c l)").bitcast(I32)
 
-        def last_plane(engine_copy, c):
+        def join(engine_copy, word, c):
             lo, hi = pieces[c]
-            h = lo // (2 * CHUNK)
-            base = h * 2 * CHUNK
-            engine_copy(pairs[h][:, 1, lo - base:hi - base, 1], window[PACK - 1][:, lo:hi])
-
-        def weave_out(engine_copy, word, c, lo, hi):
-            h = lo // (2 * CHUNK)
-            base = h * 2 * CHUNK
-            src = pairs[h][:].rearrange("p u n e -> p u (n e)").bitcast(word)[:, :, lo - base:hi - base]
+            pairs, base = (pairs_near, 0) if lo < near else (pairs_far, near)
+            src = pairs[:].rearrange("p u n e -> p u (n e)").bitcast(word)[:, :, lo - base:hi - base]
             dst = out_bf[c][:].rearrange("p n t -> p (n t)").bitcast(word).rearrange("p (n u) -> p n u", u=2)
-            engine_copy(dst[:, lo - pieces[c][0]:hi - pieces[c][0], :], src.rearrange("p u n -> p n u"))
+            engine_copy(dst, src.rearrange("p u n -> p n u"))
 
-        def quantise_out(c, queue):
+        def quantise_out(c):
             lo, hi = pieces[c]
             row = 4 * (lo // CHUNK)
             for a in range(lo, hi, half):
                 nc.vector.quantize_mx(out_codes[c][:, a - lo:a - lo + half].bitcast(E4),
                                       out_scales[row:P, a % CHUNK:a % CHUNK + half],
                                       out_bf[c][:, a - lo:a - lo + half, :].rearrange("p n t -> p (n t)"))
-            queue.dma_start(words_out[:, lo:hi], out_codes[c][:].bitcast(I32))
+            nc.sync.dma_start(words_out[:, lo:hi], out_codes[c][:].bitcast(I32))
 
+        for t in range(PACK):
+            nc.vector.tensor_copy(pairs_near[:, t // 2, :, t % 2], window[t][:, 0:near])
+        for c in range(1, len(pieces)):
+            lo, hi = pieces[c]
+            nc.scalar.copy(pairs_far[:, 1, lo - near:hi - near, 1], window[PACK - 1][:, lo:hi])
+            if c > 1:
+                join(nc.scalar.copy, U32, c)
         for c in (0, 1):
-            last_plane(nc.vector.tensor_copy, c)
-        for c in (2, 3, 4):
-            last_plane(nc.scalar.copy, c)
-            weave_out(nc.scalar.copy, U32, c, pieces[c][0], pieces[c][1])
-        for c in (0, 1):
-            weave_out(nc.vector.tensor_copy, I32, c, pieces[c][0], pieces[c][1])
+            join(nc.vector.tensor_copy, I32, c)
         for c in range(len(pieces)):
-            quantise_out(c, nc.sync)
+            quantise_out(c)
         scales_out = out_2[0].bitcast(I32)
         for q in range(4):
             nc.sync.dma_start(scales_out[4 * q:4 * q + 4, :].rearrange("i (c x) -> c i x", c=CHUNKS),

@@ -148,16 +148,14 @@ def tile_attend_gnce_pl_sgd_kernel(tc, xT, wT, y, wt, xm, offs, out_0, out_1, ou
             nc.vector.quantize_mx(xm_codes[u][:, g, :].bitcast(E4), xm_scales[u][:, g, :],
                                   src.rearrange("p e m j -> p (e m j)"))
 
-        def table_gradient(t):
+        def table_gradient(acc, t, slots):
             cols = slice((t // 2) * P, (t // 2 + 1) * P)
-            acc = grad_psum.tile([P, N], F32, name="grad%d" % t)
-            order = range(PASSES - 1, -1, -1) if t == 2 else range(PASSES)
+            order = range(PASSES - 1, -1, -1) if t > 0 else range(PASSES)
             for g in order:
-                nc.tensor.matmul_mx(acc[:], lhsT=xm_codes[t % 2][:, g, cols].bitcast(E4),
+                nc.tensor.matmul_mx(acc, lhsT=xm_codes[t % 2][:, g, cols].bitcast(E4),
                                     lhsT_scale=xm_scales[t % 2][:, g, cols],
-                                    rhs=g_codes[g][:].bitcast(E5), rhs_scale=g_scales[g][:],
+                                    rhs=g_codes[g][:, slots].bitcast(E5), rhs_scale=g_scales[g][:, slots],
                                     start=(g == order[0]), stop=(g == order[-1]))
-            return acc
 
         sig_rows = [sb([P, PACK, N], F32, "sig_rows0"), sb([P, PACK, N], F32, "sig_rows1")]
         def quantise_w(lo, hi):
@@ -218,9 +216,15 @@ def tile_attend_gnce_pl_sgd_kernel(tc, xT, wT, y, wt, xm, offs, out_0, out_1, ou
         fresh = [sb([P, N], F32, "fresh%d" % t) for t in range(PACK)]
 
         def update(t, kept):
-            nc.vector.scalar_tensor_tensor(fresh[t][:], table_gradient(t)[:], -LR, kept, ALU.mult, ALU.add)
+            acc = grad_psum.tile([P, N], F32, name="grad%d" % t)
+            table_gradient(acc[:], t, slice(0, N))
+            nc.vector.scalar_tensor_tensor(fresh[t][:], acc[:], -LR, kept, ALU.mult, ALU.add)
 
-        update(0, decayed[:, 0, :])
+        for h in range(2):
+            slots = slice(h * half, (h + 1) * half)
+            acc = score_psum.tile([P, half], F32, name="bank")
+            table_gradient(acc[:], 0, slots)
+            nc.vector.scalar_tensor_tensor(fresh[0][:, slots], acc[:], -LR, decayed[:, 0, slots], ALU.mult, ALU.add)
         quantise_xm(1, 0, xm_late[1][:])
         decayed_last = sb([P, N], F32, "decayed_last", tag="xm_bf0")
         for h in range(2):
@@ -270,8 +274,8 @@ def tile_attend_gnce_pl_sgd_kernel(tc, xT, wT, y, wt, xm, offs, out_0, out_1, ou
 
         def quantise_out(c):
             lo, hi = pieces[c]
-            row = 4 * (lo // CHUNK)
             for a in range(lo, hi, half):
+                row = 4 * (a // CHUNK)
                 nc.vector.quantize_mx(out_codes[c][:, a - lo:a - lo + half].bitcast(E4),
                                       out_scales[row:P, a % CHUNK:a % CHUNK + half],
                                       out_bf[c][:, a - lo:a - lo + half, :].rearrange("p n t -> p (n t)"))
@@ -284,9 +288,10 @@ def tile_attend_gnce_pl_sgd_kernel(tc, xT, wT, y, wt, xm, offs, out_0, out_1, ou
             nc.scalar.copy(pairs_far[:, 1, lo - near:hi - near, 1], window[PACK - 1][:, lo:hi])
             if c > 1:
                 join(nc.scalar.copy, U32, c)
-        for c in (0, 1):
-            join(nc.vector.tensor_copy, I32, c)
+        join(nc.vector.tensor_copy, I32, 0)
         for c in range(len(pieces)):
+            if c < 1:
+                join(nc.vector.tensor_copy, I32, c + 1)
             quantise_out(c)
         scales_out = out_2[0].bitcast(I32)
         for q in range(4):

@@ -29,11 +29,15 @@ def tile_attend_gnce_pl_sgd_kernel(tc, xT, wT, y, wt, xm, offs, out_0, out_1, ou
     nc = tc.nc
     with ExitStack() as ctx:
         held = ctx.enter_context(tc.tile_pool(name="held", bufs=1))
+        placed = ctx.enter_context(tc.tile_pool(name="placed", bufs=1))
         score_psum = ctx.enter_context(tc.psum_pool(name="score_psum", bufs=4))
         grad_psum = ctx.enter_context(tc.psum_pool(name="grad_psum", bufs=1))
 
         def sb(shape, dtype, name, tag=""):
             return held.tile(shape, dtype, name=name, tag=tag or name, align_bytes=64)
+
+        def at(offset, shape, dtype, name):
+            return placed.tile(shape, dtype, name=name, tag=name, align_bytes=64, offset=offset)
 
         offsets = held.tile([P, N // 16], U16, name="offsets")
 
@@ -73,7 +77,8 @@ def tile_attend_gnce_pl_sgd_kernel(tc, xT, wT, y, wt, xm, offs, out_0, out_1, ou
         picked = sb([P, 2, N], F32, "picked")
         picked_late = [sb([P, 2, half], F32, "picked_late%d" % h) for h in range(2)]
         w_bf = sb([P, N, PACK], BF16, "w_bf")
-        decayed = sb([P, PACK - 1, N], F32, "decayed")
+        decayed_first = [at(0, [P, half], F32, "decayed_first0"), sb([P, half], F32, "decayed_first1")]
+        decayed = [None, sb([P, N], F32, "decayed1"), sb([P, N], F32, "decayed2")]
         for t in range(2):
             nc.vector.tensor_copy(picked[:, t, :], source[t][:].indirect(offsets[:]))
             if t == 0:
@@ -81,13 +86,18 @@ def tile_attend_gnce_pl_sgd_kernel(tc, xT, wT, y, wt, xm, offs, out_0, out_1, ou
             else:
                 nc.vector.tensor_copy(window[t][:], source[t][:])
                 nc.scalar.copy(w_bf[:, :, 0:2], picked[:].rearrange("p e n -> p n e"))
-            nc.scalar.activation(decayed[:, t, :], picked[:, t, :], ACT.Copy, scale=1.0 - LR * WD)
+            if t == 0:
+                for h in range(2):
+                    nc.scalar.activation(decayed_first[h][:], picked[:, 0, h * half:(h + 1) * half], ACT.Copy,
+                                         scale=1.0 - LR * WD)
+            else:
+                nc.scalar.activation(decayed[t][:], picked[:, t, :], ACT.Copy, scale=1.0 - LR * WD)
         for t in range(2, PACK):
             for h in range(2):
                 nc.vector.tensor_copy(picked_late[h][:, t - 2, :],
                                       source[t][:].indirect(offsets[:, h * half // 16:(h + 1) * half // 16]))
                 if t == 2:
-                    nc.scalar.activation(decayed[:, t, h * half:(h + 1) * half], picked_late[h][:, 0, :], ACT.Copy,
+                    nc.scalar.activation(decayed[t][:, h * half:(h + 1) * half], picked_late[h][:, 0, :], ACT.Copy,
                                          scale=1.0 - LR * WD)
         nc.scalar.copy(w_bf[:, 0:half, 2:4], picked_late[0][:].rearrange("p e n -> p n e"))
         w_codes = sb([P, N], U32, "w_codes")
@@ -135,13 +145,14 @@ def tile_attend_gnce_pl_sgd_kernel(tc, xT, wT, y, wt, xm, offs, out_0, out_1, ou
             engine_copy(g_bf[g][:, lo:hi, :].rearrange("p (c i) j -> p c j i", i=4),
                         g_rows[g][:, :, lo:hi].rearrange("p j (c i) -> p c j i", i=4))
 
-        def quantise_g(g):
-            nc.vector.quantize_mx(g_codes[g][:].bitcast(E5), g_scales[g][:], g_bf[g][:].rearrange("p n j -> p (n j)"))
+        def quantise_g(g, lo=0, hi=N):
+            nc.vector.quantize_mx(g_codes[g][:, lo:hi].bitcast(E5), g_scales[g][:, lo:hi],
+                                  g_bf[g][:, lo:hi, :].rearrange("p n j -> p (n j)"))
 
-        def deal_xm(engine_copy, dst, g, u):
+        def deal_xm(engine_copy, dst, g, u, lo=0, hi=P):
             engine_copy(
-                dst.rearrange("p e m j -> p m j e"),
-                xm_raw[g][:].rearrange("p j (m t) -> p m j t", t=PACK)[:, :, :, u:PACK:2],
+                dst.rearrange("p e m j -> p m j e")[:, lo:hi],
+                xm_raw[g][:].rearrange("p j (m t) -> p m j t", t=PACK)[:, lo:hi, :, u:PACK:2],
             )
 
         def quantise_xm(u, g, src):
@@ -150,7 +161,7 @@ def tile_attend_gnce_pl_sgd_kernel(tc, xT, wT, y, wt, xm, offs, out_0, out_1, ou
 
         def table_gradient(acc, t, slots):
             cols = slice((t // 2) * P, (t // 2 + 1) * P)
-            order = range(PASSES - 1, -1, -1) if t > 0 else range(PASSES)
+            order = range(PASSES - 1, -1, -1) if t == 2 else range(PASSES)
             for g in order:
                 nc.tensor.matmul_mx(acc, lhsT=xm_codes[t % 2][:, g, cols].bitcast(E4),
                                     lhsT_scale=xm_scales[t % 2][:, g, cols],
@@ -202,17 +213,17 @@ def tile_attend_gnce_pl_sgd_kernel(tc, xT, wT, y, wt, xm, offs, out_0, out_1, ou
         xm_bf = sb([P, PASSES, 2, P, PACK], BF16, "xm_bf0")
         xm_late = [sb([P, 2, P, PACK], BF16, "xm_late0")]
         deal_xm(nc.scalar.copy, xm_bf[:, 0], 0, 0)
-        deal_xm(nc.scalar.copy, xm_bf[:, 1], 1, 0)
+        deal_xm(nc.scalar.copy, xm_bf[:, 1], 1, 0, 0, 56)
         deal_xm(nc.scalar.copy, xm_late[0][:], 1, 1)
         g_codes.append(sb([P, N], U32, "g_codes1"))
-        xm_codes.append(sb([P, PASSES, 2 * P], U32, "xm_codes1"))
         quantise_g(0)
         quantise_xm(0, 0, xm_bf[:, 0])
-        quantise_g(1)
+        quantise_g(1, 0, half)
+        deal_xm(nc.vector.tensor_copy, xm_bf[:, 1], 1, 0, 56, P)
+        quantise_g(1, half, N)
         quantise_xm(0, 1, xm_bf[:, 1])
         xm_late.append(sb([P, 2, P, PACK], BF16, "xm_late1", tag="xm_bf0"))
         deal_xm(nc.vector.tensor_copy, xm_late[1][:], 0, 1)
-        quantise_xm(1, 1, xm_late[0][:])
         fresh = [sb([P, N], F32, "fresh%d" % t) for t in range(PACK)]
 
         def update(t, kept):
@@ -224,14 +235,17 @@ def tile_attend_gnce_pl_sgd_kernel(tc, xT, wT, y, wt, xm, offs, out_0, out_1, ou
             slots = slice(h * half, (h + 1) * half)
             acc = score_psum.tile([P, half], F32, name="bank")
             table_gradient(acc[:], 0, slots)
-            nc.vector.scalar_tensor_tensor(fresh[0][:, slots], acc[:], -LR, decayed[:, 0, slots], ALU.mult, ALU.add)
-        quantise_xm(1, 0, xm_late[1][:])
+            nc.vector.scalar_tensor_tensor(fresh[0][:, slots], acc[:], -LR, decayed_first[h][:], ALU.mult, ALU.add)
+            if h == 0:
+                xm_codes.append(at(0, [P, PASSES, 2 * P], U32, "xm_codes1"))
+                quantise_xm(1, 0, xm_late[1][:])
+                quantise_xm(1, 1, xm_late[0][:])
         decayed_last = sb([P, N], F32, "decayed_last", tag="xm_bf0")
         for h in range(2):
             nc.gpsimd.tensor_scalar(decayed_last[:, h * half:(h + 1) * half], picked_late[h][:, 1, :], 1.0 - LR * WD, 0.0,
                                     ALU.mult, ALU.add)
-        update(2, decayed[:, 2, :])
-        update(1, decayed[:, 1, :])
+        update(2, decayed[2][:])
+        update(1, decayed[1][:])
         for g in range(PASSES):
             window.append(sb([P, T], F32, "window%d" % (2 + g), tag=("y_raw1", "xm_raw0")[g]))
             nc.sync.dma_start(window[2 + g][:], w_planes[:, 2 + g, :])

@@ -34,7 +34,7 @@ def tile_attend_gnce_pl_sgd_kernel(tc, xT, wT, y, wt, xm, offs, out_0, out_1, ou
         grad_psum = ctx.enter_context(tc.psum_pool(name="grad_psum", bufs=1))
 
         def sb(shape, dtype, name, tag=""):
-            return held.tile(shape, dtype, name=name, tag=tag or name, align_bytes=64)
+            return held.tile(shape, dtype, name=name, tag=tag or name, align_bytes=256)
 
         def at(offset, shape, dtype, name):
             return placed.tile(shape, dtype, name=name, tag=name, align_bytes=64, offset=offset)
@@ -71,7 +71,7 @@ def tile_attend_gnce_pl_sgd_kernel(tc, xT, wT, y, wt, xm, offs, out_0, out_1, ou
                 nc.sync.dma_start(y_raw[g][:, lo:hi, :], y_rows[:, lo:hi, :])
         for g in range(PASSES):
             nc.sync.dma_start(xm_raw[g][:], xm[0, g * 512:(g + 1) * 512, :].rearrange("(p j) d -> p j d", j=PACK))
-        window = [sb([P, T], F32, "window%d" % t) for t in range(2)]
+        window = [sb([P, T], F32, "window%d" % t) for t in range(PACK - 1)]
 
         half = N // 2
         picked = sb([P, 2, N], F32, "picked")
@@ -99,6 +99,9 @@ def tile_attend_gnce_pl_sgd_kernel(tc, xT, wT, y, wt, xm, offs, out_0, out_1, ou
                 if t == 2:
                     nc.scalar.activation(decayed[t][:, h * half:(h + 1) * half], picked_late[h][:, 0, :], ACT.Copy,
                                          scale=1.0 - LR * WD)
+            if t == 2:
+                nc.vector.tensor_copy(window[t][:, 0:3 * CHUNK], source[t][:, 0:3 * CHUNK])
+                nc.scalar.activation(window[t][:, 3 * CHUNK:T], source[t][:, 3 * CHUNK:T], ACT.Copy)
         nc.scalar.copy(w_bf[:, 0:half, 2:4], picked_late[0][:].rearrange("p e n -> p n e"))
         w_codes = sb([P, N], U32, "w_codes")
         w_scales = sb([P, N], U8, "w_scales")
@@ -115,7 +118,7 @@ def tile_attend_gnce_pl_sgd_kernel(tc, xT, wT, y, wt, xm, offs, out_0, out_1, ou
         xm_scales = [sb([P, PASSES, 2 * P], U8, "xm_scales%d" % u) for u in range(2)]
         xm_codes = [sb([P, PASSES, 2 * P], U32, "xm_codes0")]
         g_rows = [sb([P, PACK, N], BF16, "g_rows0")]
-        g_bf = [sb([P, N, PACK], BF16, "g_bf%d" % g) for g in range(PASSES)]
+        g_bf = [sb([P, N, PACK], BF16, "g_bf0"), sb([P, N, PACK], BF16, "g_bf1")]
         g_codes = [sb([P, N], U32, "g_codes0")]
         g_scales = [sb([P, N], U8, "g_scales%d" % g) for g in range(PASSES)]
 
@@ -161,7 +164,7 @@ def tile_attend_gnce_pl_sgd_kernel(tc, xT, wT, y, wt, xm, offs, out_0, out_1, ou
 
         def table_gradient(acc, t, slots):
             cols = slice((t // 2) * P, (t // 2 + 1) * P)
-            order = range(PASSES - 1, -1, -1) if t == 2 else range(PASSES)
+            order = range(PASSES - 1, -1, -1) if t == 3 else range(PASSES)
             for g in order:
                 nc.tensor.matmul_mx(acc, lhsT=xm_codes[t % 2][:, g, cols].bitcast(E4),
                                     lhsT_scale=xm_scales[t % 2][:, g, cols],
@@ -213,13 +216,13 @@ def tile_attend_gnce_pl_sgd_kernel(tc, xT, wT, y, wt, xm, offs, out_0, out_1, ou
         xm_bf = sb([P, PASSES, 2, P, PACK], BF16, "xm_bf0")
         xm_late = [sb([P, 2, P, PACK], BF16, "xm_late0")]
         deal_xm(nc.scalar.copy, xm_bf[:, 0], 0, 0)
-        deal_xm(nc.scalar.copy, xm_bf[:, 1], 1, 0, 0, 56)
+        deal_xm(nc.scalar.copy, xm_bf[:, 1], 1, 0, 0, 48)
         deal_xm(nc.scalar.copy, xm_late[0][:], 1, 1)
         g_codes.append(sb([P, N], U32, "g_codes1"))
         quantise_g(0)
         quantise_xm(0, 0, xm_bf[:, 0])
         quantise_g(1, 0, half)
-        deal_xm(nc.vector.tensor_copy, xm_bf[:, 1], 1, 0, 56, P)
+        deal_xm(nc.vector.tensor_copy, xm_bf[:, 1], 1, 0, 48, P)
         quantise_g(1, half, N)
         quantise_xm(0, 1, xm_bf[:, 1])
         xm_late.append(sb([P, 2, P, PACK], BF16, "xm_late1", tag="xm_bf0"))
@@ -240,15 +243,14 @@ def tile_attend_gnce_pl_sgd_kernel(tc, xT, wT, y, wt, xm, offs, out_0, out_1, ou
                 xm_codes.append(at(0, [P, PASSES, 2 * P], U32, "xm_codes1"))
                 quantise_xm(1, 0, xm_late[1][:])
                 quantise_xm(1, 1, xm_late[0][:])
-        decayed_last = sb([P, N], F32, "decayed_last", tag="xm_bf0")
+        decayed_last = sb([P, N], F32, "decayed_last", tag="xm_late0")
         for h in range(2):
             nc.gpsimd.tensor_scalar(decayed_last[:, h * half:(h + 1) * half], picked_late[h][:, 1, :], 1.0 - LR * WD, 0.0,
                                     ALU.mult, ALU.add)
         update(2, decayed[2][:])
         update(1, decayed[1][:])
-        for g in range(PASSES):
-            window.append(sb([P, T], F32, "window%d" % (2 + g), tag=("y_raw1", "xm_raw0")[g]))
-            nc.sync.dma_start(window[2 + g][:], w_planes[:, 2 + g, :])
+        window.append(sb([P, T], F32, "window3", tag="xm_raw0"))
+        nc.sync.dma_start(window[3][:], w_planes[:, 3, :])
 
         def scatter_on_scalar(t):
             for h in range(2):
@@ -273,7 +275,7 @@ def tile_attend_gnce_pl_sgd_kernel(tc, xT, wT, y, wt, xm, offs, out_0, out_1, ou
         pairs_near = sb([P, 2, near, 2], BF16, "pairs_near", tag="fresh3")
 
         pieces = [(0, 512), (512, 1024), (1024, 1536), (1536, 1792), (1792, 2048)]
-        reuse = ["x_bf0", "x_bf1", "g_rows0", "g_bf1", "g_bf0"]
+        reuse = ["x_bf0", "x_bf1", "g_rows0", "y_raw1", "g_bf0"]
         out_bf = [sb([P, hi - lo, PACK], BF16, "out_bf%d" % c, tag=reuse[c]) for c, (lo, hi) in enumerate(pieces)]
         out_codes = [sb([P, hi - lo], U32, "out_codes%d" % c) for c, (lo, hi) in enumerate(pieces)]
         out_scales = sb([P, CHUNK], U8, "out_scales")

@@ -303,11 +303,11 @@ def tile_attend_gnce_pl_sgd_kernel(tc, xT, wT, y, wt, xm, offs, out_0, out_1, ou
             lo, hi = pieces[c]
             nc.scalar.copy(pairs_far[:, 1, lo - near:hi - near, 1], window[PACK - 1][:, lo:hi])
             if c > 1:
-                join(nc.scalar.copy, U32, c)
-        join(nc.vector.tensor_copy, I32, 0)
+                join(nc.scalar.copy, F32, c)
+        join(nc.vector.tensor_copy, F32, 0)
         for c in range(len(pieces)):
             if c < 1:
-                join(nc.vector.tensor_copy, I32, c + 1)
+                join(nc.vector.tensor_copy, F32, c + 1)
             quantise_out(c)
         scales_out = out_2[0].bitcast(I32)
         for q in range(4):

@@ -5,6 +5,7 @@ from concourse.masks import make_identity
 
 N, T, D, R = 512, 2048, 512, 1024
 LR, WD = 0.1, 0.5
+DECAY = 1.0 - LR * WD
 FLOPS = 2 * 2 * N * D * R
 
 F32 = mybir.dt.float32
@@ -23,23 +24,27 @@ PACK = 4
 PASSES = R // (P * PACK)
 CHUNK = 512
 CHUNKS = T // CHUNK
+HALF = N // 2
+PLANES = ((0, 3), (1, 2))
 
 
 def tile_attend_gnce_pl_sgd_kernel(tc, xT, wT, y, wt, xm, offs, out_0, out_1, out_2):
     nc = tc.nc
     with ExitStack() as ctx:
         held = ctx.enter_context(tc.tile_pool(name="held", bufs=1))
-        placed = ctx.enter_context(tc.tile_pool(name="placed", bufs=1))
         score_psum = ctx.enter_context(tc.psum_pool(name="score_psum", bufs=4))
         grad_psum = ctx.enter_context(tc.psum_pool(name="grad_psum", bufs=1))
 
         def sb(shape, dtype, name, tag=""):
             return held.tile(shape, dtype, name=name, tag=tag or name, align_bytes=256)
 
-        def at(offset, shape, dtype, name):
-            return placed.tile(shape, dtype, name=name, tag=name, align_bytes=64, offset=offset)
-
         offsets = held.tile([P, N // 16], U16, name="offsets")
+
+        def slots_of(h):
+            return slice(h * HALF, (h + 1) * HALF)
+
+        def offsets_of(h):
+            return offsets[:, h * HALF // 16:(h + 1) * HALF // 16]
 
         w_planes = wT.rearrange("(p t) c -> p t c", t=PACK)
         out_planes = out_0.rearrange("(p t) c -> p t c", t=PACK)
@@ -73,11 +78,9 @@ def tile_attend_gnce_pl_sgd_kernel(tc, xT, wT, y, wt, xm, offs, out_0, out_1, ou
             nc.sync.dma_start(xm_raw[g][:], xm[0, g * 512:(g + 1) * 512, :].rearrange("(p j) d -> p j d", j=PACK))
         window = [sb([P, T], F32, "window%d" % t) for t in range(PACK - 1)]
 
-        half = N // 2
         picked = sb([P, 2, N], F32, "picked")
-        picked_late = [sb([P, 2, half], F32, "picked_late%d" % h) for h in range(2)]
+        picked_late = [sb([P, 2, HALF], F32, "picked_late%d" % h) for h in range(2)]
         w_bf = sb([P, N, PACK], BF16, "w_bf")
-        decayed_first = [at(0, [P, half], F32, "decayed_first0"), sb([P, half], F32, "decayed_first1")]
         decayed = [None, sb([P, N], F32, "decayed1"), sb([P, N], F32, "decayed2")]
         for t in range(2):
             nc.vector.tensor_copy(picked[:, t, :], source[t][:].indirect(offsets[:]))
@@ -86,23 +89,16 @@ def tile_attend_gnce_pl_sgd_kernel(tc, xT, wT, y, wt, xm, offs, out_0, out_1, ou
             else:
                 nc.vector.tensor_copy(window[t][:], source[t][:])
                 nc.scalar.copy(w_bf[:, :, 0:2], picked[:].rearrange("p e n -> p n e"))
-            if t == 0:
-                for h in range(2):
-                    nc.scalar.activation(decayed_first[h][:], picked[:, 0, h * half:(h + 1) * half], ACT.Copy,
-                                         scale=1.0 - LR * WD)
-            else:
-                nc.scalar.activation(decayed[t][:], picked[:, t, :], ACT.Copy, scale=1.0 - LR * WD)
+                nc.scalar.activation(decayed[t][:], picked[:, t, :], ACT.Copy, scale=DECAY)
         for t in range(2, PACK):
             for h in range(2):
-                nc.vector.tensor_copy(picked_late[h][:, t - 2, :],
-                                      source[t][:].indirect(offsets[:, h * half // 16:(h + 1) * half // 16]))
+                nc.vector.tensor_copy(picked_late[h][:, t - 2, :], source[t][:].indirect(offsets_of(h)))
                 if t == 2:
-                    nc.scalar.activation(decayed[t][:, h * half:(h + 1) * half], picked_late[h][:, 0, :], ACT.Copy,
-                                         scale=1.0 - LR * WD)
+                    nc.scalar.activation(decayed[t][:, slots_of(h)], picked_late[h][:, 0, :], ACT.Copy, scale=DECAY)
             if t == 2:
                 nc.vector.tensor_copy(window[t][:, 0:3 * CHUNK], source[t][:, 0:3 * CHUNK])
                 nc.scalar.activation(window[t][:, 3 * CHUNK:T], source[t][:, 3 * CHUNK:T], ACT.Copy)
-        nc.scalar.copy(w_bf[:, 0:half, 2:4], picked_late[0][:].rearrange("p e n -> p n e"))
+        nc.scalar.copy(w_bf[:, 0:HALF, 2:4], picked_late[0][:].rearrange("p e n -> p n e"))
         w_codes = sb([P, N], U32, "w_codes")
         w_scales = sb([P, N], U8, "w_scales")
 
@@ -116,11 +112,14 @@ def tile_attend_gnce_pl_sgd_kernel(tc, xT, wT, y, wt, xm, offs, out_0, out_1, ou
         x_codes = [sb([P, 512], U32, "x_codes%d" % g) for g in range(PASSES)]
         x_scales = [sb([P, 512], U8, "x_scales%d" % g) for g in range(PASSES)]
         xm_scales = [sb([P, PASSES, 2 * P], U8, "xm_scales%d" % u) for u in range(2)]
-        xm_codes = [sb([P, PASSES, 2 * P], U32, "xm_codes0")]
+        xm_codes = [sb([P, PASSES, 2 * P], U32, "xm_codes%d" % u) for u in range(2)]
         g_rows = [sb([P, PACK, N], BF16, "g_rows0")]
         g_bf = [sb([P, N, PACK], BF16, "g_bf0"), sb([P, N, PACK], BF16, "g_bf1")]
-        g_codes = [sb([P, N], U32, "g_codes0")]
+        g_codes = [sb([P, N], U32, "g_codes%d" % g) for g in range(PASSES)]
         g_scales = [sb([P, N], U8, "g_scales%d" % g) for g in range(PASSES)]
+
+        def round_on_gpsimd(dst, src):
+            nc.gpsimd.tensor_scalar(dst, src, 1.0, -0.0, ALU.mult, ALU.add)
 
         def quantise_x(g):
             nc.vector.quantize_mx(x_codes[g][:].bitcast(E4), x_scales[g][:], x_bf[g][:].rearrange("p j s t -> p (j s t)"))
@@ -144,10 +143,6 @@ def tile_attend_gnce_pl_sgd_kernel(tc, xT, wT, y, wt, xm, offs, out_0, out_1, ou
             nc.vector.scalar_tensor_tensor(g_rows[g][:, j, :], sig, weight[:, g, j:j + 1],
                                            y_raw[g][:, j, :], ALU.mult, ALU.subtract)
 
-        def weave_g(engine_copy, g, lo, hi):
-            engine_copy(g_bf[g][:, lo:hi, :].rearrange("p (c i) j -> p c j i", i=4),
-                        g_rows[g][:, :, lo:hi].rearrange("p j (c i) -> p c j i", i=4))
-
         def quantise_g(g, lo=0, hi=N):
             nc.vector.quantize_mx(g_codes[g][:, lo:hi].bitcast(E5), g_scales[g][:, lo:hi],
                                   g_bf[g][:, lo:hi, :].rearrange("p n j -> p (n j)"))
@@ -155,7 +150,7 @@ def tile_attend_gnce_pl_sgd_kernel(tc, xT, wT, y, wt, xm, offs, out_0, out_1, ou
         def deal_xm(engine_copy, dst, g, u, lo=0, hi=P):
             engine_copy(
                 dst.rearrange("p e m j -> p m j e")[:, lo:hi],
-                xm_raw[g][:].rearrange("p j (m t) -> p m j t", t=PACK)[:, lo:hi, :, u:PACK:2],
+                xm_raw[g][:].rearrange("p j (m t) -> p m j t", t=PACK)[:, lo:hi, :, (slice(0, 4, 3), slice(1, 3))[u]],
             )
 
         def quantise_xm(u, g, src):
@@ -163,22 +158,24 @@ def tile_attend_gnce_pl_sgd_kernel(tc, xT, wT, y, wt, xm, offs, out_0, out_1, ou
                                   src.rearrange("p e m j -> p (e m j)"))
 
         def table_gradient(acc, t, slots):
+            u = 0 if t in PLANES[0] else 1
             cols = slice((t // 2) * P, (t // 2 + 1) * P)
-            order = range(PASSES - 1, -1, -1) if t == 3 else range(PASSES)
+            order = range(PASSES - 1, -1, -1) if t == 2 else range(PASSES)
             for g in order:
-                nc.tensor.matmul_mx(acc, lhsT=xm_codes[t % 2][:, g, cols].bitcast(E4),
-                                    lhsT_scale=xm_scales[t % 2][:, g, cols],
+                nc.tensor.matmul_mx(acc, lhsT=xm_codes[u][:, g, cols].bitcast(E4),
+                                    lhsT_scale=xm_scales[u][:, g, cols],
                                     rhs=g_codes[g][:, slots].bitcast(E5), rhs_scale=g_scales[g][:, slots],
                                     start=(g == order[0]), stop=(g == order[-1]))
 
         sig_rows = [sb([P, PACK, N], F32, "sig_rows0"), sb([P, PACK, N], F32, "sig_rows1")]
+
         def quantise_w(lo, hi):
             nc.vector.quantize_mx(w_codes[:, lo:hi].bitcast(E4), w_scales[:, lo:hi],
                                   w_bf[:, lo:hi, :].rearrange("p n t -> p (n t)"))
 
-        quantise_w(0, half)
-        nc.vector.tensor_copy(w_bf[:, half:N, 2:4], picked_late[1][:].rearrange("p e n -> p n e"))
-        quantise_w(half, N)
+        quantise_w(0, HALF)
+        nc.vector.tensor_copy(w_bf[:, HALF:N, 2:4], picked_late[1][:].rearrange("p e n -> p n e"))
+        quantise_w(HALF, N)
         for first in (0, 2):
             deal(nc.scalar.copy, 0, 0, 64, first, first + 2)
             deal(nc.vector.tensor_copy, 0, 64, P, first, first + 2)
@@ -198,8 +195,9 @@ def tile_attend_gnce_pl_sgd_kernel(tc, xT, wT, y, wt, xm, offs, out_0, out_1, ou
         gradient(0, 1, sig0[1])
         gradient(0, 2, sig0[2])
         gradient(0, 3, sig0[3])
-        weave_g(nc.scalar.copy, 0, 0, N)
-        for lanes, cols in ((slice(0, 2), slice(0, N)), (slice(2, 4), slice(0, half)), (slice(2, 4), slice(half, N))):
+        nc.scalar.copy(g_bf[0][:].rearrange("p (c i) j -> p c j i", i=4),
+                       g_rows[0][:].rearrange("p j (c i) -> p c j i", i=4))
+        for lanes, cols in ((slice(0, 2), slice(0, N)), (slice(2, 4), slice(0, HALF)), (slice(2, 4), slice(HALF, N))):
             nc.vector.tensor_tensor(y_raw[1][:, lanes, cols], sig_rows[1][:, lanes, cols], y_raw[1][:, lanes, cols],
                                     ALU.subtract)
         share = 64
@@ -208,106 +206,120 @@ def tile_attend_gnce_pl_sgd_kernel(tc, xT, wT, y, wt, xm, offs, out_0, out_1, ou
             nc.scalar.activation(g_rows[1][:, j, :], y_raw[1][:, j, 0:share], ACT.Copy, scale=weight[:, 1, j:j + 1])
         nc.scalar.copy(g_bf[1][:, 0:share, :].rearrange("p (c i) j -> p c j i", i=4),
                        g_rows[1][:].rearrange("p j (c i) -> p c j i", i=4))
-        for lo, hi in ((share, half), (half, N)):
+        for lo, hi in ((share, HALF), (HALF, N)):
             nc.vector.tensor_tensor(g_bf[1][:, lo:hi, :].rearrange("p (c i) j -> p c j i", i=2),
                                     y_raw[1][:, :, lo:hi].rearrange("p j (c i) -> p c j i", i=2),
                                     weight[:, 1, 0:PACK].unsqueeze(1).unsqueeze(3).to_broadcast([P, (hi - lo) // 2, PACK, 2]),
                                     ALU.mult)
-        xm_bf = sb([P, PASSES, 2, P, PACK], BF16, "xm_bf0")
+        xm_early = sb([P, PASSES, 2, P, PACK], BF16, "xm_early")
         xm_late = [sb([P, 2, P, PACK], BF16, "xm_late0")]
-        deal_xm(nc.scalar.copy, xm_bf[:, 0], 0, 0)
-        deal_xm(nc.scalar.copy, xm_bf[:, 1], 1, 0, 0, 48)
-        deal_xm(nc.scalar.copy, xm_late[0][:], 1, 1)
-        g_codes.append(sb([P, N], U32, "g_codes1"))
+        deal_xm(nc.scalar.copy, xm_early[:, 0], 0, 0)
+        deal_xm(nc.scalar.copy, xm_early[:, 1], 1, 0, 0, 48)
+        deal_xm(nc.scalar.copy, xm_late[0][:], 0, 1)
         quantise_g(0)
-        quantise_xm(0, 0, xm_bf[:, 0])
-        quantise_g(1, 0, half)
-        deal_xm(nc.vector.tensor_copy, xm_bf[:, 1], 1, 0, 48, P)
-        quantise_g(1, half, N)
-        quantise_xm(0, 1, xm_bf[:, 1])
-        xm_late.append(sb([P, 2, P, PACK], BF16, "xm_late1", tag="xm_bf0"))
-        deal_xm(nc.vector.tensor_copy, xm_late[1][:], 0, 1)
-        fresh = [sb([P, N], F32, "fresh%d" % t) for t in range(PACK)]
-
-        def update(t, kept):
-            acc = grad_psum.tile([P, N], F32, name="grad%d" % t)
-            table_gradient(acc[:], t, slice(0, N))
-            nc.vector.scalar_tensor_tensor(fresh[t][:], acc[:], -LR, kept, ALU.mult, ALU.add)
-
-        for h in range(2):
-            slots = slice(h * half, (h + 1) * half)
-            acc = score_psum.tile([P, half], F32, name="bank")
-            table_gradient(acc[:], 0, slots)
-            nc.vector.scalar_tensor_tensor(fresh[0][:, slots], acc[:], -LR, decayed_first[h][:], ALU.mult, ALU.add)
-            if h == 0:
-                xm_codes.append(at(0, [P, PASSES, 2 * P], U32, "xm_codes1"))
-                quantise_xm(1, 0, xm_late[1][:])
-                quantise_xm(1, 1, xm_late[0][:])
-        decayed_last = sb([P, N], F32, "decayed_last", tag="xm_late0")
-        for h in range(2):
-            nc.gpsimd.tensor_scalar(decayed_last[:, h * half:(h + 1) * half], picked_late[h][:, 1, :], 1.0 - LR * WD, 0.0,
-                                    ALU.mult, ALU.add)
-        update(2, decayed[2][:])
-        update(1, decayed[1][:])
-        window.append(sb([P, T], F32, "window3", tag="xm_raw0"))
+        quantise_xm(0, 0, xm_early[:, 0])
+        quantise_g(1, 0, HALF)
+        deal_xm(nc.vector.tensor_copy, xm_early[:, 1], 1, 0, 48, P)
+        quantise_g(1, HALF, N)
+        quantise_xm(0, 1, xm_early[:, 1])
+        xm_late.append(sb([P, 2, P, PACK], BF16, "xm_late1", tag="xm_early"))
+        deal_xm(nc.vector.tensor_copy, xm_late[1][:], 1, 1, 0, 64)
+        deal_xm(nc.scalar.copy, xm_late[1][:], 1, 1, 64, P)
+        quantise_xm(1, 0, xm_late[0][:])
+        window.append(sb([P, T], F32, "window3", tag="x_raw1"))
         nc.sync.dma_start(window[3][:], w_planes[:, 3, :])
 
-        def scatter_on_scalar(t):
-            for h in range(2):
-                nc.scalar.activation(window[t][:].indirect(offsets[:, h * half // 16:(h + 1) * half // 16]),
-                                     fresh[t][:, h * half:(h + 1) * half], ACT.Copy)
-            nc.sync.dma_start(out_planes[:, t, :], window[t][:])
+        near = CHUNK
+        pairs_near = sb([P, 4 * near], BF16, "pairs_near")
+        pairs_far = sb([P, 4 * (T - near)], BF16, "pairs_far")
+        own = 256
+        fresh = [sb([P, N], F32, "fresh0")[:], sb([P, N], F32, "fresh1")[:],
+                 pairs_near[:].bitcast(F32)[:, near - own:near - own + N], sb([P, N], F32, "fresh3")[:]]
+
+        def update(t, acc, h):
+            old = picked[:, 0, slots_of(h)] if t == 0 else picked_late[h][:, 1, :]
+            nc.vector.scalar_tensor_tensor(fresh[t][:, slots_of(h)], acc, -LR / DECAY, old, ALU.mult, ALU.add)
+
+        def scatter(t, h):
+            nc.scalar.activation(window[t][:].indirect(offsets_of(h)), fresh[t][:, slots_of(h)], ACT.Copy, scale=DECAY)
+            if h == 1:
+                nc.sync.dma_start(out_planes[:, t, :], window[t][:])
 
         def scatter_on_vector(t):
-            nc.vector.tensor_copy(window[t][:].indirect(offsets[:]), fresh[t][:])
+            nc.vector.scalar_tensor_tensor(fresh[t], grad[t][:], -LR, decayed[t][:], ALU.mult, ALU.add)
+            nc.vector.tensor_copy(window[t][:].indirect(offsets[:]), fresh[t])
             nc.sync.dma_start(out_planes[:, t, :], window[t][:])
 
-        near = CHUNK
-        pairs_far = sb([P, 2, T - near, 2], BF16, "pairs_far")
-        scatter_on_scalar(0)
+        def halves(t, lo, hi):
+            pairs, base, width = (pairs_near, 0, near) if lo < near else (pairs_far, near, T - near)
+            first = 2 * ((t // 2) * width - base) + t % 2
+            return pairs[:, first + 2 * lo:first + 2 * hi - 1:2]
+
+        for h in range(2):
+            acc = score_psum.tile([P, HALF], F32, name="bank")
+            table_gradient(acc[:], 0, slots_of(h))
+            update(0, acc[:], h)
+            if h == 0:
+                quantise_xm(1, 1, xm_late[1][:])
+        grad = {}
+        for t in (3, 1, 2):
+            grad[t] = grad_psum.tile([P, N], F32, name="grad%d" % t)
+            table_gradient(grad[t][:], t, slice(0, N))
+        for h in range(2):
+            scatter(0, h)
+        for h in range(2):
+            update(3, grad[3][:, slots_of(h)], h)
         scatter_on_vector(1)
         for t in range(2):
-            nc.gpsimd.tensor_scalar(pairs_far[:, 0, :, t], window[t][:, near:T], 1.0, -0.0, ALU.mult, ALU.add)
-        scatter_on_scalar(2)
-        update(3, decayed_last[:])
-        scatter_on_vector(3)
-        nc.scalar.copy(pairs_far[:, 1, :, 0], window[2][:, near:T])
-        pairs_near = sb([P, 2, near, 2], BF16, "pairs_near", tag="fresh3")
+            round_on_gpsimd(halves(t, near, T), window[t][:, near:T])
+            round_on_gpsimd(halves(t, 0, near - own), window[t][:, 0:near - own])
+        for h in range(2):
+            scatter(3, h)
+        scatter_on_vector(2)
+        nc.scalar.copy(halves(3, near, T), window[3][:, near:T])
 
-        pieces = [(0, 512), (512, 1024), (1024, 1536), (1536, 1792), (1792, 2048)]
-        reuse = ["x_bf0", "x_bf1", "g_rows0", "y_raw1", "g_bf0"]
+        pieces = [(0, 512), (512, 1024), (1024, 1280), (1280, 1536), (1536, 1792), (1792, 2048)]
+        reuse = ["x_bf0", "x_bf1", "g_rows0", "y_raw1", "g_bf0", "y_raw0"]
+        on_vector = 3
         out_bf = [sb([P, hi - lo, PACK], BF16, "out_bf%d" % c, tag=reuse[c]) for c, (lo, hi) in enumerate(pieces)]
-        out_codes = [sb([P, hi - lo], U32, "out_codes%d" % c) for c, (lo, hi) in enumerate(pieces)]
+        stores = [(0, 512), (512, 1024), (1024, 1536), (1536, 1792), (1792, 2048)]
+        out_codes = [sb([P, hi - lo], U32, "out_codes%d" % c) for c, (lo, hi) in enumerate(stores)]
         out_scales = sb([P, CHUNK], U8, "out_scales")
         words_out = out_1[0].rearrange("p c l -> p (c l)").bitcast(I32)
 
-        def join(engine_copy, word, c):
+        def join(engine_copy, c):
             lo, hi = pieces[c]
-            pairs, base = (pairs_near, 0) if lo < near else (pairs_far, near)
-            src = pairs[:].rearrange("p u n e -> p u (n e)").bitcast(word)[:, :, lo - base:hi - base]
-            dst = out_bf[c][:].rearrange("p n t -> p (n t)").bitcast(word).rearrange("p (n u) -> p n u", u=2)
+            if lo < near:
+                src = pairs_near[:].bitcast(F32).rearrange("p (u n) -> p u n", u=2)[:, :, lo:hi]
+            else:
+                src = pairs_far[:].bitcast(F32).rearrange("p (u n) -> p u n", u=2)[:, :, lo - near:hi - near]
+            dst = out_bf[c][:].rearrange("p n t -> p (n t)").bitcast(F32).rearrange("p (n u) -> p n u", u=2)
             engine_copy(dst, src.rearrange("p u n -> p n u"))
 
         def quantise_out(c):
             lo, hi = pieces[c]
-            for a in range(lo, hi, half):
+            k = [last >= hi for first, last in stores].index(True)
+            first, last = stores[k]
+            for a in range(lo, hi, HALF):
                 row = 4 * (a // CHUNK)
-                nc.vector.quantize_mx(out_codes[c][:, a - lo:a - lo + half].bitcast(E4),
-                                      out_scales[row:P, a % CHUNK:a % CHUNK + half],
-                                      out_bf[c][:, a - lo:a - lo + half, :].rearrange("p n t -> p (n t)"))
-            nc.sync.dma_start(words_out[:, lo:hi], out_codes[c][:].bitcast(I32))
+                nc.vector.quantize_mx(out_codes[k][:, a - first:a - first + HALF].bitcast(E4),
+                                      out_scales[row:P, a % CHUNK:a % CHUNK + HALF],
+                                      out_bf[c][:, a - lo:a - lo + HALF, :].rearrange("p n t -> p (n t)"))
+            if hi == last:
+                nc.sync.dma_start(words_out[:, first:last], out_codes[k][:].bitcast(I32))
 
         for t in range(PACK):
-            nc.vector.tensor_copy(pairs_near[:, t // 2, :, t % 2], window[t][:, 0:near])
+            lo = near - own if t < 2 else 0
+            nc.vector.tensor_copy(halves(t, lo, near), window[t][:, lo:near])
         for c in range(1, len(pieces)):
             lo, hi = pieces[c]
-            nc.scalar.copy(pairs_far[:, 1, lo - near:hi - near, 1], window[PACK - 1][:, lo:hi])
-            if c > 1:
-                join(nc.scalar.copy, F32, c)
-        join(nc.vector.tensor_copy, F32, 0)
+            nc.scalar.copy(halves(2, lo, hi), window[2][:, lo:hi])
+            if c >= on_vector:
+                join(nc.scalar.copy, c)
+        join(nc.vector.tensor_copy, 0)
         for c in range(len(pieces)):
-            if c < 1:
-                join(nc.vector.tensor_copy, F32, c + 1)
+            if c + 1 < on_vector:
+                join(nc.vector.tensor_copy, c + 1)
             quantise_out(c)
         scales_out = out_2[0].bitcast(I32)
         for q in range(4):

@@ -25,7 +25,7 @@ PASSES = R // (P * PACK)
 CHUNK = 512
 CHUNKS = T // CHUNK
 HALF = N // 2
-PLANES = ((0, 3), (1, 2))
+PLANES = ((0, 2), (1, 3))
 
 
 def tile_attend_gnce_pl_sgd_kernel(tc, xT, wT, y, wt, xm, offs, out_0, out_1, out_2):
@@ -81,7 +81,7 @@ def tile_attend_gnce_pl_sgd_kernel(tc, xT, wT, y, wt, xm, offs, out_0, out_1, ou
         picked = sb([P, 2, N], F32, "picked")
         picked_late = [sb([P, 2, HALF], F32, "picked_late%d" % h) for h in range(2)]
         w_bf = sb([P, N, PACK], BF16, "w_bf")
-        decayed = [None, sb([P, N], F32, "decayed1"), sb([P, N], F32, "decayed2")]
+        decayed = [None, sb([P, N], F32, "decayed1"), None, sb([P, N], F32, "decayed3")]
         for t in range(2):
             nc.vector.tensor_copy(picked[:, t, :], source[t][:].indirect(offsets[:]))
             if t == 0:
@@ -93,12 +93,12 @@ def tile_attend_gnce_pl_sgd_kernel(tc, xT, wT, y, wt, xm, offs, out_0, out_1, ou
         for t in range(2, PACK):
             for h in range(2):
                 nc.vector.tensor_copy(picked_late[h][:, t - 2, :], source[t][:].indirect(offsets_of(h)))
-                if t == 2:
-                    nc.scalar.activation(decayed[t][:, slots_of(h)], picked_late[h][:, 0, :], ACT.Copy, scale=DECAY)
             if t == 2:
                 nc.vector.tensor_copy(window[t][:, 0:3 * CHUNK], source[t][:, 0:3 * CHUNK])
                 nc.scalar.activation(window[t][:, 3 * CHUNK:T], source[t][:, 3 * CHUNK:T], ACT.Copy)
         nc.scalar.copy(w_bf[:, 0:HALF, 2:4], picked_late[0][:].rearrange("p e n -> p n e"))
+        for h in range(2):
+            nc.scalar.activation(decayed[3][:, slots_of(h)], picked_late[h][:, 1, :], ACT.Copy, scale=DECAY)
         w_codes = sb([P, N], U32, "w_codes")
         w_scales = sb([P, N], U8, "w_scales")
 
@@ -150,7 +150,7 @@ def tile_attend_gnce_pl_sgd_kernel(tc, xT, wT, y, wt, xm, offs, out_0, out_1, ou
         def deal_xm(engine_copy, dst, g, u, lo=0, hi=P):
             engine_copy(
                 dst.rearrange("p e m j -> p m j e")[:, lo:hi],
-                xm_raw[g][:].rearrange("p j (m t) -> p m j t", t=PACK)[:, lo:hi, :, (slice(0, 4, 3), slice(1, 3))[u]],
+                xm_raw[g][:].rearrange("p j (m t) -> p m j t", t=PACK)[:, lo:hi, :, u:PACK:2],
             )
 
         def quantise_xm(u, g, src):
@@ -160,7 +160,7 @@ def tile_attend_gnce_pl_sgd_kernel(tc, xT, wT, y, wt, xm, offs, out_0, out_1, ou
         def table_gradient(acc, t, slots):
             u = 0 if t in PLANES[0] else 1
             cols = slice((t // 2) * P, (t // 2 + 1) * P)
-            order = range(PASSES - 1, -1, -1) if t == 2 else range(PASSES)
+            order = range(PASSES - 1, -1, -1) if t == 3 else range(PASSES)
             for g in order:
                 nc.tensor.matmul_mx(acc, lhsT=xm_codes[u][:, g, cols].bitcast(E4),
                                     lhsT_scale=xm_scales[u][:, g, cols],
@@ -226,18 +226,18 @@ def tile_attend_gnce_pl_sgd_kernel(tc, xT, wT, y, wt, xm, offs, out_0, out_1, ou
         deal_xm(nc.vector.tensor_copy, xm_late[1][:], 1, 1, 0, 64)
         deal_xm(nc.scalar.copy, xm_late[1][:], 1, 1, 64, P)
         quantise_xm(1, 0, xm_late[0][:])
-        window.append(sb([P, T], F32, "window3", tag="x_raw1"))
+        window.append(sb([P, T], F32, "window3", tag="xm_raw1"))
         nc.sync.dma_start(window[3][:], w_planes[:, 3, :])
 
         near = CHUNK
         pairs_near = sb([P, 4 * near], BF16, "pairs_near")
         pairs_far = sb([P, 4 * (T - near)], BF16, "pairs_far")
         own = 256
-        fresh = [sb([P, N], F32, "fresh0")[:], sb([P, N], F32, "fresh1")[:],
-                 pairs_near[:].bitcast(F32)[:, near - own:near - own + N], sb([P, N], F32, "fresh3")[:]]
+        fresh = [sb([P, N], F32, "fresh%d" % t)[:] for t in range(PACK - 1)]
+        fresh.append(pairs_near[:].bitcast(F32)[:, near - own:near - own + N])
 
         def update(t, acc, h):
-            old = picked[:, 0, slots_of(h)] if t == 0 else picked_late[h][:, 1, :]
+            old = picked[:, 0, slots_of(h)] if t == 0 else picked_late[h][:, 0, :]
             nc.vector.scalar_tensor_tensor(fresh[t][:, slots_of(h)], acc, -LR / DECAY, old, ALU.mult, ALU.add)
 
         def scatter(t, h):
@@ -262,21 +262,21 @@ def tile_attend_gnce_pl_sgd_kernel(tc, xT, wT, y, wt, xm, offs, out_0, out_1, ou
             if h == 0:
                 quantise_xm(1, 1, xm_late[1][:])
         grad = {}
-        for t in (3, 1, 2):
+        for t in (2, 1, 3):
             grad[t] = grad_psum.tile([P, N], F32, name="grad%d" % t)
             table_gradient(grad[t][:], t, slice(0, N))
         for h in range(2):
             scatter(0, h)
         for h in range(2):
-            update(3, grad[3][:, slots_of(h)], h)
+            update(2, grad[2][:, slots_of(h)], h)
         scatter_on_vector(1)
         for t in range(2):
             round_on_gpsimd(halves(t, near, T), window[t][:, near:T])
             round_on_gpsimd(halves(t, 0, near - own), window[t][:, 0:near - own])
         for h in range(2):
-            scatter(3, h)
-        scatter_on_vector(2)
-        nc.scalar.copy(halves(3, near, T), window[3][:, near:T])
+            scatter(2, h)
+        scatter_on_vector(3)
+        nc.scalar.copy(halves(2, near, T), window[2][:, near:T])
 
         pieces = [(0, 512), (512, 1024), (1024, 1280), (1280, 1536), (1536, 1792), (1792, 2048)]
         reuse = ["x_bf0", "x_bf1", "g_rows0", "y_raw1", "g_bf0", "y_raw0"]
@@ -313,7 +313,7 @@ def tile_attend_gnce_pl_sgd_kernel(tc, xT, wT, y, wt, xm, offs, out_0, out_1, ou
             nc.vector.tensor_copy(halves(t, lo, near), window[t][:, lo:near])
         for c in range(1, len(pieces)):
             lo, hi = pieces[c]
-            nc.scalar.copy(halves(2, lo, hi), window[2][:, lo:hi])
+            nc.scalar.copy(halves(3, lo, hi), window[3][:, lo:hi])
             if c >= on_vector:
                 join(nc.scalar.copy, c)
         join(nc.vector.tensor_copy, 0)

@@ -232,7 +232,7 @@ def tile_attend_gnce_pl_sgd_kernel(tc, xT, wT, y, wt, xm, offs, out_0, out_1, ou
         near = CHUNK
         pairs_near = sb([P, 4 * near], BF16, "pairs_near")
         pairs_far = sb([P, 4 * (T - near)], BF16, "pairs_far")
-        own = 256
+        own = 512
         fresh = [sb([P, N], F32, "fresh%d" % t)[:] for t in range(PACK - 1)]
         fresh.append(pairs_near[:].bitcast(F32)[:, near - own:near - own + N])
 
@@ -272,7 +272,6 @@ def tile_attend_gnce_pl_sgd_kernel(tc, xT, wT, y, wt, xm, offs, out_0, out_1, ou
         scatter_on_vector(1)
         for t in range(2):
             round_on_gpsimd(halves(t, near, T), window[t][:, near:T])
-            round_on_gpsimd(halves(t, 0, near - own), window[t][:, 0:near - own])
         for h in range(2):
             scatter(2, h)
         scatter_on_vector(3)

@@ -234,7 +234,7 @@ def tile_attend_gnce_pl_sgd_kernel(tc, xT, wT, y, wt, xm, offs, out_0, out_1, ou
         pairs_far = sb([P, 4 * (T - near)], BF16, "pairs_far")
         own = 512
         fresh = [sb([P, N], F32, "fresh%d" % t)[:] for t in range(PACK - 1)]
-        fresh.append(pairs_near[:].bitcast(F32)[:, near - own:near - own + N])
+        fresh.append(pairs_near[:].bitcast(F32)[:, near - HALF:near + HALF])
 
         def update(t, acc, h):
             old = picked[:, 0, slots_of(h)] if t == 0 else picked_late[h][:, 0, :]

@@ -68,6 +68,12 @@ def tile_attend_gnce_pl_sgd_kernel(tc, xT, wT, y, wt, xm, offs, out_0, out_1, ou
             nc.tensor.transpose(turned[:, j * P:(j + 1) * P], wt_rows[:, j:512:PACK], identity[:])
         weight = sb([P, PASSES, PACK], F32, "weight")
         nc.scalar.copy(weight[:], turned[:].rearrange("p (j k) -> p k j", j=PACK)[:, 0:PASSES, :])
+        spread = score_psum.tile([P, 512], F32, name="bank")
+        for j in range(PACK):
+            nc.tensor.transpose(spread[:, j * P:(j + 1) * P], weight[:, 1, j:j + 1].to_broadcast([P, P]), identity[:])
+        minus_wt = sb([P, 512], F32, "minus_wt")
+        nc.scalar.activation(minus_wt[:].rearrange("p (s j) -> p s j", j=PACK),
+                             spread[:].rearrange("p (j s) -> p s j", j=PACK), ACT.Copy, scale=-1.0)
         for g in range(PASSES):
             nc.sync.dma_start(x_raw[g][:], xT[0, :, g * 512:(g + 1) * 512].rearrange("(p t) r -> p t r", t=PACK))
         for g in range(PASSES):
@@ -129,7 +135,7 @@ def tile_attend_gnce_pl_sgd_kernel(tc, xT, wT, y, wt, xm, offs, out_0, out_1, ou
             cols = slice(j * P, (j + 1) * P)
             nc.tensor.matmul_mx(bank[:], lhsT=x_codes[g][:, cols].bitcast(E4), lhsT_scale=x_scales[g][:, cols],
                                 rhs=w_codes[:].bitcast(E4), rhs_scale=w_scales[:], start=True, stop=True)
-            nc.scalar.activation(sig_rows[g][:, j, :], bank[:], ACT.Sigmoid)
+            nc.scalar.activation(sig_rows[g][:, j, :], bank[:], ACT.Sigmoid, scale=1.0 if g == 0 else -1.0)
             return sig_rows[g][:, j, :]
 
         def weigh_y(on_vector, g, j):
@@ -186,34 +192,39 @@ def tile_attend_gnce_pl_sgd_kernel(tc, xT, wT, y, wt, xm, offs, out_0, out_1, ou
         sig0 = [score(0, j) for j in range(PACK)]
         weigh_y(True, 0, 0)
         quantise_x(1)
-        weigh_y(False, 0, 3)
         for j in range(PACK):
             score(1, j)
         weigh_y(True, 0, 1)
         gradient(0, 0, sig0[0])
         weigh_y(True, 0, 2)
         gradient(0, 1, sig0[1])
+        weigh_y(True, 0, 3)
         gradient(0, 2, sig0[2])
         gradient(0, 3, sig0[3])
         nc.scalar.copy(g_bf[0][:].rearrange("p (c i) j -> p c j i", i=4),
                        g_rows[0][:].rearrange("p j (c i) -> p c j i", i=4))
-        for lanes, cols in ((slice(0, 2), slice(0, N)), (slice(2, 4), slice(0, HALF)), (slice(2, 4), slice(HALF, N))):
-            nc.vector.tensor_tensor(y_raw[1][:, lanes, cols], sig_rows[1][:, lanes, cols], y_raw[1][:, lanes, cols],
-                                    ALU.subtract)
-        share = 64
-        g_rows.append(sb([P, PACK, share], BF16, "g_rows1"))
-        for j in range(PACK):
-            nc.scalar.activation(g_rows[1][:, j, :], y_raw[1][:, j, 0:share], ACT.Copy, scale=weight[:, 1, j:j + 1])
-        nc.scalar.copy(g_bf[1][:, 0:share, :].rearrange("p (c i) j -> p c j i", i=4),
-                       g_rows[1][:].rearrange("p j (c i) -> p c j i", i=4))
-        for lo, hi in ((share, HALF), (HALF, N)):
-            nc.vector.tensor_tensor(g_bf[1][:, lo:hi, :].rearrange("p (c i) j -> p c j i", i=2),
-                                    y_raw[1][:, :, lo:hi].rearrange("p j (c i) -> p c j i", i=2),
-                                    weight[:, 1, 0:PACK].unsqueeze(1).unsqueeze(3).to_broadcast([P, (hi - lo) // 2, PACK, 2]),
-                                    ALU.mult)
+        blocks = N // P
+        g_turned = [sb([P, 512], BF16, "g_turned%d" % b) for b in range(blocks)]
+        for b in range(blocks):
+            total = grad_psum.tile([P, 512], F32, name="grad%d" % b)
+            parts = [rows[:, j, b * P:(b + 1) * P] for rows in (y_raw[1], sig_rows[1]) for j in range(PACK)]
+            for k, part in enumerate(parts):
+                j = k % PACK
+                nc.tensor.matmul(total[:, j * P:(j + 1) * P], lhsT=part, rhs=identity[:], is_transpose=True,
+                                 start=(k == 0), stop=(k == len(parts) - 1))
+            nc.vector.scalar_tensor_tensor(g_turned[b][:].rearrange("p (s j) -> p s j", j=PACK),
+                                           total[:].rearrange("p (j s) -> p s j", j=PACK), -1.0,
+                                           minus_wt[:].rearrange("p (s j) -> p s j", j=PACK), ALU.add, ALU.mult)
+        for b in range(blocks):
+            back = score_psum.tile([P, 2 * P], F32, name="bank")
+            words = g_turned[b][:].bitcast(F32)
+            for u in range(2):
+                nc.tensor.transpose(back[:, u * P:(u + 1) * P], words[:, u:2 * P:2], identity[:])
+            nc.scalar.copy(g_bf[1][:, b * P:(b + 1) * P, :].rearrange("p n j -> p (n j)").bitcast(F32)
+                           .rearrange("p (n u) -> p n u", u=2), back[:].rearrange("p (u n) -> p n u", u=2))
         xm_early = sb([P, PASSES, 2, P, PACK], BF16, "xm_early")
-        xm_late = [sb([P, 2, P, PACK], BF16, "xm_late0")]
-        deal_xm(nc.scalar.copy, xm_early[:, 0], 0, 0)
+        xm_late = [sb([P, 2, P, PACK], BF16, "xm_late0", tag="g_turned3")]
+        deal_xm(nc.vector.tensor_copy, xm_early[:, 0], 0, 0)
         deal_xm(nc.scalar.copy, xm_early[:, 1], 1, 0, 0, 48)
         deal_xm(nc.scalar.copy, xm_late[0][:], 0, 1)
         quantise_g(0)
@@ -223,9 +234,7 @@ def tile_attend_gnce_pl_sgd_kernel(tc, xT, wT, y, wt, xm, offs, out_0, out_1, ou
         quantise_g(1, HALF, N)
         quantise_xm(0, 1, xm_early[:, 1])
         xm_late.append(sb([P, 2, P, PACK], BF16, "xm_late1", tag="xm_early"))
-        deal_xm(nc.vector.tensor_copy, xm_late[1][:], 1, 1, 0, 64)
-        deal_xm(nc.scalar.copy, xm_late[1][:], 1, 1, 64, P)
-        quantise_xm(1, 0, xm_late[0][:])
+        deal_xm(nc.vector.tensor_copy, xm_late[1][:], 1, 1)
         window.append(sb([P, T], F32, "window3", tag="xm_raw1"))
         nc.sync.dma_start(window[3][:], w_planes[:, 3, :])
 
@@ -260,6 +269,7 @@ def tile_attend_gnce_pl_sgd_kernel(tc, xT, wT, y, wt, xm, offs, out_0, out_1, ou
             table_gradient(acc[:], 0, slots_of(h))
             update(0, acc[:], h)
             if h == 0:
+                quantise_xm(1, 0, xm_late[0][:])
                 quantise_xm(1, 1, xm_late[1][:])
         grad = {}
         for t in (2, 1, 3):

@@ -32,7 +32,7 @@ def tile_attend_gnce_pl_sgd_kernel(tc, xT, wT, y, wt, xm, offs, out_0, out_1, ou
     nc = tc.nc
     with ExitStack() as ctx:
         held = ctx.enter_context(tc.tile_pool(name="held", bufs=1))
-        score_psum = ctx.enter_context(tc.psum_pool(name="score_psum", bufs=4))
+        score_psum = ctx.enter_context(tc.psum_pool(name="score_psum", bufs=3))
         grad_psum = ctx.enter_context(tc.psum_pool(name="grad_psum", bufs=1))
 
         def sb(shape, dtype, name, tag=""):
@@ -67,19 +67,24 @@ def tile_attend_gnce_pl_sgd_kernel(tc, xT, wT, y, wt, xm, offs, out_0, out_1, ou
         for j in range(PACK):
             nc.tensor.transpose(turned[:, j * P:(j + 1) * P], wt_rows[:, j:512:PACK], identity[:])
         weight = sb([P, PASSES, PACK], F32, "weight")
-        nc.scalar.copy(weight[:], turned[:].rearrange("p (j k) -> p k j", j=PACK)[:, 0:PASSES, :])
+        nc.scalar.copy(weight[:, 0, :], turned[:, 0:512:P])
+        turned = score_psum.tile([P, N], F32, name="bank")
+        for j in range(PACK):
+            first = 256 * (j % 2) + j // 2
+            nc.tensor.transpose(turned[:, j * P:(j + 1) * P], wt_rows[:, first:first + 255:2], identity[:])
+        nc.scalar.copy(weight[:, 1, :], turned[:, 1:512:P])
         spread = score_psum.tile([P, 512], F32, name="bank")
         for j in range(PACK):
             nc.tensor.transpose(spread[:, j * P:(j + 1) * P], weight[:, 1, j:j + 1].to_broadcast([P, P]), identity[:])
         minus_wt = sb([P, 512], F32, "minus_wt")
-        nc.scalar.activation(minus_wt[:].rearrange("p (s j) -> p s j", j=PACK),
-                             spread[:].rearrange("p (j s) -> p s j", j=PACK), ACT.Copy, scale=-1.0)
+        nc.scalar.activation(minus_wt[:], spread[:], ACT.Copy, scale=-1.0)
         for g in range(PASSES):
             nc.sync.dma_start(x_raw[g][:], xT[0, :, g * 512:(g + 1) * 512].rearrange("(p t) r -> p t r", t=PACK))
-        for g in range(PASSES):
-            y_rows = y[0, g * 512:(g + 1) * 512, :].rearrange("(p j) n -> p j n", j=PACK)
-            for lo, hi in ((0, 2), (2, 4)) if g == 0 else ((0, PACK),):
-                nc.sync.dma_start(y_raw[g][:, lo:hi, :], y_rows[:, lo:hi, :])
+        y_rows = y[0, 0:512, :].rearrange("(p j) n -> p j n", j=PACK)
+        for lo, hi in ((0, 2), (2, 4)):
+            nc.sync.dma_start(y_raw[0][:, lo:hi, :], y_rows[:, lo:hi, :])
+        nc.sync.dma_start(y_raw[1][:].rearrange("p (h u) n -> p h (u n)", h=2),
+                          y[0, 512:R, :].rearrange("(h p u) n -> p h (u n)", h=2, u=2))
         for g in range(PASSES):
             nc.sync.dma_start(xm_raw[g][:], xm[0, g * 512:(g + 1) * 512, :].rearrange("(p j) d -> p j d", j=PACK))
         window = [sb([P, T], F32, "window%d" % t) for t in range(PACK - 1)]
@@ -154,10 +159,16 @@ def tile_attend_gnce_pl_sgd_kernel(tc, xT, wT, y, wt, xm, offs, out_0, out_1, ou
                                   g_bf[g][:, lo:hi, :].rearrange("p n j -> p (n j)"))
 
         def deal_xm(engine_copy, dst, g, u, lo=0, hi=P):
-            engine_copy(
-                dst.rearrange("p e m j -> p m j e")[:, lo:hi],
-                xm_raw[g][:].rearrange("p j (m t) -> p m j t", t=PACK)[:, lo:hi, :, u:PACK:2],
-            )
+            if g == 0:
+                engine_copy(
+                    dst.rearrange("p e m j -> p m j e")[:, lo:hi],
+                    xm_raw[g][:].rearrange("p j (m t) -> p m j t", t=PACK)[:, lo:hi, :, u:PACK:2],
+                )
+            else:
+                engine_copy(
+                    dst.rearrange("p e m (a b) -> p m a b e", a=2)[:, lo:hi],
+                    xm_raw[g][:].rearrange("p (b a) (m t) -> p m a b t", b=2, t=PACK)[:, lo:hi, :, :, u:PACK:2],
+                )
 
         def quantise_xm(u, g, src):
             nc.vector.quantize_mx(xm_codes[u][:, g, :].bitcast(E4), xm_scales[u][:, g, :],
@@ -188,7 +199,8 @@ def tile_attend_gnce_pl_sgd_kernel(tc, xT, wT, y, wt, xm, offs, out_0, out_1, ou
         for lo in (0, 2):
             nc.vector.quantize_mx(x_codes[0][:, lo * P:(lo + 2) * P].bitcast(E4), x_scales[0][:, lo * P:(lo + 2) * P],
                                   x_bf[0][:, lo:lo + 2].rearrange("p j s t -> p (j s t)"))
-        deal(nc.vector.tensor_copy, 1, 0, P)
+        nc.vector.tensor_copy(x_bf[1][:].rearrange("p (u h) s t -> p (h s) t u", u=2),
+                              x_raw[1][:].rearrange("p t (c u) -> p c t u", u=2))
         sig0 = [score(0, j) for j in range(PACK)]
         weigh_y(True, 0, 0)
         quantise_x(1)
@@ -207,19 +219,18 @@ def tile_attend_gnce_pl_sgd_kernel(tc, xT, wT, y, wt, xm, offs, out_0, out_1, ou
         g_turned = [sb([P, 512], BF16, "g_turned%d" % b) for b in range(blocks)]
         for b in range(blocks):
             total = grad_psum.tile([P, 512], F32, name="grad%d" % b)
-            parts = [rows[:, j, b * P:(b + 1) * P] for rows in (y_raw[1], sig_rows[1]) for j in range(PACK)]
-            for k, part in enumerate(parts):
-                j = k % PACK
-                nc.tensor.matmul(total[:, j * P:(j + 1) * P], lhsT=part, rhs=identity[:], is_transpose=True,
-                                 start=(k == 0), stop=(k == len(parts) - 1))
-            nc.vector.scalar_tensor_tensor(g_turned[b][:].rearrange("p (s j) -> p s j", j=PACK),
-                                           total[:].rearrange("p (j s) -> p s j", j=PACK), -1.0,
-                                           minus_wt[:].rearrange("p (s j) -> p s j", j=PACK), ALU.add, ALU.mult)
+            parts = [(sig_rows[1], 0), (sig_rows[1], 1)] + [(y_raw[1], j) for j in range(PACK)]
+            parts = parts + [(sig_rows[1], 2), (sig_rows[1], 3)]
+            for k, (rows, j) in enumerate(parts):
+                lane = j if rows is sig_rows[1] else 2 * (j % 2) + j // 2
+                nc.tensor.matmul(total[:, j * P:(j + 1) * P], lhsT=rows[:, lane, b * P:(b + 1) * P], rhs=identity[:],
+                                 is_transpose=True, start=(k == 0), stop=(k == len(parts) - 1))
+            nc.vector.scalar_tensor_tensor(g_turned[b][:], total[:], -1.0, minus_wt[:], ALU.add, ALU.mult)
         for b in range(blocks):
             back = score_psum.tile([P, 2 * P], F32, name="bank")
             words = g_turned[b][:].bitcast(F32)
             for u in range(2):
-                nc.tensor.transpose(back[:, u * P:(u + 1) * P], words[:, u:2 * P:2], identity[:])
+                nc.tensor.transpose(back[:, u * P:(u + 1) * P], words[:, u * P:(u + 1) * P], identity[:])
             nc.scalar.copy(g_bf[1][:, b * P:(b + 1) * P, :].rearrange("p n j -> p (n j)").bitcast(F32)
                            .rearrange("p (n u) -> p n u", u=2), back[:].rearrange("p (u n) -> p n u", u=2))
         xm_early = sb([P, PASSES, 2, P, PACK], BF16, "xm_early")

@@ -140,8 +140,17 @@ def tile_attend_gnce_pl_sgd_kernel(tc, xT, wT, y, wt, xm, offs, out_0, out_1, ou
             cols = slice(j * P, (j + 1) * P)
             nc.tensor.matmul_mx(bank[:], lhsT=x_codes[g][:, cols].bitcast(E4), lhsT_scale=x_scales[g][:, cols],
                                 rhs=w_codes[:].bitcast(E4), rhs_scale=w_scales[:], start=True, stop=True)
-            nc.scalar.activation(sig_rows[g][:, j, :], bank[:], ACT.Sigmoid, scale=1.0 if g == 0 else -1.0)
-            return sig_rows[g][:, j, :]
+            nc.scalar.activation(sig_rows[:, j, :], bank[:], ACT.Sigmoid)
+            return sig_rows[:, j, :]
+
+        def score_block(b):
+            bank = score_psum.tile([P, N], F32, name="bank")
+            slots = slice(b * P, (b + 1) * P)
+            for j in range(PACK):
+                cols = slice(j * P, (j + 1) * P)
+                nc.tensor.matmul_mx(bank[:, cols], lhsT=x_codes[1][:, cols].bitcast(E4), lhsT_scale=x_scales[1][:, cols],
+                                    rhs=w_codes[:, slots].bitcast(E4), rhs_scale=w_scales[:, slots], start=True, stop=True)
+            nc.scalar.activation(sig_blocks[b][:], bank[:], ACT.Sigmoid, scale=-1.0)
 
         def weigh_y(on_vector, g, j):
             rows = y_raw[g][:, j, :]
@@ -184,7 +193,9 @@ def tile_attend_gnce_pl_sgd_kernel(tc, xT, wT, y, wt, xm, offs, out_0, out_1, ou
                                     rhs=g_codes[g][:, slots].bitcast(E5), rhs_scale=g_scales[g][:, slots],
                                     start=(g == order[0]), stop=(g == order[-1]))
 
-        sig_rows = [sb([P, PACK, N], F32, "sig_rows0"), sb([P, PACK, N], F32, "sig_rows1")]
+        blocks = N // P
+        sig_rows = sb([P, PACK, N], F32, "sig_rows")
+        sig_blocks = [sb([P, PACK * P], F32, "sig_block%d" % b) for b in range(blocks)]
 
         def quantise_w(lo, hi):
             nc.vector.quantize_mx(w_codes[:, lo:hi].bitcast(E4), w_scales[:, lo:hi],
@@ -204,8 +215,8 @@ def tile_attend_gnce_pl_sgd_kernel(tc, xT, wT, y, wt, xm, offs, out_0, out_1, ou
         sig0 = [score(0, j) for j in range(PACK)]
         weigh_y(True, 0, 0)
         quantise_x(1)
-        for j in range(PACK):
-            score(1, j)
+        for b in range(blocks):
+            score_block(b)
         weigh_y(True, 0, 1)
         gradient(0, 0, sig0[0])
         weigh_y(True, 0, 2)
@@ -215,15 +226,14 @@ def tile_attend_gnce_pl_sgd_kernel(tc, xT, wT, y, wt, xm, offs, out_0, out_1, ou
         gradient(0, 3, sig0[3])
         nc.scalar.copy(g_bf[0][:].rearrange("p (c i) j -> p c j i", i=4),
                        g_rows[0][:].rearrange("p j (c i) -> p c j i", i=4))
-        blocks = N // P
         g_turned = [sb([P, 512], BF16, "g_turned%d" % b) for b in range(blocks)]
         for b in range(blocks):
             total = grad_psum.tile([P, 512], F32, name="grad%d" % b)
-            parts = [(sig_rows[1], 0), (sig_rows[1], 1)] + [(y_raw[1], j) for j in range(PACK)]
-            parts = parts + [(sig_rows[1], 2), (sig_rows[1], 3)]
-            for k, (rows, j) in enumerate(parts):
-                lane = j if rows is sig_rows[1] else 2 * (j % 2) + j // 2
-                nc.tensor.matmul(total[:, j * P:(j + 1) * P], lhsT=rows[:, lane, b * P:(b + 1) * P], rhs=identity[:],
+            parts = [sig_blocks[b][:, j * P:(j + 1) * P] for j in range(PACK)]
+            parts = parts + [y_raw[1][:, 2 * (j % 2) + j // 2, b * P:(b + 1) * P] for j in range(PACK)]
+            for k, part in enumerate(parts):
+                j = k % PACK
+                nc.tensor.matmul(total[:, j * P:(j + 1) * P], lhsT=part, rhs=identity[:],
                                  is_transpose=True, start=(k == 0), stop=(k == len(parts) - 1))
             nc.vector.scalar_tensor_tensor(g_turned[b][:], total[:], -1.0, minus_wt[:], ALU.add, ALU.mult)
         for b in range(blocks):
@@ -236,14 +246,14 @@ def tile_attend_gnce_pl_sgd_kernel(tc, xT, wT, y, wt, xm, offs, out_0, out_1, ou
         xm_early = sb([P, PASSES, 2, P, PACK], BF16, "xm_early")
         xm_late = [sb([P, 2, P, PACK], BF16, "xm_late0", tag="g_turned3")]
         deal_xm(nc.vector.tensor_copy, xm_early[:, 0], 0, 0)
-        deal_xm(nc.scalar.copy, xm_early[:, 1], 1, 0, 0, 48)
+        deal_xm(nc.scalar.copy, xm_early[:, 1], 1, 0, 0, 96)
         deal_xm(nc.scalar.copy, xm_late[0][:], 0, 1)
         quantise_g(0)
         quantise_xm(0, 0, xm_early[:, 0])
         quantise_g(1, 0, HALF)
-        deal_xm(nc.vector.tensor_copy, xm_early[:, 1], 1, 0, 48, P)
-        quantise_g(1, HALF, N)
+        deal_xm(nc.vector.tensor_copy, xm_early[:, 1], 1, 0, 96, P)
         quantise_xm(0, 1, xm_early[:, 1])
+        quantise_g(1, HALF, N)
         xm_late.append(sb([P, 2, P, PACK], BF16, "xm_late1", tag="xm_early"))
         deal_xm(nc.vector.tensor_copy, xm_late[1][:], 1, 1)
         window.append(sb([P, T], F32, "window3", tag="xm_raw1"))

from contextlib import ExitStack

import concourse.mybir as mybir
from concourse.masks import make_identity

N, T, D, R = 512, 2048, 512, 1024
LR, WD = 0.1, 0.5
DECAY = 1.0 - LR * WD
FLOPS = 2 * 2 * N * D * R

F32 = mybir.dt.float32
BF16 = mybir.dt.bfloat16
I32 = mybir.dt.int32
U32 = mybir.dt.uint32
U16 = mybir.dt.uint16
U8 = mybir.dt.uint8
E4 = mybir.dt.float8_e4m3fn_x4
E5 = mybir.dt.float8_e5m2_x4
ACT = mybir.ActivationFunctionType
ALU = mybir.AluOpType

P = 128
PACK = 4
PASSES = R // (P * PACK)
CHUNK = 512
CHUNKS = T // CHUNK
HALF = N // 2
PLANES = ((0, 2), (1, 3))


def tile_attend_gnce_pl_sgd_kernel(tc, xT, wT, y, wt, xm, offs, out_0, out_1, out_2):
    nc = tc.nc
    with ExitStack() as ctx:
        held = ctx.enter_context(tc.tile_pool(name="held", bufs=1))
        score_psum = ctx.enter_context(tc.psum_pool(name="score_psum", bufs=3))
        grad_psum = ctx.enter_context(tc.psum_pool(name="grad_psum", bufs=1))

        def sb(shape, dtype, name, tag=""):
            return held.tile(shape, dtype, name=name, tag=tag or name, align_bytes=256)

        offsets = held.tile([P, N // 16], U16, name="offsets")

        def slots_of(h):
            return slice(h * HALF, (h + 1) * HALF)

        def offsets_of(h):
            return offsets[:, h * HALF // 16:(h + 1) * HALF // 16]

        w_planes = wT.rearrange("(p t) c -> p t c", t=PACK)
        out_planes = out_0.rearrange("(p t) c -> p t c", t=PACK)
        source = [sb([P, T], F32, "source%d" % t) for t in range(PACK)]
        wt_rows = sb([P, 512], F32, "wt_rows")
        nc.gpsimd.memset(wt_rows[:], 0.0)
        for t in range(PACK):
            nc.sync.dma_start(source[t][:], w_planes[:, t, :])
            if t == 0:
                nc.sync.dma_start(offsets[:], offs)
                nc.sync.dma_start(wt_rows[0:PASSES, :], wt[0].rearrange("(g r) o -> g (r o)", g=PASSES))
        x_raw = [sb([P, PACK, 512], F32, "x_raw%d" % g) for g in range(PASSES)]
        y_raw = [sb([P, PACK, N], F32, "y_raw%d" % g) for g in range(PASSES)]
        xm_raw = [sb([P, PACK, D], F32, "xm_raw%d" % g) for g in range(PASSES)]
        warm = sb([P, 1], F32, "warm")
        nc.scalar.activation(warm[:], wt_rows[:, 0:1], ACT.Sigmoid)
        identity = sb([P, P], F32, "identity")
        make_identity(nc, identity[:])
        turned = score_psum.tile([P, N], F32, name="bank")
        for j in range(PACK):
            nc.tensor.transpose(turned[:, j * P:(j + 1) * P], wt_rows[:, j:512:PACK], identity[:])
        weight = sb([P, PASSES, PACK], F32, "weight")
        nc.scalar.copy(weight[:, 0, :], turned[:, 0:512:P])
        turned = score_psum.tile([P, N], F32, name="bank")
        for j in range(PACK):
            first = 256 * (j % 2) + j // 2
            nc.tensor.transpose(turned[:, j * P:(j + 1) * P], wt_rows[:, first:first + 255:2], identity[:])
        nc.scalar.copy(weight[:, 1, :], turned[:, 1:512:P])
        spread = score_psum.tile([P, 512], F32, name="bank")
        for j in range(PACK):
            nc.tensor.transpose(spread[:, j * P:(j + 1) * P], weight[:, 1, j:j + 1].to_broadcast([P, P]), identity[:])
        minus_wt = sb([P, 512], F32, "minus_wt")
        nc.scalar.activation(minus_wt[:], spread[:], ACT.Copy, scale=-1.0)
        for g in range(PASSES):
            nc.sync.dma_start(x_raw[g][:], xT[0, :, g * 512:(g + 1) * 512].rearrange("(p t) r -> p t r", t=PACK))
        y_rows = y[0, 0:512, :].rearrange("(p j) n -> p j n", j=PACK)
        for lo, hi in ((0, 2), (2, 4)):
            nc.sync.dma_start(y_raw[0][:, lo:hi, :], y_rows[:, lo:hi, :])
        nc.sync.dma_start(y_raw[1][:].rearrange("p (h u) n -> p h (u n)", h=2),
                          y[0, 512:R, :].rearrange("(h p u) n -> p h (u n)", h=2, u=2))
        for g in range(PASSES):
            nc.sync.dma_start(xm_raw[g][:], xm[0, g * 512:(g + 1) * 512, :].rearrange("(p j) d -> p j d", j=PACK))
        window = [sb([P, T], F32, "window%d" % t) for t in range(PACK - 1)]

        picked = sb([P, 2, N], F32, "picked")
        picked_late = [sb([P, 2, HALF], F32, "picked_late%d" % h) for h in range(2)]
        w_bf = sb([P, N, PACK], BF16, "w_bf")
        decayed = [None, sb([P, N], F32, "decayed1"), None, sb([P, N], F32, "decayed3")]
        for t in range(2):
            nc.vector.tensor_copy(picked[:, t, :], source[t][:].indirect(offsets[:]))
            if t == 0:
                nc.scalar.activation(window[t][:], source[t][:], ACT.Copy)
            else:
                nc.vector.tensor_copy(window[t][:], source[t][:])
                nc.scalar.copy(w_bf[:, :, 0:2], picked[:].rearrange("p e n -> p n e"))
                nc.scalar.activation(decayed[t][:], picked[:, t, :], ACT.Copy, scale=DECAY)
        for t in range(2, PACK):
            for h in range(2):
                nc.vector.tensor_copy(picked_late[h][:, t - 2, :], source[t][:].indirect(offsets_of(h)))
            if t == 2:
                nc.vector.tensor_copy(window[t][:, 0:3 * CHUNK], source[t][:, 0:3 * CHUNK])
                nc.scalar.activation(window[t][:, 3 * CHUNK:T], source[t][:, 3 * CHUNK:T], ACT.Copy)
        nc.scalar.copy(w_bf[:, 0:HALF, 2:4], picked_late[0][:].rearrange("p e n -> p n e"))
        for h in range(2):
            nc.scalar.activation(decayed[3][:, slots_of(h)], picked_late[h][:, 1, :], ACT.Copy, scale=DECAY)
        w_codes = sb([P, N], U32, "w_codes")
        w_scales = sb([P, N], U8, "w_scales")

        def deal(engine_copy, g, lo, hi, first=0, last=PACK):
            engine_copy(
                x_bf[g][:, first:last, lo:hi, :].rearrange("p j s t -> p s t j"),
                x_raw[g][:].rearrange("p t (s j) -> p s t j", j=PACK)[:, lo:hi, :, first:last],
            )

        x_bf = [sb([P, PACK, P, PACK], BF16, "x_bf%d" % g) for g in range(PASSES)]
        x_codes = [sb([P, 512], U32, "x_codes%d" % g) for g in range(PASSES)]
        x_scales = [sb([P, 512], U8, "x_scales%d" % g) for g in range(PASSES)]
        xm_scales = [sb([P, PASSES, 2 * P], U8, "xm_scales%d" % u) for u in range(2)]
        xm_codes = [sb([P, PASSES, 2 * P], U32, "xm_codes%d" % u) for u in range(2)]
        g_rows = [sb([P, PACK, N], BF16, "g_rows0")]
        g_bf = [sb([P, N, PACK], BF16, "g_bf0"), sb([P, N, PACK], BF16, "g_bf1")]
        g_codes = [sb([P, N], U32, "g_codes%d" % g) for g in range(PASSES)]
        g_scales = [sb([P, N], U8, "g_scales%d" % g) for g in range(PASSES)]

        def round_on_gpsimd(dst, src):
            nc.gpsimd.tensor_scalar(dst, src, 1.0, -0.0, ALU.mult, ALU.add)

        def quantise_x(g):
            nc.vector.quantize_mx(x_codes[g][:].bitcast(E4), x_scales[g][:], x_bf[g][:].rearrange("p j s t -> p (j s t)"))

        def score(g, j):
            bank = score_psum.tile([P, N], F32, name="bank")
            cols = slice(j * P, (j + 1) * P)
            nc.tensor.matmul_mx(bank[:], lhsT=x_codes[g][:, cols].bitcast(E4), lhsT_scale=x_scales[g][:, cols],
                                rhs=w_codes[:].bitcast(E4), rhs_scale=w_scales[:], start=True, stop=True)
            nc.scalar.activation(sig_rows[:, j, :], bank[:], ACT.Sigmoid)
            return sig_rows[:, j, :]

        def score_block(b):
            bank = score_psum.tile([P, N], F32, name="bank")
            slots = slice(b * P, (b + 1) * P)
            for j in range(PACK):
                cols = slice(j * P, (j + 1) * P)
                nc.tensor.matmul_mx(bank[:, cols], lhsT=x_codes[1][:, cols].bitcast(E4), lhsT_scale=x_scales[1][:, cols],
                                    rhs=w_codes[:, slots].bitcast(E4), rhs_scale=w_scales[:, slots], start=True, stop=True)
            nc.scalar.activation(sig_blocks[b][:], bank[:], ACT.Sigmoid, scale=-1.0)

        def weigh_y(on_vector, g, j):
            rows = y_raw[g][:, j, :]
            if on_vector:
                nc.vector.tensor_scalar(rows, rows, weight[:, g, j:j + 1], None, ALU.mult)
            else:
                nc.scalar.activation(rows, rows, ACT.Copy, scale=weight[:, g, j:j + 1])

        def gradient(g, j, sig):
            nc.vector.scalar_tensor_tensor(g_rows[g][:, j, :], sig, weight[:, g, j:j + 1],
                                           y_raw[g][:, j, :], ALU.mult, ALU.subtract)

        def quantise_g(g, lo=0, hi=N):
            nc.vector.quantize_mx(g_codes[g][:, lo:hi].bitcast(E5), g_scales[g][:, lo:hi],
                                  g_bf[g][:, lo:hi, :].rearrange("p n j -> p (n j)"))

        def deal_xm(engine_copy, dst, g, u, lo=0, hi=P):
            if g == 0:
                engine_copy(
                    dst.rearrange("p e m j -> p m j e")[:, lo:hi],
                    xm_raw[g][:].rearrange("p j (m t) -> p m j t", t=PACK)[:, lo:hi, :, u:PACK:2],
                )
            else:
                engine_copy(
                    dst.rearrange("p e m (a b) -> p m a b e", a=2)[:, lo:hi],
                    xm_raw[g][:].rearrange("p (b a) (m t) -> p m a b t", b=2, t=PACK)[:, lo:hi, :, :, u:PACK:2],
                )

        def quantise_xm(u, g, src):
            nc.vector.quantize_mx(xm_codes[u][:, g, :].bitcast(E4), xm_scales[u][:, g, :],
                                  src.rearrange("p e m j -> p (e m j)"))

        def table_gradient(acc, t, slots):
            u = 0 if t in PLANES[0] else 1
            cols = slice((t // 2) * P, (t // 2 + 1) * P)
            order = range(PASSES - 1, -1, -1) if t == 3 else range(PASSES)
            for g in order:
                nc.tensor.matmul_mx(acc, lhsT=xm_codes[u][:, g, cols].bitcast(E4),
                                    lhsT_scale=xm_scales[u][:, g, cols],
                                    rhs=g_codes[g][:, slots].bitcast(E5), rhs_scale=g_scales[g][:, slots],
                                    start=(g == order[0]), stop=(g == order[-1]))

        blocks = N // P
        sig_rows = sb([P, PACK, N], F32, "sig_rows")
        sig_blocks = [sb([P, PACK * P], F32, "sig_block%d" % b) for b in range(blocks)]

        def quantise_w(lo, hi):
            nc.vector.quantize_mx(w_codes[:, lo:hi].bitcast(E4), w_scales[:, lo:hi],
                                  w_bf[:, lo:hi, :].rearrange("p n t -> p (n t)"))

        quantise_w(0, HALF)
        nc.vector.tensor_copy(w_bf[:, HALF:N, 2:4], picked_late[1][:].rearrange("p e n -> p n e"))
        quantise_w(HALF, N)
        for first in (0, 2):
            deal(nc.scalar.copy, 0, 0, 64, first, first + 2)
            deal(nc.vector.tensor_copy, 0, 64, P, first, first + 2)
        for lo in (0, 2):
            nc.vector.quantize_mx(x_codes[0][:, lo * P:(lo + 2) * P].bitcast(E4), x_scales[0][:, lo * P:(lo + 2) * P],
                                  x_bf[0][:, lo:lo + 2].rearrange("p j s t -> p (j s t)"))
        nc.vector.tensor_copy(x_bf[1][:].rearrange("p (u h) s t -> p (h s) t u", u=2),
                              x_raw[1][:].rearrange("p t (c u) -> p c t u", u=2))
        sig0 = [score(0, j) for j in range(PACK)]
        weigh_y(True, 0, 0)
        quantise_x(1)
        for b in range(blocks):
            score_block(b)
        weigh_y(True, 0, 1)
        gradient(0, 0, sig0[0])
        weigh_y(True, 0, 2)
        gradient(0, 1, sig0[1])
        weigh_y(True, 0, 3)
        gradient(0, 2, sig0[2])
        gradient(0, 3, sig0[3])
        nc.scalar.copy(g_bf[0][:].rearrange("p (c i) j -> p c j i", i=4),
                       g_rows[0][:].rearrange("p j (c i) -> p c j i", i=4))
        g_turned = [sb([P, 512], BF16, "g_turned%d" % b) for b in range(blocks)]
        for b in range(blocks):
            total = grad_psum.tile([P, 512], F32, name="grad%d" % b)
            parts = [sig_blocks[b][:, j * P:(j + 1) * P] for j in range(PACK)]
            parts = parts + [y_raw[1][:, 2 * (j % 2) + j // 2, b * P:(b + 1) * P] for j in range(PACK)]
            for k, part in enumerate(parts):
                j = k % PACK
                nc.tensor.matmul(total[:, j * P:(j + 1) * P], lhsT=part, rhs=identity[:],
                                 is_transpose=True, start=(k == 0), stop=(k == len(parts) - 1))
            nc.vector.scalar_tensor_tensor(g_turned[b][:], total[:], -1.0, minus_wt[:], ALU.add, ALU.mult)
        for b in range(blocks):
            back = score_psum.tile([P, 2 * P], F32, name="bank")
            words = g_turned[b][:].bitcast(F32)
            for u in range(2):
                nc.tensor.transpose(back[:, u * P:(u + 1) * P], words[:, u * P:(u + 1) * P], identity[:])
            nc.scalar.copy(g_bf[1][:, b * P:(b + 1) * P, :].rearrange("p n j -> p (n j)").bitcast(F32)
                           .rearrange("p (n u) -> p n u", u=2), back[:].rearrange("p (u n) -> p n u", u=2))
        xm_early = sb([P, PASSES, 2, P, PACK], BF16, "xm_early")
        xm_late = [sb([P, 2, P, PACK], BF16, "xm_late0", tag="g_turned3")]
        deal_xm(nc.vector.tensor_copy, xm_early[:, 0], 0, 0)
        deal_xm(nc.scalar.copy, xm_early[:, 1], 1, 0, 0, 96)
        deal_xm(nc.scalar.copy, xm_late[0][:], 0, 1)
        quantise_g(0)
        quantise_xm(0, 0, xm_early[:, 0])
        quantise_g(1, 0, HALF)
        deal_xm(nc.vector.tensor_copy, xm_early[:, 1], 1, 0, 96, P)
        quantise_xm(0, 1, xm_early[:, 1])
        quantise_g(1, HALF, N)
        xm_late.append(sb([P, 2, P, PACK], BF16, "xm_late1", tag="xm_early"))
        deal_xm(nc.vector.tensor_copy, xm_late[1][:], 1, 1)
        window.append(sb([P, T], F32, "window3", tag="xm_raw1"))
        nc.sync.dma_start(window[3][:], w_planes[:, 3, :])

        near = CHUNK
        pairs_near = sb([P, 4 * near], BF16, "pairs_near")
        pairs_far = sb([P, 4 * (T - near)], BF16, "pairs_far")
        own = 512
        fresh = [sb([P, N], F32, "fresh%d" % t)[:] for t in range(PACK - 1)]
        fresh.append(pairs_near[:].bitcast(F32)[:, near - HALF:near + HALF])

        def update(t, acc, h):
            old = picked[:, 0, slots_of(h)] if t == 0 else picked_late[h][:, 0, :]
            nc.vector.scalar_tensor_tensor(fresh[t][:, slots_of(h)], acc, -LR / DECAY, old, ALU.mult, ALU.add)

        def scatter(t, h):
            nc.scalar.activation(window[t][:].indirect(offsets_of(h)), fresh[t][:, slots_of(h)], ACT.Copy, scale=DECAY)
            if h == 1:
                nc.sync.dma_start(out_planes[:, t, :], window[t][:])

        def scatter_on_vector(t):
            nc.vector.scalar_tensor_tensor(fresh[t], grad[t][:], -LR, decayed[t][:], ALU.mult, ALU.add)
            nc.vector.tensor_copy(window[t][:].indirect(offsets[:]), fresh[t])
            nc.sync.dma_start(out_planes[:, t, :], window[t][:])

        def halves(t, lo, hi):
            pairs, base, width = (pairs_near, 0, near) if lo < near else (pairs_far, near, T - near)
            first = 2 * ((t // 2) * width - base) + t % 2
            return pairs[:, first + 2 * lo:first + 2 * hi - 1:2]

        for h in range(2):
            acc = score_psum.tile([P, HALF], F32, name="bank")
            table_gradient(acc[:], 0, slots_of(h))
            update(0, acc[:], h)
            if h == 0:
                quantise_xm(1, 0, xm_late[0][:])
                quantise_xm(1, 1, xm_late[1][:])
        grad = {}
        for t in (2, 1, 3):
            grad[t] = grad_psum.tile([P, N], F32, name="grad%d" % t)
            table_gradient(grad[t][:], t, slice(0, N))
        for h in range(2):
            scatter(0, h)
        for h in range(2):
            update(2, grad[2][:, slots_of(h)], h)
        scatter_on_vector(1)
        for t in range(2):
            round_on_gpsimd(halves(t, near, T), window[t][:, near:T])
        for h in range(2):
            scatter(2, h)
        scatter_on_vector(3)
        nc.scalar.copy(halves(2, near, T), window[2][:, near:T])

        pieces = [(0, 512), (512, 1024), (1024, 1280), (1280, 1536), (1536, 1792), (1792, 2048)]
        reuse = ["x_bf0", "x_bf1", "g_rows0", "y_raw1", "g_bf0", "y_raw0"]
        on_vector = 3
        out_bf = [sb([P, hi - lo, PACK], BF16, "out_bf%d" % c, tag=reuse[c]) for c, (lo, hi) in enumerate(pieces)]
        stores = [(0, 512), (512, 1024), (1024, 1536), (1536, 1792), (1792, 2048)]
        out_codes = [sb([P, hi - lo], U32, "out_codes%d" % c) for c, (lo, hi) in enumerate(stores)]
        out_scales = sb([P, CHUNK], U8, "out_scales")
        words_out = out_1[0].rearrange("p c l -> p (c l)").bitcast(I32)

        def join(engine_copy, c):
            lo, hi = pieces[c]
            if lo < near:
                src = pairs_near[:].bitcast(F32).rearrange("p (u n) -> p u n", u=2)[:, :, lo:hi]
            else:
                src = pairs_far[:].bitcast(F32).rearrange("p (u n) -> p u n", u=2)[:, :, lo - near:hi - near]
            dst = out_bf[c][:].rearrange("p n t -> p (n t)").bitcast(F32).rearrange("p (n u) -> p n u", u=2)
            engine_copy(dst, src.rearrange("p u n -> p n u"))

        def quantise_out(c):
            lo, hi = pieces[c]
            k = [last >= hi for first, last in stores].index(True)
            first, last = stores[k]
            for a in range(lo, hi, HALF):
                row = 4 * (a // CHUNK)
                nc.vector.quantize_mx(out_codes[k][:, a - first:a - first + HALF].bitcast(E4),
                                      out_scales[row:P, a % CHUNK:a % CHUNK + HALF],
                                      out_bf[c][:, a - lo:a - lo + HALF, :].rearrange("p n t -> p (n t)"))
            if hi == last:
                nc.sync.dma_start(words_out[:, first:last], out_codes[k][:].bitcast(I32))

        for t in range(PACK):
            lo = near - own if t < 2 else 0
            nc.vector.tensor_copy(halves(t, lo, near), window[t][:, lo:near])
        for c in range(1, len(pieces)):
            lo, hi = pieces[c]
            nc.scalar.copy(halves(3, lo, hi), window[3][:, lo:hi])
            if c >= on_vector:
                join(nc.scalar.copy, c)
        join(nc.vector.tensor_copy, 0)
        for c in range(len(pieces)):
            if c + 1 < on_vector:
                join(nc.vector.tensor_copy, c + 1)
            quantise_out(c)
        scales_out = out_2[0].bitcast(I32)
        for q in range(4):
            nc.sync.dma_start(scales_out[4 * q:4 * q + 4, :].rearrange("i (c x) -> c i x", c=CHUNKS),
                              out_scales[32 * q:32 * q + 16, :].bitcast(I32))
